import numpy as np, ml_dtypes
CORES = [113,118,241,246]
N = 4
BF = ml_dtypes.bfloat16
W, B, L, J, VIS, ST = 1792, 1280, 128, 512, 5, 3
def pick(rng, share, *tail):
    v = rng.integers(0, W, (N, 8) + tail); pool = rng.integers(0, W, (N, 8, 64)); ix = rng.integers(0, 64, (N, 8) + tail)
    h = np.take_along_axis(pool, ix.reshape(N, 8, -1), 2).reshape(v.shape)
    return np.where(rng.random(v.shape) < np.reshape(share, (N, 8) + (1,) * len(tail)), h, v)
def thread(rng, par, share, out):
    ft = np.full((N, 8, J), W, np.int64); a = np.arange(N)[:, None]; g = np.arange(8)[None, :]
    order = B + np.argsort(rng.random((N, 8, J)), axis=-1)
    for s in range(J):
        n = order[:, :, s]; base = rng.integers(0, B, (N, 8)); o = rng.random((N, 8)) < out
        x = np.where(rng.random((N, 8)) < (share if s else 0.0), order[a, g, rng.integers(0, max(s, 1), (N, 8))], base)
        up = par[a, g, x]
        par[a, g, n] = np.where(o, base, up); par[a, g, x] = np.where(o, up, n); ft[a, g, n - B] = np.where(o, W, x)
        v = np.maximum(up - B, 0); cur = ft[a, g, v]
        ft[a, g, v] = np.where(~o & (up >= B) & (cur == x), n, cur)
    return ft
def parts(rng):
    sh = np.array([0.05, 0.1, 0.3, 0.5])
    x = rng.integers(0, 256, (N, 8, 16, W)); kn = np.zeros((N, 8, 16, W), np.int64)
    kn[:, :, 1:] = pick(rng, rng.choice(sh, (N, 8)), 15, W)
    par = np.zeros((N, 8, W), np.int64); par[:, :, :B] = (rng.random((N, 8, B)) * np.arange(B)).astype(np.int64)
    ft = thread(rng, par, rng.choice(np.array([0.2, 0.5, 0.8]), (N, 8)), 0.0625); kn[:, :, 0] = par
    tr = pick(rng, rng.choice(sh, (N, 8)), W); b = pick(rng, rng.choice(sh, (N, 8)), L); z = rng.integers(0, 256, (N, 8, 16, L))
    m = rng.random((N, 8, L)) < 0.08
    oj = B + L * np.arange(N)[:, None, None] + rng.integers(0, L, (N, 8, L))
    near = np.take_along_axis(x, oj[:, :, None, :], 3) + rng.integers(-9, 10, z.shape)
    b = np.where(m, oj, b); z = np.where(m[:, :, None, :], np.minimum(np.maximum(near, 0), 255), z)
    return x, kn, tr, ft, z, b
def pack(x, kn, tr, ft, z, b):
    return {"x0": np.ascontiguousarray(x.reshape(N, 128, W)).astype(np.float32).astype(BF), "kn": np.ascontiguousarray(kn.reshape(N, 128, W)).astype(np.int32), "tr": tr.astype(np.int32),
            "ft": ft.astype(np.int32), "z0": np.ascontiguousarray(z.reshape(N, 128, L)).astype(np.float32).astype(BF), "bs": b.astype(np.int32)}
def setup_inputs(rng):
    return pack(*parts(rng))
def uneven(rng, top, p, *shape):
    return np.minimum((top * rng.random(shape) ** p).astype(np.int64), top - 1)
def setup_inputs_spread(rng):
    x, kn, tr, ft, z, b = parts(rng); ps = np.array([0.25, 0.5, 1.0, 2.0, 4.0, 8.0])
    x = uneven(rng, 256, rng.choice(ps, (N, 8, 1, W)), N, 8, 16, W); z = uneven(rng, 256, rng.choice(ps, (N, 8, 1, L)), N, 8, 16, L)
    k2 = uneven(rng, W, rng.choice(ps, (N, 8, 16, 1)), N, 8, 16, W); kn[:, :, 1:] = k2[:, :, 1:]; kn[:, 1::2, 0] = k2[:, 1::2, 0]
    f2 = uneven(rng, W + 1, rng.choice(ps, (N, 8, 1)), N, 8, J); ft[:, 1::2] = f2[:, 1::2]
    tr = uneven(rng, W, rng.choice(ps, (N, 8, 1)), N, 8, W); b = uneven(rng, W, rng.choice(ps, (N, 8, 1)), N, 8, L)
    return pack(x, kn, tr, ft, z, b)
def two(rng, lo, hi, *shape):
    return np.where(rng.random(shape) < 0.5, lo, hi)
def setup_inputs_ends(rng):
    x, kn, tr, ft, z, b = parts(rng); e = np.array([0, W - 1])
    x = np.where(rng.random((N, 8, 1, W)) < 0.5, two(rng, 0, 255, N, 8, 1, W), two(rng, 0, 255, N, 8, 16, W))
    z = np.where(rng.random((N, 8, 1, L)) < 0.6, two(rng, 0, 255, N, 8, 1, L), two(rng, 0, 255, N, 8, 16, L))
    kn = np.where(rng.random((N, 8, 16, W)) < 0.72, two(rng, 0, W - 1, N, 8, 16, W), kn)
    tr = np.where(rng.random((N, 8, W)) < 0.7, two(rng, 0, W - 1, N, 8, W), tr)
    ft = np.where(rng.random((N, 8, J)) < 0.7, two(rng, 0, W, N, 8, J), ft)
    b = np.where(rng.random((N, 8, L)) < 0.7, two(rng, 0, W - 1, N, 8, L), b)
    s = int(rng.integers(0, 4))
    for q in range(N):
        for g in range(8):
            c = (q + g + s) % 4
            x[q, g, :, 0] = 255 * (c & 1); x[q, g, :, W - 1] = 255 * (c >> 1)
        v = 255 * ((q + s) & 1); w = (q >> 1) & 1
        x[q, 7, :, 0] = v; x[q, 7, :, W - 1] = v
        kn[q, 7][:, e] = two(rng, 0, W - 1, 16, 2); kn[q, 7, 14, e] = 0; kn[q, 7, 15, e] = W - 1
        z[q, 7, :, w::2] = 255 - v; z[q, 7, :, 1 - w::2] = v
        b[q, 7, :] = two(rng, 0, W - 1, L); b[q, 7, L - 2:] = W - 1
        z[q, :, :, L - 1] = np.where(np.arange(8)[:, None] % 2 == q % 2, 0, 255)
        lo = B + L * ((q - 1) % N)
        x[q, 6] = 255 * (q & 1); z[q, 6] = 255 * (q & 1); tr[q, 6] = 0
        kn[q, 6, :, 0] = rng.integers(lo, lo + L, 16); b[q, 6] = np.where(b[q, 6] == 0, W - 1, b[q, 6])
    return pack(x, kn, tr, ft, z, b)
def chain(par, fo, seq, x):
    up = int(par[x]); par[x] = seq[0]; fo[seq[0] - B] = x
    par[seq[:-1]] = seq[1:]; fo[seq[1:] - B] = seq[:-1]; par[seq[-1]] = up
def setup_inputs_corners(rng):
    x, kn, tr, ft, z, b = parts(rng); sh = int(rng.integers(0, 8)); jn = B + np.arange(J); sits = []
    kinj = B + L * rng.integers(0, N, (N, 8, 1, W)) + rng.integers(0, L, (N, 8, 15, W))
    kn[:, :, 1:] = np.where(rng.random((N, 8, 1, W)) < 0.15, kinj, kn[:, :, 1:])
    for q in range(N):
        nx = L * ((q + 1) % N)
        for g in range(8):
            c = (q + g + sh) % 8; par = kn[q, g, 0]; fo = ft[q, g]
            if c == 7: continue
            par[:] = rng.integers(0, B, W); fo[:] = W; p = rng.permutation(B)[:J]
            if c == 0:
                m = rng.random(W) < 0.1; kn[q, g][:, m] = B + L * rng.integers(0, N, (1, W))[:, m] + rng.integers(0, L, (16, W))[:, m]
            if c == 1: chain(par, fo, jn, int(rng.integers(0, B)))
            if c == 2: chain(par, fo, np.ascontiguousarray(jn.reshape(N, L).T).reshape(-1), int(rng.integers(0, B)))
            if c == 3:
                up = par[p].copy(); par[p] = jn; fo[:] = p; par[B:] = up
                if q % 2 == 0: sits.append((q, g, np.arange(L), p[nx:nx + L]))
            if c == 4:
                fo[:] = rng.integers(0, W + 1, J); par[B:] = rng.integers(0, W, J)
                i = int(rng.integers(0, L)); m = L * min(q, N - 2) + i
                fo[m] = W; par[B + m] = rng.integers(0, B); par[W - 1] = B + m
                if q > 0:
                    n = L * q + (i + 1) % (L - 1); y = int(rng.integers(1, B))
                    fo[n] = y; par[y] = B + n; par[B + n] = rng.integers(0, B)
                    fo[0] = B + n; par[B] = B + 1; fo[1] = W; x[q, g, :, B] = 255 * (np.arange(16) % 2)
            if c == 5:
                fo[:] = 0; par[0] = B + rng.integers(0, J); par[B:] = two(rng, 0, B - 1, J)
            if c == 6:
                w = np.arange(J) % 3
                fo[:] = np.where(w == 0, jn, np.where(w == 1, W, p)); par[p[w == 2]] = jn[w == 2]
                par[B:] = np.where(w == 1, jn, np.where(w == 2, B + (np.arange(J) + L) % J, par[B:]))
                ls = rng.permutation(np.nonzero(w[L * q:L * q + L] == 2)[0])[:8]; js = B + nx + ls
                fo[js - B] = js; par[js] = js; sits.append((q, g, ls, js))
    ch = rng.integers(0, 5, (N, 8, L)); ro = B + L * np.arange(N)[:, None, None] + 0 * ch
    b = np.choose(ch, [0 * ch, 0 * ch + W - 1, ro + np.arange(L), ro + rng.integers(0, L, (N, 8, L)), b])
    h = rng.integers(0, 4, (N, 8, W)); tr = np.choose(h, [rng.integers(B, W, (N, 8, W)), two(rng, 0, W - 1, N, 8, W), tr, tr])
    for q, g, i, v in sits:
        b[q, g, i] = v; z[q, g][:, i] = x[q, g][:, v]
    return pack(x, kn, tr, ft, z, b)
def setup_inputs_crowd(rng):
    x, kn, tr, ft, z, b = parts(rng); hs = np.zeros((N, 8), np.int64)
    for q in range(N):
        own = B + L * q
        kn[q, :, 0, own:own + L] = rng.integers(0, B, (8, L)); ft[q, :, L * q:L * q + L] = W
        for g in range(8):
            h = int(rng.integers(1, B - 1)); h2 = h + 1; c = (g + q) % 4; hs[q, g] = h
            if q < 2:
                b[q, g] = h; kn[q, g, :, h] = h; kn[q, g, :, h2] = h2
                if q == 1 and g % 2: b[q, g, int(rng.integers(0, L))] = h2
            elif q == N - 1:
                b[q, g] = W - 1; kn[q, g, 1:, W - 1] = rng.integers(own, own + L, 15)
                up = int(kn[q, g, 0, W - 1]); x[q, g, :, up] = x[q, g, :, W - 1]
            elif q == 2:
                s = rng.permutation(B)[:L]; b[q, g] = s; kn[q, g][:, s] = s
            else: b[q, g] = rng.choice(np.array([0, h, h2, W - 1]), L)
            if c == 0: tr[q, g] = W - 1
            if c == 1: tr[q, g] = two(rng, 0, h, W)
            if c == 2: tr[q, g] = h
    for g in range(8):
        h = int(hs[0, g]); e = (h + 3) % B; e2 = (h + 4) % B
        kn[0, g, :, e] = e2; kn[0, g, :, e2] = e2; x[0, g, :, e2] = x[0, g, :, e]; tr[N - 1, g, W - 1] = e
    for g in (3, 7):
        h = int(hs[0, g]); e = (int(hs[1, g]) + 3) % B; js = B + rng.permutation(L)[:16]
        z[0, g] = 0; x[0, g, :, h] = 0; tr[0, g, h] = e
        x[1, g, :, e] = 255; kn[1, g, :, e] = js; x[1, g][:, js] = 0; ft[1, g, js[0] - B] = W
    return pack(x, kn, tr, ft, z, b)
def setup_inputs_ties(rng):
    x, kn, tr, ft, z, b = parts(rng)
    lo = rng.integers(0, 247, (N, 8, 1, 1)); sp = np.array([1, 2, 4, 9])[(np.arange(8)[None, :] + rng.integers(0, 4, (N, 1))) % 4].reshape(N, 8, 1, 1)
    x = lo + (rng.random((N, 8, 16, W)) * sp).astype(np.int64); z = lo + (rng.random((N, 8, 16, L)) * sp).astype(np.int64)
    x[..., 1::2] = np.where(rng.random((N, 8, 1, W // 2)) < 0.5, x[..., ::2], x[..., 1::2])
    kn[:, :, 9:] = np.where(rng.random((N, 8, 7, W)) < 0.5, kn[:, :, 2:9], kn[:, :, 9:])
    return pack(x, kn, tr, ft, z, b)
def check_inputs(d):
    bad = []
    for k, lo, hi in (("x0", 0, 255), ("kn", 0, W - 1), ("tr", 0, W - 1), ("ft", 0, W), ("z0", 0, 255), ("bs", 0, W - 1)):
        a = np.asarray(d[k]).astype(np.float64)
        if not (np.min(a) >= lo and np.max(a) <= hi): bad.append("range of " + k)
        elif np.any(np.floor(a) != a): bad.append("whole numbers in " + k)
    return bad
def own(v, r):
    return (v >= B + L * r) & (v < B + L * r + L)
def lowest(key):
    return np.argmax(key[:, :, None] == key[:, None, :], axis=2) == np.arange(L)
def reference(x0, kn, tr, ft, z0, bs):
    X = x0.astype(np.float32).astype(np.int32).reshape(N, 8, 16, W); KN = kn.astype(np.int64).reshape(N, 8, 16, W)
    TR = tr.astype(np.int64); FT = ft.astype(np.int64)
    z = z0.astype(np.float32).astype(np.int32).reshape(N, 8, 16, L); b = bs.astype(np.int64); b0 = np.zeros((N, 8, L), np.int64); A = [0] * N
    g = np.arange(8)[:, None]; lane = np.arange(L)
    for t in range(VIS):
        for q in range(N):
            r = (q - t) % N; lo = B + L * r; Xq = X[q]; Kq = KN[q]; par = Kq[:, 0]; fo = FT[q]; zz = z[r].copy(); s = b[r].copy()
            n = lo + lane; y = fo[:, L * r:L * r + L].copy(); u = par[:, lo:lo + L].copy()
            live = ~own(y, r) & ~own(u, r)
            held = live & (y < W) & (par[g, np.minimum(y, W - 1)] == n)
            uj = np.maximum(u - B, 0); turn = held & (u >= B) & (fo[g, uj] == n)
            gi, li = np.nonzero(held); par[gi, y[gi, li]] = u[gi, li]
            gi, li = np.nonzero(turn); fo[gi, uj[gi, li]] = y[gi, li]
            fo[:, L * r:L * r + L] = np.where(live, W, y)
            for step in range(ST):
                c = Kq[g, :, s]
                xc = np.take_along_axis(Xq, c.reshape(8, 1, L * 16), 2).reshape(8, 16, L, 16)
                d = np.where(own(c, r), 2 ** 20, np.add.reduce(np.abs(xc - zz[:, :, :, None]), axis=1))
                k = np.argmin(d, axis=2)[:, :, None]
                best = np.take_along_axis(d, k, 2)[:, :, 0]; cand = np.take_along_axis(c, k, 2)[:, :, 0]
                here = np.add.reduce(np.abs(np.take_along_axis(Xq, s[:, None, :], 2) - zz), axis=1)
                s = np.where(best < here + (A[r] & 31), cand, s)
            may = live & ~own(s, r); seat = may & lowest(np.where(may, s, W + lane))
            xs = np.take_along_axis(Xq, s[:, None, :], 2)
            gi, li = np.nonzero(seat); m = s[gi, li]; nn = lo + li
            cols = Kq[gi, :, m]; up = cols[:, 0].copy()
            hit = (up >= B) & (fo[gi, np.maximum(up - B, 0)] == m)
            Kq[gi, :, nn] = cols; par[gi, m] = nn
            fo[gi[hit], up[hit] - B] = nn[hit]; fo[gi, nn - B] = m
            Xq[gi, :, nn] = (xs[gi, :, li] + zz[gi, :, li]) >> 1
            A[r] = int(np.sum(live & ~seat))
            z[r] = (zz + xs) >> 1; b[r] = s
        if t > 0:
            for q in range(N):
                r = (q - t) % N; o = b0[r]; gi, li = np.nonzero(lowest(o))
                TR[(q - 1) % N][gi, o[gi, li]] = b[r][gi, li]
        b0 = b.copy()
        if t < VIS - 1:
            for q in range(N):
                r = (q - t) % N; b[r] = np.take_along_axis(TR[q], b0[r], 1)
    zq = np.stack([z[(q - VIS + 1) % N] for q in range(N)])
    return {"yk": np.ascontiguousarray(KN[:, :, :, B:]).reshape(N, 128, J).astype(np.float32), "yp": np.ascontiguousarray(KN[:, :, 0, :B]).astype(np.float32), "yf": FT.astype(np.float32),
            "yt": TR.astype(np.float32), "yx": np.ascontiguousarray(X[:, :, :, B:]).reshape(N, 128, J).astype(np.float32).astype(BF), "yz": zq.reshape(N, 128, L).astype(np.float32).astype(BF)}

@@ -1,0 +1,695 @@
+from concourse.mybir import AluOpType as ALU, ActivationFunctionType as AF
+
+W, B0, NR, VIS, ST = 1792, 1280, 4, 5, 3
+TR = 1808
+TW = TR + 128
+MAGIC = 12582912.0
+NENG = 8
+f32, bf, i32, u16 = "float32", "bfloat16", "int32", "uint16"
+h16 = "float16"
+CUTS = ((0, 16), (16, 32), (32, 48), (48, 64))
+VCUTS = CUTS
+EARLY = True
+TURN = True
+
+SB = {
+    "KIN": (TW, f32), "FT": (TW, f32), "TT": (TW, f32), "TO": (TW, f32), "XX": (2 * W, bf), "IOTA": (W, f32),
+    "KRAW": (W, i32), "FRAW": (512, i32), "BRAW": (128, i32), "TRAW": (112, i32), "TCF": (112, f32), "EE": (2048, bf),
+    "PI": (8, i32), "PC": (16, f32), "JK": (72, f32), "J2": (128, f32), "JM": (256, f32), "JD": (128, f32), "J8": (32, f32),
+    "JP": (144, f32), "MASK": (128, f32), "MASK2": (128, f32), "PAIR": (128, f32), "SWAP": (128, f32), "BLK": (128, bf),
+    "BLKS": (128, bf), "IDB": (128, bf), "IDF": (128, f32), "SELX": (128, f32), "SELB": (128, bf), "SELH": (128, h16),
+    "R3": (24, f32), "RH": (24, h16), "RBIG": (16, bf), "RX2": (64, h16), "THR": (256, f32), "BOM": (8, bf), "BOX": (8, bf),
+    "PERM": (144, f32), "KC": (72, bf), "RST": (72, f32), "SG": (128, f32), "CO": (16, u16), "TRI": (256, bf),
+    "B24": (24, f32), "A24": (24, f32), "B32": (32, f32), "A32": (32, f32), "S8": (128, f32), "ONES": (128, f32),
+    "C16": (8, f32), "EQ": (9 * 128, bf), "MK": (256, h16), "MKB": (256, bf), "MKV": (128, h16), "MKT": (128, bf),
+    "KH": (128, h16), "OYU": (16, u16), "AB": (48, f32), "REL": (48, bf), "NL": (16, f32), "U32": (32, f32), "U24": (24, f32),
+    "OSC": (24, u16), "NLX": (128, bf), "KM": (128, f32), "U0": (128, f32), "N0": (128, f32), "YC": (144, f32),
+    "WK": (256, f32), "WF": (256, f32), "TM": (256, f32), "TS": (128, f32), "KP": (256, h16), "OB": (8, u16),
+    "XS2": (128, bf), "XS3": (128, bf), "MS2": (128, bf), "MS3": (128, bf), "ZT": (128, bf), "XB": (128, bf), "RB": (8, bf),
+    "OV": (8, u16), "NH": (256, bf), "AT": (24, f32),
+}
+for _h in range(2):
+    SB.update({"OFF%d" % _h: (68, u16), "XG%d" % _h: (1024, bf), "MX%d" % _h: (1024, bf), "CF%d" % _h: (130, f32),
+               "XS%d" % _h: (128, bf), "MS%d" % _h: (128, bf), "SW%d" % _h: (16, f32), "M%d" % _h: (72, f32),
+               "E%d" % _h: (72, f32), "VL%d" % _h: (72, f32), "S2%d" % _h: (72, f32), "BE%d" % _h: (128, h16)})
+SB.update({"WX": (256 * VIS, bf), "ZIN": (128 * VIS, bf), "BW": (8 * VIS, u16), "BIN": (8 * VIS, u16),
+           "OL": (32 * VIS, u16), "LIN": (8 * VIS, u16), "AO": (4 * VIS, f32), "AIN": (4 * VIS, f32)})
+SCRATCH = {k: ("sbuf", [128, v[0]], v[1]) for k, v in SB.items()}
+for _k in range(8):
+    SCRATCH["P%d" % _k] = ("psum", [128, 512], f32)
+for _k in ("DT0", "DT1", "DT2"):
+    SCRATCH[_k] = ("dram", [128, 112], f32)
+DMASEM = ["dk0", "dk1", "dk2", "dk3", "dpre", "dx0", "dx1", "dz", "df", "db", "dt", "dtt", "dd1", "dto", "dout"]
+RSEM = ["r%s%d" % (k, t) for k in "bzla" for t in range(VIS)] + ["rt0", "rt1"]
+SEMAPHORES = ["cV", "cS", "cP", "cG", "sent"] + DMASEM + RSEM
+CY = 0.83 * 1.2
+CG, CS, HOP, NET = 1.5, 3.5, 90.0, 2500.0
+PF, PE = 8, 0.55
+SLACK = 60.0
+NUDGE = {'f20_5': -1200, 'w21_8': 100, 'w01_3': -1100, 'w10_2': 3700, 's12': 2500, 's79': 2500, 'f21_11': -2500, 's70': -300, 'e24': -900, 'w21_3': -600, 'f01_6': 600, 's28': 2500, 'q3': -600, 'e37': -1200, 's40': 2500, 's22': 400, 's10': 1200, 'e53': 1500, 'e48': -1200, 's48': 100, 'w01_19': -600, 's46': -300, 'f11_5': 1200, 's20': -600, 's24': 300, 'w11_15': 600, 'e68': -2500, 'w00_0': -100, 'f10_5': -600, 'w01_9': 1200, 'e63': -1200, 'e28': -1200, 's4': -1200, 'w00_21': 1200, 'w10_16': -300, 'w21_19': -1200, 'w00_27': -600, 'o13': 500, 'w10_27': 2500, 'f10_1': 1200, 'i76': 600, 'i31': -1200, 'i72': 1200, 'w20_15': 2500, 'q6': -1200, 'f00_4': -400, 'w21_24': 3700, 'i41': -2500, 'f11_4': -300, 'i30': -3700, 'w20_16': 1200, 'i96': -600, 'i113': -100, 'i101': -2500, 'w01_30': 300, 'w10_23': 1200, 'f00_2': -1200, 's32': 100, 's77': 100, 'o7': 600, 's23': 300, 'w20_8': 100, 'i51': 300, 'w01_0': -600, 'w10_4': -1200, 'w01_29': 2500, 'f00_9': 1200, 'i124': -1200, 'b1': 2500, 'e73': 2500, 'b4': 2500, 'i6': -600, 'f00_11': -300, 'e61': 300, 'w20_32': 2500, 'f01_2': -100, 'w20_21': 1200, 'w00_10': 300, 's62': 300, 'p1': 900, 'w21_33': -1200, 'e27': -1200, 'i79': -600, 'w20_19': 100, 'f21_8': -600, 'e14': -100, 'a5': -2500, 'i118': 2500, 'e54': 300, 'w21_26': 100, 's71': -1200, 'e13': -300}
+
+
+def ap(name, c0=0, c1=None, st=1, p0=0, p1=128, ps=1, off=None):
+    if c1 is None:
+        c1 = SCRATCH[name][1][1]
+    return {"n": name, "c0": c0, "c1": c1, "st": st, "p0": p0, "p1": p1, "ps": ps, "off": off}
+
+
+def ind(win, off):
+    d = dict(win)
+    d["off"] = off
+    return d
+
+
+def width(a):
+    if a["off"] is not None:
+        return 16 * width(a["off"])
+    return len(range(a["c0"], a["c1"], a["st"]))
+
+
+def two(a):
+    return SCRATCH[a["n"]][2] in (bf, u16, "float16")
+
+
+def psum(a):
+    return SCRATCH[a["n"]][0] == "psum"
+
+
+def build(rank):
+    ops = []
+    tag = ["i", 0]
+    prev = {}
+
+    def add(eng, kind, args, rd, wr, cost, **kw):
+        r = []
+        for a in rd + wr:
+            if isinstance(a, dict) and a["off"] is not None:
+                r.append(a["off"])
+        r += [a for a in rd if isinstance(a, dict)]
+        o = {"e": eng, "k": kind, "a": args, "r": r, "w": [a for a in wr if isinstance(a, dict)], "c": cost}
+        o.update(kw)
+        o["cl"] = "%s%d" % (tag[0], tag[1])
+        tag[1] += 1
+        ops.append(o)
+        return len(ops) - 1
+
+    def chain(q, i):
+        if q in prev:
+            ops[i]["after"] = prev[q]
+        prev[q] = i
+
+    def vcost(out, ins, per):
+        n = width(out)
+        if out["off"] is not None:
+            return 60 + n * CS * CY
+        if ins[0]["off"] is not None:
+            return 60 + n * CG * CY
+        return 30 + max(64, n * per) * CY
+
+    def cp(out, a):
+        add("V", "copy", (out, a), [a], [out], vcost(out, [a], 0.5 if two(out) and two(a) else 1))
+
+    def tt(out, a, b, op):
+        add("V", "tt", (out, a, b, op), [a, b], [out], vcost(out, [a, b], 1 if psum(a) or psum(b) else 2))
+
+    def ts(out, a, s1, op0, s2=None, op1=None):
+        add("V", "ts", (out, a, s1, s2, op0, op1), [a, s1, s2], [out], vcost(out, [a], 0.5 if two(out) and two(a) else 1))
+
+    def scan(out, d0, d1, op0, op1):
+        add("V", "scan", (out, d0, d1, 0.0, op0, op1), [d0, d1], [out], vcost(out, [d0], 1))
+
+    def ms(out, v):
+        add("V", "memset", (out, v), [], [out], vcost(out, [out], 0.5 if two(out) else 1))
+
+    def act(out, a, fn=AF.Identity, bias=0.0, scale=1.0, acc=None):
+        add("S", "act", (out, a, fn, bias, scale, acc), [a, bias, scale], [out, acc], vcost(out, [a], 1) + 10)
+
+    def mm(out, l, r, start=True, stop=True):
+        c = max(min(64, width(l)), width(r)) * (1 if two(l) else 4)
+        add("P", "mm", (out, l, r, start, stop), [l, r], [out], PF + c * PE)
+
+    def iota(out, pat, base=0, cm=0):
+        chain("G", add("G", "iota", (out, pat, base, cm), [], [out], 130 + 2 * width(out) * CY))
+
+    def dma(q, out, a, sem, nbytes, behind=None):
+        i = add(q, "dma", (out, a), [a], [out], 60, sem=sem, lat=1900 + nbytes / 180.0, behind=behind)
+        if tag[0] == "i":
+            chain(q, i)
+
+    def send(dst, out, a, sem, nbytes):
+        i = add("G", "send", (dst, out, a, sem), [a], [], 300)
+        add("R", "recv", (), [], [out], 0, sem=sem, after=i, lat=NET + nbytes / 40.0)
+
+    nxt, prv = (rank + 1) % NR, (rank - 1) % NR
+    dma("S", ap("FRAW", p1=8), ("ft",), "df", 16e3)
+    dma("S", ap("BRAW", p1=8), ("bs",), "db", 4e3)
+    for k, c in enumerate((3, 2, 1, 0)):
+        dma("Y", ap("KRAW", 448 * c, 448 * c + 448), ("kn", 0, 128, 1, 448 * c, 448 * c + 448), "dk%d" % c, 240e3 * (k + 1))
+    dma("S", ap("ZIN", 0, 128), ("z0",), "dz", 300e3)
+    dma("S", ap("TRAW"), ("tr",), "dt", 400e3)
+    dma("Y", ap("XX", W, 2 * W), ("x0",), "dx1", 1450e3)
+    dma("Y", ap("XX", 0, W), ("x0",), "dx0", 1900e3)
+    pid, pmod, pdiv, podd, phalf, pm2, p32, row0, nrow0, k8, kst, k0 = [ap("PC", k, k + 1) for k in range(12)]
+    iota(ap("PI", 0, 1), [[0, 1]], 0, 1)
+    iota(ap("IOTA", 0, 128), [[1, 128]])
+    iota(ap("JD"), [[1, 8], [0, 16]])
+    iota(ap("JM"), [[0, 16], [1, 16]])
+    iota(ap("J8"), [[0, 4], [1, 8]])
+    iota(ap("JP"), [[8, 2], [16, 8], [1, 9]], -1)
+    iota(ap("JK"), [[0, 8], [2048, 9]])
+    iota(ap("J2"), [[1, 64], [0, 2]])
+    ts(ap("PI", 1, 2), ap("PI", 0, 1), 15, ALU.bitwise_and)
+    ts(ap("PI", 2, 3), ap("PI", 0, 1), 4, ALU.logical_shift_right)
+    ts(ap("PI", 3, 4), ap("PI", 0, 1), 1, ALU.bitwise_and)
+    ts(ap("PI", 4, 5), ap("PI", 0, 1), 1, ALU.logical_shift_right)
+    ts(ap("PI", 5, 6), ap("PI", 0, 1), 1, ALU.logical_shift_right, 15, ALU.bitwise_and)
+    ts(ap("PI", 6, 7), ap("PI", 0, 1), 5, ALU.logical_shift_right)
+    cp(ap("PC", 0, 7), ap("PI", 0, 7))
+    ts(row0, pmod, 0.0, ALU.is_equal)
+    ts(nrow0, pmod, 0.0, ALU.not_equal)
+    ts(ap("MASK"), ap("JM", 0, 128), pmod, ALU.is_equal)
+    ts(ap("BLK"), ap("JD"), pdiv, ALU.is_equal)
+    ts(ap("RX2"), ap("JD", 0, 64), p32, ALU.is_equal)
+    ts(ap("MASK2"), ap("JM", 0, 128), pm2, ALU.is_equal)
+    ts(ap("PAIR"), ap("J2"), phalf, ALU.is_equal)
+    act(ap("PC", 12, 13), podd, scale=-65536.0, bias=65536.0)
+    act(k8, podd, scale=8.0 * 2048)
+    act(ap("KC"), ap("JK"), bias=k8)
+    act(k0, podd, scale=1024.0)
+    act(kst, podd, scale=1024.0 - 15.5 * 65536, bias=15.5 * 65536)
+    act(ap("KC", 0, 72, 9), ap("JK", 0, 72, 9), bias=k0)
+    act(ap("C16"), ap("JK", 0, 72, 9), bias=ap("PC", 12, 13))
+    act(ap("BLKS"), ap("BLK"), scale=2.0 ** -8)
+    ts(ap("SELX"), ap("JD"), pdiv, ALU.is_equal, row0, ALU.mult)
+    ts(ap("SELH"), ap("JD"), pdiv, ALU.is_equal, row0, ALU.mult)
+    act(ap("SELB"), ap("SELX"))
+    ts(ap("IDF"), ap("IOTA", 0, 128), pid, ALU.is_equal)
+    act(ap("IDB"), ap("IDF"))
+    ts(ap("S8", p1=8), ap("JD", p1=8), ap("PC", 0, 1, p1=8), ALU.is_equal)
+    ts(ap("R3"), ap("J8", 0, 24), pdiv, ALU.is_equal)
+    ts(ap("RH"), ap("J8", 0, 24), pdiv, ALU.is_equal)
+    act(ap("RBIG"), ap("R3", 0, 16), scale=4096.0)
+    act(ap("THR", 0, 128), ap("MASK"), scale=-1023.25, bias=1024.0)
+    act(ap("THR", 128, 256), ap("MASK"), scale=-1024.0 + 2.0 ** -9, bias=1024.0)
+    act(ap("BOM"), ap("R3", 0, 8), scale=2.0 ** 17)
+    act(ap("BOX"), ap("R3", 0, 8), scale=-2.0 ** 16)
+    ts(ap("PERM"), ap("JP"), pid, ALU.is_equal)
+    ms(ap("PERM", 0, 144, 9), 0.0)
+    tt(ap("SWAP"), ap("PAIR"), ap("IDF"), ALU.subtract)
+    ms(ap("RST"), 0.0)
+    ms(ap("RST", 0, 72, 9), 2.0 ** 40)
+    act(ap("SG"), ap("JM", 0, 128), AF.Sign)
+    cp(ap("CO", 8, 16), ap("J8", 0, 8))
+    ts(ap("TRI", 0, 128), ap("JM", 0, 128), pmod, ALU.is_le, 4096.0, ALU.mult)
+    act(ap("A32", 0, 8), ap("J8", 0, 8), scale=16.0, bias=pmod)
+    for c0, off in ((0, TR), (8, TR), (16, 16)):
+        act(ap("B24", c0, c0 + 8), ap("A32", 0, 8), bias=float(off))
+    for c0, off in ((0, 128), (8, TR), (16, TR), (24, TR)):
+        act(ap("B32", c0, c0 + 8), ap("A32", 0, 8), bias=float(off))
+    for n, c0, c1, v in (("A24", 16, 24, 0.0), ("YC", 0, 16, float(W)),
+                         ("KIN", W, TW, -1.0), ("FT", W, TW, -1.0), ("TT", W, TW, -1.0), ("AO", 0, 4 * VIS, 0.0)):
+        act(ap(n, c0, c1), ap("JM", 0, c1 - c0), scale=0.0, bias=v)
+    act(ap("ONES"), ap("JD"), scale=0.0, bias=1.0)
+    act(ap("TRI", 128, 256), ap("JD"), scale=0.0, bias=-0.5)
+    for h in range(2):
+        act(ap("XS%d" % h), ap("JD"), scale=0.0)
+        act(ap("MS%d" % h), ap("JD"), scale=0.0, bias=1024.0)
+        act(ap("CF%d" % h), ap("JM", 0, 130), scale=0.0)
+    act(ap("TM"), ap("JM"), scale=0.0)
+    if EARLY:
+        ms(ap("KP"), 0.0)
+    ms(ap("EQ", 0, 896), 0.0)
+    for k in range(16):
+        (cp if k % 2 else act)(ap("EE", k, 2048, 16), ap("IDF"))
+    for c in range(4):
+        cp(ap("KIN", 448 * c, 448 * c + 448), ap("KRAW", 448 * c, 448 * c + 448))
+    cp(ap("TO", 0, 512, p1=8), ap("FRAW", p1=8))
+    cp(ap("TM", 0, 256, 2, p1=8), ap("BRAW", p1=8))
+    mm(ap("P3"), ap("S8", p1=8), ap("TO", 0, 512, p1=8))
+    act(ap("FT", B0, W), ap("P3"))
+    iota(ap("IOTA", B0, W), [[1, W - B0]], B0)
+    iota(ap("FT", 0, B0), [[0, B0]], -1)
+    cp(ap("TCF"), ap("TRAW"))
+    send(nxt, ap("DT0"), ap("TCF"), "rt0", 57e3)
+    iota(ap("IOTA", 128, B0), [[1, B0 - 128]], 128)
+    iota(ap("TO"), [[0, TW]], -1)
+    for a in range(16):
+        dma("Y", ap("TT", 0, W, p0=a, ps=16), ap("DT0"), "dtt", 920e3)
+
+    R8 = ap("R3", 0, 8)
+    turn = []
+    for t in range(VIS):
+        r = (rank - t) % NR
+        lo = B0 + 128 * r
+        mid = lo + 63.5
+        last = t == VIS - 1
+        zin = ap("ZIN", 128 * t, 128 * t + 128)
+        wx = 256 * t
+        tag[:] = ["o", 0]
+        nrep = ap("IOTA", lo, lo + 128)
+        mm(ap("P6", 128, 256), ap("KIN", lo, lo + 128), ap("SELX"))
+        tt(ap("MK", 128, 256), ap("P6", 128, 256), ap("MASK"), ALU.mult)
+        mm(ap("P7", 88, 112), ap("MK", 128, 256), ap("RH"))
+        mm(ap("P4", 256, 384), ap("FT", lo, lo + 128), ap("SELX"))
+        ms(ap("XX", W + lo, W + lo + 128), 1024.0)
+        tt(ap("MK", 0, 128), ap("P4", 256, 384), ap("MASK"), ALU.mult)
+        mm(ap("P7", 64, 88), ap("MK", 0, 128), ap("RH"))
+        cp(ap("OYU"), ap("P7", 80, 96))
+        tt(ap("NH", 0, 128), ind(ap("KIN"), ap("OYU", 0, 8)), nrep, ALU.not_equal)
+        tt(ap("NH", 128, 256), ind(ap("FT"), ap("OYU", 8, 16)), nrep, ALU.not_equal)
+        act(ap("AB"), ap("P7", 64, 112), AF.Abs, bias=-mid)
+        act(ap("A24", 0, 16), ap("P7", 80, 96))
+        act(ap("REL"), ap("AB"), AF.Relu, bias=2.0 ** 30, scale=-2.0 ** 24)
+        act(ap("KM"), ind(ap("KIN"), ap("OYU", 0, 8)), scale=nrow0)
+        act(ap("U0"), ap("KIN", lo, lo + 128), scale=row0)
+        act(ap("YC", 16, 144), ap("FT", lo, lo + 128))
+        act(ap("WK", 128, 256), ap("KIN", lo, lo + 128))
+        act(ap("WX", wx + 128, wx + 256), ap("XX", lo, lo + 128))
+        act(ap("N0"), nrep, scale=row0)
+        mm(ap("P6", 256, 384), ap("NH", 0, 128), ap("SELB"))
+        tt(ap("MKB", 0, 128), ap("P6", 256, 384), ap("MASK"), ALU.mult)
+        mm(ap("P4", 384, 512), ap("NH", 128, 256), ap("SELB"))
+        tt(ap("MKB", 128, 256), ap("P4", 384, 512), ap("MASK"), ALU.mult)
+        mm(ap("P7", 128, 152), ap("IDF"), ap("A24"), True, False)
+        mm(ap("P7", 128, 152), ap("IDB"), ap("REL", 0, 24), False, False)
+        mm(ap("P7", 128, 152), ap("IDB"), ap("REL", 24, 48), False, False)
+        mm(ap("P7", 128, 144), ap("MKB", 0, 128), ap("RBIG", 0, 16), False, False)
+        mm(ap("P7", 136, 144), ap("MKB", 128, 256), ap("RBIG", 0, 8), False, True)
+        tt(ap("U24"), ap("P7", 128, 152), ap("B24"), ALU.min)
+        cp(ap("OSC"), ap("U24"))
+        tag[:] = ["b" if t else "a", 0]
+        if t == 0:
+            mm(ap("P2", 0, 128), ap("TM", 0, 256, 2, p1=8), ap("S8", p1=8))
+            tt(ap("MKV"), ap("P2", 0, 128), ap("MASK"), ALU.mult)
+            mm(ap("P1", 0, 8), ap("MKV"), ap("RH", 0, 8))
+            for h in range(2):
+                cp(ap("OFF%d" % h, 0, 4), ap("P1", 4 * h, 4 * h + 4))
+            if EARLY:
+                cp(ap("OB"), ap("P1", 0, 8))
+        else:
+            tt(ap("TM", 0, 256, 2), ind(ap("TT"), ap("BIN", 8 * t - 8, 8 * t)), ap("MASK"), ALU.mult)
+            scan(ap("TS"), ap("SG"), ap("TM", 0, 256, 2), ALU.mult, ALU.add)
+            for h in range(2):
+                cp(ap("OFF%d" % h, 0, 4), ap("TS", 64 * h + 15, 64 * h + 64, 16))
+            if EARLY:
+                cp(ap("OB"), ap("TS", 15, 128, 16))
+            act(ap("KC", 0, 72, 9), ap("C16"), scale=ap("AIN", 4 * t - 4, 4 * t - 3), bias=kst)
+            if last:
+                dma("Y", ap("DT1"), ap("TT", 0, W, ps=16), "dd1", 57e3)
+                send(prv, ap("DT2"), ap("DT1"), "rt1", 57e3)
+                dma("Y", ap("TO", 0, W, ps=16), ap("DT2"), "dto", 57e3)
+        tag[:] = ["z", 0]
+        mm(ap("P5", 384, 512), zin, ap("IDB"))
+        act(ap("ZT"), ap("P5", 384, 512))
+        for h in range(2):
+            mm(ap("P%d" % (6 + h), 448, 512), ap("IDB"), ap("ZIN", 128 * t + 64 * h, 128 * t + 64 * h + 64))
+        for k in range(4):
+            mm(ap("P%d" % k), ap("ZT"), ap("EE", 512 * k, 512 * k + 512))
+
+        def names(h):
+            return ["%s%d" % (n, h) for n in ("OFF", "XG", "MX", "CF", "M", "E", "VL", "S2", "BE", "SW")]
+
+        def front(s, h):
+            off, xg, mx, cf = names(h)[:4]
+            xs, ms_ = [("%s%d" % (n, h + (2 if s == 0 and EARLY else 0))) for n in ("XS", "MS")]
+            tag[:] = ["f%d%d_" % (s, h), 0]
+            cp(ap(off, 4, 68), ind(ap("KIN"), ap(off, 0, 4)))
+            for c0, c1 in CUTS:
+                act(ap(xg, 16 * c0, 16 * c1), ind(ap("XX", W, 2 * W), ap(off, 4 + c0, 4 + c1)))
+                if turn and TURN:
+                    ops[-1]["after"] = turn[0]
+                turn[:] = [len(ops) - 1]
+            act(ap(xs, 0, 128, 2), ind(ap("XX", 0, W), ap(off, 0, 4)))
+            act(ap(cf, 1, 129, 2), ind(ap("KIN"), ap(off, 0, 4)))
+            tt(ap(ms_, 0, 128, 2), ap(xs, 0, 128, 2), ap("P%d" % (6 + h), 448, 512), ALU.max)
+            for c0, c1 in VCUTS:
+                z0 = 16 * c0 % 512
+                tt(ap(mx, 16 * c0, 16 * c1), ap(xg, 16 * c0, 16 * c1), ap("P%d" % (2 * h + c0 // 32), z0, z0 + 16 * (c1 - c0)), ALU.max)
+
+        def back(s, h):
+            off, xg, mx, cf, mm_, ee, vl, s2, be, sw = names(h)
+            late = s == 0 and EARLY
+            xs, ms_ = [("%s%d" % (n, h + (2 if late else 0))) for n in ("XS", "MS")]
+            kb, nb = "P%d" % (4 + h), "P%d" % (6 + h)
+            tag[:] = ["w%d%d_" % (s, h), 0]
+            mm(ap(nb, 0, 72), ap(cf, 1, 129), ap("PERM", 0, 72), True, False)
+            mm(ap(nb, 0, 72), ap(cf, 0, 128), ap("PERM", 72, 144), False, False)
+            stay = ap(nb, 0, 72, 9)
+            if late:
+                mm(stay, ap("KP", 128 * h, 128 * h + 128), ap("SELH", 0, 128, 16), False, False)
+            if s > 0:
+                mm(stay, ap("PAIR"), ap(sw, 0, 8), False, True)
+            elif t > 0:
+                mm(stay, ap("TM", 128 * h, 128 * h + 128), R8, False, True)
+            else:
+                mm(stay, ap("TM", 128 * h, 128 * h + 128, p1=8), ap("IDF", 0, 8, p1=8), False, True)
+            grp = [(ap(kb, 0, 72), ap("IDB"), ap("KC"))]
+            own = [(ap(kb, 0, 72, 9), ap(xs), ap("BOX")), (ap(kb, 0, 72, 9), ap(ms_), ap("BOM"))]
+            kin = [(ap(kb, 1 + k, 72, 9), ap(src, k, 1024, 8), ap(wt)) for src, wt in ((xg, "BOX"), (mx, "BOM")) for k in range(8)]
+            grp += kin + own if late else own + kin
+            for k, x in enumerate(grp):
+                mm(x[0], x[1], x[2], k == 0, k == len(grp) - 1)
+            key = ap(kb, 0, 72)
+            scan(ap(mm_), ap("RST"), key, ALU.add, ALU.min)
+            tt(ap(ee), key, ap(mm_), ALU.subtract)
+            tt(ap(vl), ap(nb, 0, 72), ap(ee), ALU.subtract)
+            mm(ap(kb, 128, 136), ap("SWAP"), ap(mm_, 8, 72, 9))
+            scan(ap(s2), ap(ee), ap(vl), ALU.min, ALU.max)
+            tt(ap(sw, 8, 16), ap(kb, 128, 136), ap(mm_, 8, 72, 9), ALU.is_gt)
+            tt(ap(sw, 0, 8), ap(s2, 8, 72, 9), ap(sw, 8, 16), ALU.mult)
+            tt(ap(be), ind(ap(sw, 0, 8), ap("CO", 8, 16)), ap("MASK2"), ALU.mult)
+            mm(ap(kb, 272, 276), ap(be), ap("RX2", 0, 64, 16))
+            if s < ST - 1:
+                cp(ap(off, 0, 4), ap(kb, 272, 276))
+            else:
+                bw = ap("BW", 8 * t + 4 * h, 8 * t + 4 * h + 4)
+                cp(bw, ap(kb, 272, 276))
+                act(ap("WF", 64 * h, 64 * h + 64), ind(ap("IOTA"), bw))
+                act(ap("A32", 8 + 4 * h, 12 + 4 * h), ap(kb, 272, 276))
+                cp(ap("KH", 64 * h, 64 * h + 64), ind(ap("KIN"), bw))
+                act(ap("XB", 64 * h, 64 * h + 64), ind(ap("XX", 0, W), bw))
+                act(ap("WK", 64 * h, 64 * h + 64), ind(ap("KIN"), bw))
+
+        if EARLY:
+            front(0, 0)
+            front(0, 1)
+        tag[:] = ["p", 0]
+        tt(ind(ap("KIN"), ap("OSC", 0, 8)), ap("KM"), ap("U0"), ALU.add)
+        act(ap("FT", lo, lo + 128), ind(ap("YC"), ap("OSC", 16, 24)))
+        cp(ind(ap("FT"), ap("OSC", 8, 16)), ap("YC", 16, 144))
+        act(ap("WF", 128, 256), ind(ap("YC"), ap("OSC", 16, 24)))
+        act(ap("NL", 0, 8), ap("U24", 16, 24), AF.Sign)
+        act(ap("NL", 8, 16), ap("NL", 0, 8), scale=2.0 ** -8 - 1.0, bias=1.0)
+        act(ap("NLX"), ind(ap("NL", 0, 8), ap("CO", 8, 16)), scale=4096.0)
+        if not last:
+            act(ap("AT", 8, 16), ap("NL", 0, 8), scale=-1.0, bias=-523.5 / 1024, acc=ap("AT", 16, 17))
+        if EARLY:
+            tag[:] = ["q", 0]
+            cp(ap("KP", 1, 256, 2), ind(ap("KIN"), ap("OB")))
+            mm(ap("P6", 0, 128), ap("KP", 1, 256, 2), ap("SELH"))
+            tt(ap("MKV"), ap("P6", 0, 128), ap("MASK"), ALU.mult)
+            mm(ap("P7", 0, 8), ap("MKV"), ap("RH", 0, 8))
+            cp(ap("OV"), ap("P7", 0, 8))
+            for h in range(2):
+                act(ap("XS%d" % (h + 2), 1, 128, 2), ind(ap("XX", W, 2 * W), ap("OV", 4 * h, 4 * h + 4)))
+                tt(ap("MS%d" % (h + 2), 1, 128, 2), ap("XS%d" % (h + 2), 1, 128, 2), ap("P%d" % (6 + h), 448, 512), ALU.max)
+        tag[:] = ["r", 0]
+        if last:
+            rest = [(c0, c1) for c0, c1 in ((B0, lo), (lo + 128, W)) if c0 < c1]
+            for c0, c1 in rest:
+                dma("Y", ("yx", 0, 128, 1, c0 - B0, c1 - B0), ap("XX", c0, c1), "dpre", 100e3)
+                dma("Y", ("yk", 0, 128, 1, c0 - B0, c1 - B0), ap("KIN", c0, c1), "dpre", 200e3)
+        for s in range(ST):
+            for h in range(2):
+                if s or not EARLY:
+                    front(s, h)
+                back(s, h)
+        tag[:] = ["e" if last else "s", 0]
+        bw = ap("BW", 8 * t, 8 * t + 8)
+        send(prv if last else nxt, ap("BIN", 8 * t, 8 * t + 8), bw, "rb%d" % t, 2e3)
+        brep = ap("WF", 0, 128)
+        mm(ap("P0", 0, 128), ap("IDB"), zin, True, False)
+        mm(ap("P0", 0, 128), ap("IDB"), ap("TRI", 128, 256), False, False)
+        mm(ap("P0", 0, 128), ap("IDB"), ap("XB"), False, True)
+        act(ap("TS"), ap("P0", 0, 128), scale=0.5, bias=MAGIC)
+        act(ap("WX", wx, wx + 128), ap("TS"), bias=-MAGIC)
+        if not last:
+            send(nxt, ap("ZIN", 128 * t + 128, 128 * t + 256), ap("WX", wx, wx + 128), "rz%d" % t, 32e3)
+        else:
+            dma("Y", ("yz",), ap("WX", wx, wx + 128), "dout", 32e3)
+        mm(ap("P2", 0, 128), ap("KH"), ap("SELH"))
+        tt(ap("MKV"), ap("P2", 0, 128), ap("MASK"), ALU.mult)
+        mm(ap("P3", 0, 8), ap("MKV"), ap("RH", 0, 8))
+        cp(ap("OV"), ap("P3", 0, 8))
+        act(ap("A32", 16, 24), ap("P3", 0, 8))
+        for d in range(2):
+            mm(ap("P1", 128 * d, 128 * d + 128), ap("IDB"), ap("TRI", 0, 128), True, False)
+            if d:
+                mm(ap("P1", 128, 256), ap("IDB"), ap("NLX"), False, False)
+            for h in range(2):
+                mm(ap("P1", 128 * d + 64 * h, 128 * d + 64 * h + 64), ap("BE%d" % h), ap("RX2"), False, h == 1)
+        for c in range(7):
+            ts(ap("EQ", 144 * c + 16, 128 * c + 128), ap("WF", 16 * c + 16, 128), ap("A32", 8 + c, 9 + c), ALU.is_equal,
+               ap("NL", 8 + c, 9 + c), ALU.mult)
+        tt(ap("EQ", 896, 1024), ap("P1", 0, 128), brep, ALU.is_equal)
+        tt(ap("EQ", 1024, 1152), ap("P1", 128, 256), brep, ALU.is_equal)
+        tt(ap("NH", 0, 128), ind(ap("FT"), ap("OV")), brep, ALU.not_equal)
+        act(ap("AB", 0, 8), ap("A32", 8, 16), AF.Abs, bias=-mid)
+        act(ap("RB"), ap("AB", 0, 8), AF.Relu, bias=2.0 ** 30, scale=-2.0 ** 24)
+        act(ap("KM"), ap("WK", 0, 128), scale=nrow0)
+        for c in range(9):
+            mm(ap("P6", 0, 128), ap("EQ", 128 * c, 128 * c + 128), ap("BLKS" if c == 7 else "BLK"), c == 0, c == 8)
+        tt(ap("MKB", 0, 128), ap("P6", 0, 128), ap("THR", 0, 128), ALU.is_ge)
+        mm(ap("P4", 128, 256), ap("NH", 0, 128), ap("SELB"))
+        tt(ap("MKB", 128, 256), ap("P4", 128, 256), ap("MASK"), ALU.mult)
+        ol = 32 * t
+        l1, l2, lh, lt = [ap("OL", ol + 8 * k, ol + 8 * k + 8) for k in range(4)]
+        for bk, c0, c1 in (("P7", 0, 16), ("P5", 16, 24)):
+            mm(ap(bk, c0, c1), ap("IDF"), ap("A32", c0, c1), True, False)
+            mm(ap(bk, c0, c1), ap("IDB"), ap("REL", c0, c1), False, False)
+            mm(ap(bk, c0, c1), ap("IDB"), ap("REL", 24 + c0, 24 + c1), False, False)
+            for c in range(c0, c1, 8):
+                mm(ap(bk, c, c + 8), ap("IDB"), ap("RB"), False, False)
+            mm(ap(bk, c0, c1), ap("MKB", 0, 128), ap("RBIG", 0, c1 - c0), False, c0 == 0)
+            if c0:
+                mm(ap(bk, c0, c1), ap("MKB", 128, 256), ap("RBIG", 0, 8), False, True)
+            tt(ap("U32", c0, c1), ap(bk, c0, c1), ap("B32", c0, c1), ALU.min)
+            cp(ap("OL", ol + c0, ol + c1), ap("U32", c0, c1))
+        if not last:
+            tt(ap("MKT"), ap("P6", 0, 128), ap("THR", 128, 256), ALU.is_ge)
+            mm(ap("P3", 24, 32), ap("IDF"), ap("A32", 8, 16), True, False)
+            mm(ap("P3", 24, 32), ap("MKT"), ap("RBIG", 0, 8), False, True)
+            tt(ap("U32", 24, 32), ap("P3", 24, 32), ap("B32", 24, 32), ALU.min)
+            cp(lt, ap("U32", 24, 32))
+        act(ap("FT", lo, lo + 128), ind(ap("WF"), l1))
+        tt(ind(ap("KIN"), l2), ap("KM"), ap("N0"), ALU.add)
+        act(ap("XX", lo, lo + 128), ind(ap("WX", wx, wx + 256), l1))
+        cp(ind(ap("FT"), lh), nrep)
+        act(ap("KIN", lo, lo + 128), ind(ap("WK"), l1))
+        if not last:
+            act(ap("XX", W + lo, W + lo + 128), ap("XX", lo, lo + 128))
+            act(ap("AT", 8, 16), ap("U32", 0, 8), scale=1.0 / 128, acc=ap("AT", 17, 18))
+            mm(ap("P4", 0, 1), ap("ONES"), ap("AT", 16, 17), True, False)
+            mm(ap("P4", 0, 1), ap("ONES"), ap("AT", 17, 18), False, True)
+            act(ap("AT", 0, 1), ap("P4", 0, 1), scale=1.0 / 32, bias=MAGIC)
+            act(ap("AT", 1, 2), ap("AT", 0, 1), scale=-32.0, bias=32.0 * MAGIC)
+            act(ap("AO", 4 * t, 4 * t + 1), ap("P4", 0, 1), bias=ap("AT", 1, 2))
+            send(nxt, ap("AIN", 4 * t, 4 * t + 4), ap("AO", 4 * t, 4 * t + 4), "ra%d" % t, 2e3)
+            if t < VIS - 2:
+                send(nxt, ap("LIN", 8 * t, 8 * t + 8), lt, "rl%d" % t, 2e3)
+            if t > 0:
+                cp(ind(ap("TT"), ap("LIN", 8 * t - 8, 8 * t)), brep)
+        else:
+            act(ap("TS"), ind(ap("IOTA"), ap("BIN", 8 * t, 8 * t + 8)))
+            cp(ind(ap("TO"), ap("OL", ol - 8, ol)), ap("TS"))
+            dma("Y", ("yt",), ap("TO", 0, W, ps=16), "dout", 57e3)
+            dma("Y", ("yx", 0, 128, 1, lo - B0, lo - B0 + 128), ap("XX", lo, lo + 128), "dout", 32e3)
+            dma("S", ("yf",), ap("FT", B0, W, ps=16), "dout", 16e3)
+            dma("S", ("yp",), ap("KIN", 0, B0, ps=16), "dout", 41e3)
+            dma("Y", ("yk", 0, 128, 1, lo - B0, lo - B0 + 128), ap("KIN", lo, lo + 128), "dout", 64e3)
+            for c0, c1 in rest:
+                dma("Y", ("yk", 0, 128, 16, c0 - B0, c1 - B0), ap("KIN", c0, c1, ps=16), "dout", 12e3, "dpre")
+    return ops
+
+
+def depend(ops):
+    hist = {}
+    bank = {}
+    deps = []
+    for i, o in enumerate(ops):
+        d = {}
+        acc = [(a, False) for a in o["r"]] + [(a, True) for a in o["w"]]
+        for a, wr in acc:
+            if psum(a):
+                bk = bank.setdefault(a["n"], [o["e"], []])
+                if bk[0] != o["e"]:
+                    bk[:] = [o["e"], [x[0] for x in hist[a["n"]]]]
+                    hist[a["n"]] = []
+                for j in bk[1]:
+                    d[j] = True
+            for (j, b, bw) in hist.get(a["n"], []):
+                if j != i and (wr or bw) and a["c0"] < b["c1"] and b["c0"] < a["c1"] and a["p0"] < b["p1"] and b["p0"] < a["p1"]:
+                    if ops[j]["k"] == "dma" and o["k"] == "dma" and ops[j]["sem"] == o["sem"]:
+                        continue
+                    if a["st"] == b["st"] > 1 and (a["c0"] - b["c0"]) % a["st"] and not psum(a):
+                        continue
+                    d[j] = d.get(j, False) or not (o["e"] == "P" and ops[j]["e"] == "P")
+        for a, wr in acc:
+            h = hist.setdefault(a["n"], [])
+            if psum(a):
+                if o["e"] == "P":
+                    h[:] = []
+            elif wr and a["st"] == 1 and a["ps"] == 1 and a["off"] is None:
+                h[:] = [x for x in h if x[0] == i or not (a["c0"] <= x[1]["c0"] and x[1]["c1"] <= a["c1"] and a["p0"] <= x[1]["p0"] and x[1]["p1"] <= a["p1"])]
+            elif wr and a["off"] is not None:
+                h[:] = [x for x in h if x[0] == i]
+            if o["e"] == "P":
+                h[:] = [x for x in h if ops[x[0]]["e"] != "P" or ops[x[0]]["w"][0]["n"] != o["w"][0]["n"] or x[2] != wr or x[1] != a]
+            h.append((i, a, wr))
+        if "after" in o:
+            d.setdefault(o["after"], False)
+        deps.append(d)
+    grp = {}
+    for i, o in enumerate(ops):
+        if o["k"] == "dma":
+            grp.setdefault(o["sem"], []).append(i)
+    for i, d in enumerate(deps):
+        if ops[i].get("behind"):
+            d[grp[ops[i]["behind"]][0]] = True
+        for j in list(d):
+            if ops[j]["k"] == "dma" and d[j]:
+                for k in grp[ops[j]["sem"]]:
+                    d[k] = True
+    lastmm = {}
+    for i, o in enumerate(ops):
+        if o["e"] == "P":
+            n = o["w"][0]["n"]
+            if n in lastmm:
+                deps[i].setdefault(lastmm[n], False)
+            lastmm[n] = i
+    return deps, grp
+
+
+def schedule(ops, deps):
+    n = len(ops)
+    users = [[] for _ in range(n)]
+    for i, d in enumerate(deps):
+        for j, s in d.items():
+            users[j].append((i, (HOP if s else 0.0) + (ops[j].get("lat", 0.0) if s or ops[i]["e"] == "R" else 0.0)))
+    prio = [0.0] * n
+    for i in range(n - 1, -1, -1):
+        prio[i] = ops[i]["c"] + max([ops[i].get("lat", 0.0)] + [prio[u] + w for u, w in users[i]])
+    prio = [p + NUDGE.get(o["cl"], 0.0) for p, o in zip(prio, ops)]
+    left = [len(d) for d in deps]
+    rdy = [0.0] * n
+    ready = {e: [] for e in "VSPGYR"}
+    for i in range(n):
+        if not left[i]:
+            ready[ops[i]["e"]].append(i)
+    free = {e: 0.0 for e in ready}
+    order = {e: [] for e in ready}
+    end = 0.0
+    seq = ops[0]["seq"] = []
+    for _ in range(n):
+        t0, e = min((max(free[e], min(rdy[i] for i in l)), e) for e, l in ready.items() if l)
+        i = max((i for i in ready[e] if rdy[i] <= t0 + SLACK), key=lambda k: (prio[k], -k))
+        ready[e].remove(i)
+        st = max(free[e], rdy[i])
+        free[e] = st + ops[i]["c"]
+        ops[i]["t"] = (st, free[e] + ops[i].get("lat", 0.0))
+        end = max(end, ops[i]["t"][1])
+        order[e].append(i)
+        seq.append(i)
+        for u, w in users[i]:
+            rdy[u] = max(rdy[u], free[e] + w)
+            left[u] -= 1
+            if not left[u]:
+                ready[ops[u]["e"]].append(u)
+    return order, end
+
+
+def plan(rank):
+    ops = build(rank)
+    deps, grp = depend(ops)
+    order, total = schedule(ops, deps)
+    pos = {}
+    for e, l in order.items():
+        for k, i in enumerate(l):
+            pos[i] = k
+    waits = {}
+    marked = set()
+    seen = {e: {} for e in order}
+    knew = {}
+    for i in ops[0]["seq"]:
+        e = ops[i]["e"]
+        need = {}
+        for j, s in deps[i].items():
+            if s:
+                o = ops[j]
+                if o["k"] == "dma":
+                    need[o["sem"]] = 16 * len(grp[o["sem"]])
+                elif o["k"] == "recv":
+                    need[o["sem"]] = NENG
+                else:
+                    need[o["e"]] = max(need.get(o["e"], -1), pos[j])
+        w = []
+        for k, v in sorted(need.items(), key=lambda x: -ops[order[x[0]][x[1]]]["t"][0] if x[0] in order else 0):
+            if seen[e].get(k, -1) < v:
+                w.append((k, v))
+                seen[e][k] = v
+                if k in order:
+                    marked.add(order[k][v])
+                    for k2, v2 in knew[order[k][v]].items():
+                        seen[e][k2] = max(seen[e].get(k2, -1), v2)
+        waits[i] = w
+        knew[i] = dict(seen[e])
+    return ops, order, waits, marked, grp, total
+
+
+def rank_program(g, core, T, topo):
+    rank = T.rank_of(core)
+    if rank is None:
+        return
+    ops, order, waits, marked, grp, total = plan(rank)
+    q = {"V": g.vector, "S": g.scalar, "P": g.tensor, "G": g, "Y": g.sync}
+    count = {}
+    for e in "VSPG":
+        c = 0
+        for k, i in enumerate(order[e]):
+            c += i in marked
+            count[e, k] = c
+
+    def real(a):
+        if isinstance(a, tuple):
+            return T[a[0]][:] if len(a) == 1 else T[a[0]][a[1]:a[2]:a[3], a[4]:a[5]]
+        if not isinstance(a, dict):
+            return a
+        if SCRATCH[a["n"]][0] == "dram":
+            return T[a["n"]][:]
+        x = T[a["n"]][a["p0"]:a["p1"]:a["ps"], a["c0"]:a["c1"]:a["st"]]
+        return x if a["off"] is None else x.indirect(real(a["off"]))
+
+    sent = 0
+    for e in "YSVPG":
+        E = q[e]
+        for i in order[e]:
+            o = ops[i]
+            for k, v in waits[i]:
+                if k in q:
+                    E.wait_ge(T.sem["c" + k], count[k, v])
+                else:
+                    E.wait_ge(T.sem[k], v)
+            a = [real(x) for x in o["a"]]
+            k = o["k"]
+            if k == "send":
+                dst = T.cores[a[0]]
+                rid, pid = topo.addr(dst, core)
+                m = sum(1 << x for x in topo.engines(core, dst)[:NENG])
+                g.remote_dma(a[1], a[2], T.sem[a[3]], T.sem["sent"], pid, rid, m)
+                sent += NENG
+                continue
+            if k == "dma":
+                E.dma_start(a[0], a[1]).then_inc(T.sem[o["sem"]], 16)
+                continue
+            if k == "copy":
+                x = E.tensor_copy(a[0], a[1])
+            elif k == "tt":
+                x = E.tensor_tensor(*a)
+            elif k == "ts":
+                x = E.tensor_scalar(*(a if a[5] is not None else a[:5]))
+            elif k == "scan":
+                x = E.tensor_tensor_scan(*a)
+            elif k == "memset":
+                x = E.memset(*a)
+            elif k == "act":
+                x = E.activation(a[0], a[1], a[2], bias=a[3], scale=a[4], accum_out=a[5])
+            elif k == "mm":
+                x = E.matmul(*a)
+            elif SCRATCH[o["a"][0]["n"]][2] == i32:
+                x = E.iota(*a)
+            else:
+                x = E.iota(*a, allow_small_or_imprecise_dtypes=True)
+            if i in marked:
+                x.then_inc(T.sem["c" + e], 1)
+    g.wait_ge(T.sem["sent"], sent)
+    g.sync.wait_ge(T.sem["dout"], 16 * len(grp["dout"]))

@@ -7,26 +7,27 @@ MAGIC = 12582912.0
 NENG = 8
 f32, bf, i32, u16 = "float32", "bfloat16", "int32", "uint16"
 h16 = "float16"
-CUTS = ((0, 16), (16, 32), (32, 48), (48, 64))
+CUTS = ((0, 32), (32, 48), (48, 64))
 VCUTS = CUTS
+SHIFT = ()
 EARLY = True
 TURN = True
 
 SB = {
     "KIN": (TW, f32), "FT": (TW, f32), "TT": (TW, f32), "TO": (TW, f32), "XX": (2 * W, bf), "IOTA": (W, f32),
-    "KRAW": (W, i32), "FRAW": (512, i32), "BRAW": (128, i32), "TRAW": (112, i32), "TCF": (112, f32), "EE": (2048, bf),
+    "KRAW": (W, i32), "FRAW": (512, i32), "BRAW": (128, i32), "TRAW": (112, i32), "TCF": (112, f32), "EE": (2560, bf),
     "PI": (8, i32), "PC": (16, f32), "JK": (72, f32), "J2": (128, f32), "JM": (256, f32), "JD": (128, f32), "J8": (32, f32),
     "JP": (144, f32), "MASK": (128, f32), "MASK2": (128, f32), "PAIR": (128, f32), "SWAP": (128, f32), "BLK": (128, bf),
     "BLKS": (128, bf), "IDB": (128, bf), "IDF": (128, f32), "SELX": (128, f32), "SELB": (128, bf), "SELH": (128, h16),
-    "R3": (24, f32), "RH": (24, h16), "RBIG": (16, bf), "RX2": (64, h16), "THR": (256, f32), "BOM": (8, bf), "BOX": (8, bf),
+    "R3": (24, f32), "RH": (24, h16), "RBIG": (16, bf), "RX2": (64, h16), "THR": (256, f32), "BOM": (8, bf), "BOX": (16, bf),
     "PERM": (144, f32), "KC": (72, bf), "RST": (72, f32), "SG": (128, f32), "CO": (16, u16), "TRI": (256, bf),
     "B24": (24, f32), "A24": (24, f32), "B32": (32, f32), "A32": (32, f32), "S8": (128, f32), "ONES": (128, f32),
-    "C16": (8, f32), "EQ": (9 * 128, bf), "MK": (256, h16), "MKB": (256, bf), "MKV": (128, h16), "MKT": (128, bf),
-    "KH": (128, h16), "OYU": (16, u16), "AB": (48, f32), "REL": (48, bf), "NL": (16, f32), "U32": (32, f32), "U24": (24, f32),
-    "OSC": (24, u16), "NLX": (128, bf), "KM": (128, f32), "U0": (128, f32), "N0": (128, f32), "YC": (144, f32),
-    "WK": (256, f32), "WF": (256, f32), "TM": (256, f32), "TS": (128, f32), "KP": (256, h16), "OB": (8, u16),
-    "XS2": (128, bf), "XS3": (128, bf), "MS2": (128, bf), "MS3": (128, bf), "ZT": (128, bf), "XB": (128, bf), "RB": (8, bf),
-    "OV": (8, u16), "NH": (256, bf), "AT": (24, f32),
+    "EQ": (9 * 128, bf), "MK": (256, h16), "MKB": (256, bf), "MKV": (128, h16), "MKT": (128, bf),
+    "KH": (128, h16), "OYU": (16, u16), "AB": (48, f32), "REL": (56, bf), "NL": (16, f32), "U32": (32, f32), "U24": (24, f32),
+    "OSC": (24, u16), "NLX": (128, bf), "KM": (128, f32), "U0": (128, f32), "N0": (512, f32), "YC": (144, f32),
+    "WK": (256, f32), "WF": (256, f32), "TM": (256, f32), "TS": (128, f32), "KP": (384, h16), "OB": (8, u16),
+    "XS2": (128, bf), "XS3": (128, bf), "MS2": (128, bf), "MS3": (128, bf), "ZT": (320, bf), "XB": (128, bf),
+    "OV": (16, u16), "NH": (256, bf), "AT": (32, f32), "NQ": (768, bf), "AQ": (256, f32),
 }
 for _h in range(2):
     SB.update({"OFF%d" % _h: (68, u16), "XG%d" % _h: (1024, bf), "MX%d" % _h: (1024, bf), "CF%d" % _h: (130, f32),
@@ -40,13 +41,15 @@ for _k in range(8):
 for _k in ("DT0", "DT1", "DT2"):
     SCRATCH[_k] = ("dram", [128, 112], f32)
 DMASEM = ["dk0", "dk1", "dk2", "dk3", "dpre", "dx0", "dx1", "dz", "df", "db", "dt", "dtt", "dd1", "dto", "dout"]
+DMASEM += ["d%s%d" % (k, t) for k in "ywv" for t in range(VIS)]
 RSEM = ["r%s%d" % (k, t) for k in "bzla" for t in range(VIS)] + ["rt0", "rt1"]
 SEMAPHORES = ["cV", "cS", "cP", "cG", "sent"] + DMASEM + RSEM
-CY = 0.83 * 1.2
-CG, CS, HOP, NET = 1.5, 3.5, 90.0, 2500.0
-PF, PE = 8, 0.55
-SLACK = 60.0
+CY = 0.9
+CG, CS, HOP, NET = 1.5, 3.5, 150.0, 3000.0
+PF, PE, FX = 8, 0.6, 50
+SLACK = 90.0
 NUDGE = {'f20_5': -1200, 'w21_8': 100, 'w01_3': -1100, 'w10_2': 3700, 's12': 2500, 's79': 2500, 'f21_11': -2500, 's70': -300, 'e24': -900, 'w21_3': -600, 'f01_6': 600, 's28': 2500, 'q3': -600, 'e37': -1200, 's40': 2500, 's22': 400, 's10': 1200, 'e53': 1500, 'e48': -1200, 's48': 100, 'w01_19': -600, 's46': -300, 'f11_5': 1200, 's20': -600, 's24': 300, 'w11_15': 600, 'e68': -2500, 'w00_0': -100, 'f10_5': -600, 'w01_9': 1200, 'e63': -1200, 'e28': -1200, 's4': -1200, 'w00_21': 1200, 'w10_16': -300, 'w21_19': -1200, 'w00_27': -600, 'o13': 500, 'w10_27': 2500, 'f10_1': 1200, 'i76': 600, 'i31': -1200, 'i72': 1200, 'w20_15': 2500, 'q6': -1200, 'f00_4': -400, 'w21_24': 3700, 'i41': -2500, 'f11_4': -300, 'i30': -3700, 'w20_16': 1200, 'i96': -600, 'i113': -100, 'i101': -2500, 'w01_30': 300, 'w10_23': 1200, 'f00_2': -1200, 's32': 100, 's77': 100, 'o7': 600, 's23': 300, 'w20_8': 100, 'i51': 300, 'w01_0': -600, 'w10_4': -1200, 'w01_29': 2500, 'f00_9': 1200, 'i124': -1200, 'b1': 2500, 'e73': 2500, 'b4': 2500, 'i6': -600, 'f00_11': -300, 'e61': 300, 'w20_32': 2500, 'f01_2': -100, 'w20_21': 1200, 'w00_10': 300, 's62': 300, 'p1': 900, 'w21_33': -1200, 'e27': -1200, 'i79': -600, 'w20_19': 100, 'f21_8': -600, 'e14': -100, 'a5': -2500, 'i118': 2500, 'e54': 300, 'w21_26': 100, 's71': -1200, 'e13': -300}
+NUDGE = {'q18': 5000, 'e2': -2500, 'i37': 2500, 'o16': -1200, 'e29': 5000, 'w11_23': -5000, 's3': 300, 'i127': 5000, 'i85': -2500, 'f00_5': 300, 'f11_7': -2500, 'q5': 1200, 'w11_7': 1200, 'i96': 300, 'f01_6': -300, 'a3': -100, 'q12': 100, 'w20_4': 2500, 'e63': 2500, 'w20_10': 600, 'i74': -2500, 'w00_18': 300, 'i33': -1200, 's58': 2500, 'i54': 100, 'w01_1': -100, 'w01_14': -1300, 'w20_27': 1200, 'w20_12': -5000, 's72': 1200, 'f10_1': -600, 'w21_35': -300, 'i59': -2500, 's28': -1200, 's45': -900, 'w00_22': 2500, 'w00_20': 1200, 'f21_0': 1200, 'f10_5': -2500, 'i66': -600, 'o22': -100, 'w21_31': -200, 'o9': -300, 'w01_4': -300, 'i91': 1200, 'i70': 4900, 'e39': 5000, 'o17': -1200, 's50': -1200, 'f20_6': -1200, 'i63': -100, 'e68': 600, 'i32': 600, 'i72': -2500, 'w10_24': 300, 'w21_32': 2500, 'e33': -2500, 'i47': 4700, 'f21_9': -1200, 's33': -100, 'w21_0': -6200, 'z5': -2500, 'w21_28': 600, 's48': 1300, 'i103': 5000, 's32': -100, 'e27': -2500, 'w00_19': 5000, 'f21_7': 1200, 'i71': -2500, 'o26': 1200, 'e13': -600, 'f20_2': 2500, 'o20': -600, 'f01_7': -2500, 'o12': 1200, 'e9': 5000, 'f21_6': -4700, 'w21_4': 100, 'f01_0': -600, 'f11_6': -2500, 'w21_25': -300, 'f00_1': -2200, 'w20_1': 100, 'i106': 1200, 'w01_5': -600, 'i81': -2500, 'f11_9': -5000, 'i42': -1200, 'e43': -300, 's38': 100, 's68': -100, 'e28': 2500, 'f11_4': 5000, 'w21_34': -5000, 'i94': -1200, 'f01_8': -2500, 'w00_25': 600, 's11': -700, 'w21_33': 300, 'w01_29': -300, 'f01_4': -300, 'i34': 600, 'w00_6': -2500, 'q15': 300, 's49': -1200, 'i99': 600, 'w00_7': -5000, 'f01_3': 600, 'r0': 600, 'w11_13': 600, 'i52': 300, 'f10_4': -100, 'f11_1': -2500, 'o5': -1200, 'e21': 600, 's53': 5000, 'i17': 1200, 's2': 100, 'w01_13': -5000, 'z7': -2500, 'w01_16': 2500, 'w01_19': 5000, 'o21': 300, 'i101': 2500, 's27': 300, 'w11_17': 2500, 'q9': 2200, 'w10_5': -1200, 'w10_0': 5000, 'w20_6': -6200, 'e7': -600, 'w01_32': 100, 'w00_21': -300, 'f00_4': 5000, 'i87': 600, 'w10_6': -5000, 'q8': -1200, 's75': 5000, 'i46': 5000, 'w00_33': 100, 'i107': -5000, 'e49': -1200, 'o1': -100, 'e25': 5000, 'i10': -600, 's39': 5000, 'w11_0': 600, 'i25': -2500, 'z3': 2500, 'w01_9': 1200, 'f01_5': 2500, 'i83': 2500, 'o18': -5000, 'w21_27': 2500, 'w21_23': 300, 'w11_31': -300, 'e57': 300, 'e3': 600, 'i27': -1200, 'e18': 300, 'w21_5': -5000, 'w21_8': -300, 'e6': -5000}
 
 
 def ap(name, c0=0, c1=None, st=1, p0=0, p1=128, ps=1, off=None):
@@ -101,10 +104,10 @@ def build(rank):
     def vcost(out, ins, per):
         n = width(out)
         if out["off"] is not None:
-            return 60 + n * CS * CY
+            return FX + 30 + n * CS * CY
         if ins[0]["off"] is not None:
-            return 60 + n * CG * CY
-        return 30 + max(64, n * per) * CY
+            return FX + 30 + n * CG * CY
+        return FX + max(64, n * per) * CY
 
     def cp(out, a):
         add("V", "copy", (out, a), [a], [out], vcost(out, [a], 0.5 if two(out) and two(a) else 1))
@@ -178,7 +181,7 @@ def build(rank):
     act(k0, podd, scale=1024.0)
     act(kst, podd, scale=1024.0 - 15.5 * 65536, bias=15.5 * 65536)
     act(ap("KC", 0, 72, 9), ap("JK", 0, 72, 9), bias=k0)
-    act(ap("C16"), ap("JK", 0, 72, 9), bias=ap("PC", 12, 13))
+    act(ap("AT", 24, 32), ap("JK", 0, 72, 9), bias=ap("PC", 12, 13))
     act(ap("BLKS"), ap("BLK"), scale=2.0 ** -8)
     ts(ap("SELX"), ap("JD"), pdiv, ALU.is_equal, row0, ALU.mult)
     ts(ap("SELH"), ap("JD"), pdiv, ALU.is_equal, row0, ALU.mult)
@@ -192,12 +195,13 @@ def build(rank):
     act(ap("THR", 0, 128), ap("MASK"), scale=-1023.25, bias=1024.0)
     act(ap("THR", 128, 256), ap("MASK"), scale=-1024.0 + 2.0 ** -9, bias=1024.0)
     act(ap("BOM"), ap("R3", 0, 8), scale=2.0 ** 17)
-    act(ap("BOX"), ap("R3", 0, 8), scale=-2.0 ** 16)
+    act(ap("BOX", 0, 8), ap("R3", 0, 8), scale=-2.0 ** 16)
+    act(ap("BOX", 8, 16), ap("SELX", 0, 128, 16), scale=2.0 ** 32)
     ts(ap("PERM"), ap("JP"), pid, ALU.is_equal)
     ms(ap("PERM", 0, 144, 9), 0.0)
     tt(ap("SWAP"), ap("PAIR"), ap("IDF"), ALU.subtract)
     ms(ap("RST"), 0.0)
-    ms(ap("RST", 0, 72, 9), 2.0 ** 40)
+    ms(ap("RST", 0, 72, 9), 2.0 ** 60)
     act(ap("SG"), ap("JM", 0, 128), AF.Sign)
     cp(ap("CO", 8, 16), ap("J8", 0, 8))
     ts(ap("TRI", 0, 128), ap("JM", 0, 128), pmod, ALU.is_le, 4096.0, ALU.mult)
@@ -217,8 +221,11 @@ def build(rank):
         act(ap("CF%d" % h), ap("JM", 0, 130), scale=0.0)
     act(ap("TM"), ap("JM"), scale=0.0)
     if EARLY:
-        ms(ap("KP"), 0.0)
+        ms(ap("KP", 0, 256), 0.0)
+        ms(ap("NQ"), 0.0)
     ms(ap("EQ", 0, 896), 0.0)
+    if SHIFT:
+        ms(ap("XG1", 0, 512), 0.0)
     for k in range(16):
         (cp if k % 2 else act)(ap("EE", k, 2048, 16), ap("IDF"))
     for c in range(4):
@@ -229,6 +236,7 @@ def build(rank):
     act(ap("FT", B0, W), ap("P3"))
     iota(ap("IOTA", B0, W), [[1, W - B0]], B0)
     iota(ap("FT", 0, B0), [[0, B0]], -1)
+    act(ap("N0"), ap("IOTA", B0, W), scale=row0)
     cp(ap("TCF"), ap("TRAW"))
     send(nxt, ap("DT0"), ap("TCF"), "rt0", 57e3)
     iota(ap("IOTA", 128, B0), [[1, B0 - 128]], 128)
@@ -259,13 +267,12 @@ def build(rank):
         tt(ap("NH", 128, 256), ind(ap("FT"), ap("OYU", 8, 16)), nrep, ALU.not_equal)
         act(ap("AB"), ap("P7", 64, 112), AF.Abs, bias=-mid)
         act(ap("A24", 0, 16), ap("P7", 80, 96))
-        act(ap("REL"), ap("AB"), AF.Relu, bias=2.0 ** 30, scale=-2.0 ** 24)
+        act(ap("REL", 0, 48), ap("AB"), AF.Relu, bias=2.0 ** 30, scale=-2.0 ** 24)
         act(ap("KM"), ind(ap("KIN"), ap("OYU", 0, 8)), scale=nrow0)
         act(ap("U0"), ap("KIN", lo, lo + 128), scale=row0)
-        act(ap("YC", 16, 144), ap("FT", lo, lo + 128))
-        act(ap("WK", 128, 256), ap("KIN", lo, lo + 128))
-        act(ap("WX", wx + 128, wx + 256), ap("XX", lo, lo + 128))
-        act(ap("N0"), nrep, scale=row0)
+        dma("Y", ap("YC", 16, 144), ap("FT", lo, lo + 128), "dy%d" % t, 64e3)
+        dma("Y", ap("WK", 128, 256), ap("KIN", lo, lo + 128), "dw%d" % t, 64e3)
+        dma("Y", ap("WX", wx + 128, wx + 256), ap("XX", lo, lo + 128), "dw%d" % t, 32e3)
         mm(ap("P6", 256, 384), ap("NH", 0, 128), ap("SELB"))
         tt(ap("MKB", 0, 128), ap("P6", 256, 384), ap("MASK"), ALU.mult)
         mm(ap("P4", 384, 512), ap("NH", 128, 256), ap("SELB"))
@@ -282,29 +289,27 @@ def build(rank):
             mm(ap("P2", 0, 128), ap("TM", 0, 256, 2, p1=8), ap("S8", p1=8))
             tt(ap("MKV"), ap("P2", 0, 128), ap("MASK"), ALU.mult)
             mm(ap("P1", 0, 8), ap("MKV"), ap("RH", 0, 8))
-            for h in range(2):
-                cp(ap("OFF%d" % h, 0, 4), ap("P1", 4 * h, 4 * h + 4))
-            if EARLY:
-                cp(ap("OB"), ap("P1", 0, 8))
+            cp(ap("OB"), ap("P1", 0, 8))
         else:
             tt(ap("TM", 0, 256, 2), ind(ap("TT"), ap("BIN", 8 * t - 8, 8 * t)), ap("MASK"), ALU.mult)
             scan(ap("TS"), ap("SG"), ap("TM", 0, 256, 2), ALU.mult, ALU.add)
-            for h in range(2):
-                cp(ap("OFF%d" % h, 0, 4), ap("TS", 64 * h + 15, 64 * h + 64, 16))
-            if EARLY:
-                cp(ap("OB"), ap("TS", 15, 128, 16))
-            act(ap("KC", 0, 72, 9), ap("C16"), scale=ap("AIN", 4 * t - 4, 4 * t - 3), bias=kst)
+            cp(ap("OB"), ap("TS", 15, 128, 16))
+            act(ap("KC", 0, 72, 9), ap("AT", 24, 32), scale=ap("AIN", 4 * t - 4, 4 * t - 3), bias=kst)
             if last:
                 dma("Y", ap("DT1"), ap("TT", 0, W, ps=16), "dd1", 57e3)
                 send(prv, ap("DT2"), ap("DT1"), "rt1", 57e3)
                 dma("Y", ap("TO", 0, W, ps=16), ap("DT2"), "dto", 57e3)
         tag[:] = ["z", 0]
         mm(ap("P5", 384, 512), zin, ap("IDB"))
-        act(ap("ZT"), ap("P5", 384, 512))
+        act(ap("ZT", 0, 128), ap("P5", 384, 512))
+        if SHIFT:
+            act(ap("ZT", 128, 256), ap("P5", 384, 512), scale=-1.0)
+            for k in range(2):
+                act(ap("ZT", 256 + k, 320, 2), ap("ZIN", 128 * t + 64, 128 * t + 96))
         for h in range(2):
             mm(ap("P%d" % (6 + h), 448, 512), ap("IDB"), ap("ZIN", 128 * t + 64 * h, 128 * t + 64 * h + 64))
-        for k in range(4):
-            mm(ap("P%d" % k), ap("ZT"), ap("EE", 512 * k, 512 * k + 512))
+        for k in (0, 1, 3) if SHIFT else range(4):
+            mm(ap("P%d" % k), ap("ZT", 0, 128), ap("EE", 512 * k, 512 * k + 512))
 
         def names(h):
             return ["%s%d" % (n, h) for n in ("OFF", "XG", "MX", "CF", "M", "E", "VL", "S2", "BE", "SW")]
@@ -313,17 +318,23 @@ def build(rank):
             off, xg, mx, cf = names(h)[:4]
             xs, ms_ = [("%s%d" % (n, h + (2 if s == 0 and EARLY else 0))) for n in ("XS", "MS")]
             tag[:] = ["f%d%d_" % (s, h), 0]
-            cp(ap(off, 4, 68), ind(ap("KIN"), ap(off, 0, 4)))
+            at = ap(off, 0, 4) if s else ap("OB", 4 * h, 4 * h + 4)
+            cp(ap(off, 4, 68), ind(ap("KIN"), at))
             for c0, c1 in CUTS:
-                act(ap(xg, 16 * c0, 16 * c1), ind(ap("XX", W, 2 * W), ap(off, 4 + c0, 4 + c1)))
+                act(ap("EE", 2048, 2560) if h in SHIFT and c0 == 0 else ap(xg, 16 * c0, 16 * c1), ind(ap("XX", W, 2 * W), ap(off, 4 + c0, 4 + c1)))
                 if turn and TURN:
                     ops[-1]["after"] = turn[0]
                 turn[:] = [len(ops) - 1]
-            act(ap(xs, 0, 128, 2), ind(ap("XX", 0, W), ap(off, 0, 4)))
-            act(ap(cf, 1, 129, 2), ind(ap("KIN"), ap(off, 0, 4)))
+            act(ap(xs, 0, 128, 2), ind(ap("XX", 0, W), at))
+            act(ap(cf, 1, 129, 2), ind(ap("KIN"), at))
             tt(ap(ms_, 0, 128, 2), ap(xs, 0, 128, 2), ap("P%d" % (6 + h), 448, 512), ALU.max)
             for c0, c1 in VCUTS:
                 z0 = 16 * c0 % 512
+                if h in SHIFT and c0 == 0:
+                    mm(ap("P2"), ap("ZT", 128, 256), ap("EE", 1024, 1536), True, False)
+                    mm(ap("P2"), ap("IDB"), ap("EE", 2048, 2560), False, True)
+                    act(ap(mx, 0, 512), ap("P2"), AF.Abs, scale=0.5)
+                    continue
                 tt(ap(mx, 16 * c0, 16 * c1), ap(xg, 16 * c0, 16 * c1), ap("P%d" % (2 * h + c0 // 32), z0, z0 + 16 * (c1 - c0)), ALU.max)
 
         def back(s, h):
@@ -344,9 +355,12 @@ def build(rank):
             else:
                 mm(stay, ap("TM", 128 * h, 128 * h + 128, p1=8), ap("IDF", 0, 8, p1=8), False, True)
             grp = [(ap(kb, 0, 72), ap("IDB"), ap("KC"))]
-            own = [(ap(kb, 0, 72, 9), ap(xs), ap("BOX")), (ap(kb, 0, 72, 9), ap(ms_), ap("BOM"))]
-            kin = [(ap(kb, 1 + k, 72, 9), ap(src, k, 1024, 8), ap(wt)) for src, wt in ((xg, "BOX"), (mx, "BOM")) for k in range(8)]
-            grp += kin + own if late else own + kin
+            if h in SHIFT:
+                grp.append((ap(kb, 0, 72, 9, p1=64), ap("ZT", 256, 320), ap("BOX", 0, 8)))
+            own = [(ap(kb, 0, 72, 9), ap(xs), ap("BOX", 0, 8)), (ap(kb, 0, 72, 9), ap(ms_), ap("BOM"))]
+            kin = [(ap(kb, 1 + k, 72, 9), ap(src, k, 1024, 8), ap(wt, 0, 8)) for src, wt in ((xg, "BOX"), (mx, "BOM")) for k in range(8)]
+            shut = [(ap(kb, 0, 72, 9), ap("NQ", 256 * k + 128 * h, 256 * k + 128 * h + 128), ap("BOX", 8, 16)) for k in (1, 2, 0)]
+            grp += kin + shut + own if late else own + kin
             for k, x in enumerate(grp):
                 mm(x[0], x[1], x[2], k == 0, k == len(grp) - 1)
             key = ap(kb, 0, 72)
@@ -373,26 +387,37 @@ def build(rank):
         if EARLY:
             front(0, 0)
             front(0, 1)
+            tag[:] = ["q", 0]
+            cp(ap("KP", 256, 384), ind(ap("KIN"), ap("OB")))
+            mm(ap("P5", 128, 256), ap("KP", 256, 384), ap("SELH"))
+            tt(ap("MKV"), ap("P5", 128, 256), ap("MASK"), ALU.mult)
+            mm(ap("P5", 256, 264), ap("MKV"), ap("RH", 0, 8))
+            cp(ap("OV", 8, 16), ap("P5", 256, 264))
+            act(ap("TS"), ind(ap("IOTA"), ap("OB")))
+            cp(ap("KP", 1, 256, 2), ind(ap("KIN"), ap("OV", 8, 16)))
+            tt(ap("NQ", 1, 256, 2), ind(ap("FT"), ap("OV", 8, 16)), ap("TS"), ALU.not_equal)
+            mm(ap("P5", 128, 256), ap("KP", 1, 256, 2), ap("SELH"))
+            tt(ap("MKV"), ap("P5", 128, 256), ap("MASK"), ALU.mult)
+            mm(ap("P5", 256, 264), ap("MKV"), ap("RH", 0, 8))
+            cp(ap("OV", 0, 8), ap("P5", 256, 264))
+            for h in range(2):
+                act(ap("XS%d" % (h + 2), 1, 128, 2), ind(ap("XX", W, 2 * W), ap("OV", 4 * h, 4 * h + 4)))
+                tt(ap("MS%d" % (h + 2), 1, 128, 2), ap("XS%d" % (h + 2), 1, 128, 2), ap("P%d" % (6 + h), 448, 512), ALU.max)
+            act(ap("AQ", 0, 128), ap("TS"), AF.Abs, bias=-mid)
+            act(ap("NQ", 257, 512, 2), ap("AQ", 0, 128), AF.Relu, scale=-1.0, bias=64.0)
+            for h in range(2):
+                act(ap("AQ", 128 + 64 * h, 192 + 64 * h), ap("CF%d" % h, 1, 129, 2), AF.Abs, bias=-mid)
+            act(ap("NQ", 513, 768, 2), ap("AQ", 128, 256), AF.Relu, bias=-64.0)
         tag[:] = ["p", 0]
         tt(ind(ap("KIN"), ap("OSC", 0, 8)), ap("KM"), ap("U0"), ALU.add)
         act(ap("FT", lo, lo + 128), ind(ap("YC"), ap("OSC", 16, 24)))
         cp(ind(ap("FT"), ap("OSC", 8, 16)), ap("YC", 16, 144))
-        act(ap("WF", 128, 256), ind(ap("YC"), ap("OSC", 16, 24)))
+        dma("Y", ap("WF", 128, 256), ap("FT", lo, lo + 128), "dv%d" % t, 64e3)
         act(ap("NL", 0, 8), ap("U24", 16, 24), AF.Sign)
         act(ap("NL", 8, 16), ap("NL", 0, 8), scale=2.0 ** -8 - 1.0, bias=1.0)
         act(ap("NLX"), ind(ap("NL", 0, 8), ap("CO", 8, 16)), scale=4096.0)
         if not last:
             act(ap("AT", 8, 16), ap("NL", 0, 8), scale=-1.0, bias=-523.5 / 1024, acc=ap("AT", 16, 17))
-        if EARLY:
-            tag[:] = ["q", 0]
-            cp(ap("KP", 1, 256, 2), ind(ap("KIN"), ap("OB")))
-            mm(ap("P6", 0, 128), ap("KP", 1, 256, 2), ap("SELH"))
-            tt(ap("MKV"), ap("P6", 0, 128), ap("MASK"), ALU.mult)
-            mm(ap("P7", 0, 8), ap("MKV"), ap("RH", 0, 8))
-            cp(ap("OV"), ap("P7", 0, 8))
-            for h in range(2):
-                act(ap("XS%d" % (h + 2), 1, 128, 2), ind(ap("XX", W, 2 * W), ap("OV", 4 * h, 4 * h + 4)))
-                tt(ap("MS%d" % (h + 2), 1, 128, 2), ap("XS%d" % (h + 2), 1, 128, 2), ap("P%d" % (6 + h), 448, 512), ALU.max)
         tag[:] = ["r", 0]
         if last:
             rest = [(c0, c1) for c0, c1 in ((B0, lo), (lo + 128, W)) if c0 < c1]
@@ -420,7 +445,7 @@ def build(rank):
         mm(ap("P2", 0, 128), ap("KH"), ap("SELH"))
         tt(ap("MKV"), ap("P2", 0, 128), ap("MASK"), ALU.mult)
         mm(ap("P3", 0, 8), ap("MKV"), ap("RH", 0, 8))
-        cp(ap("OV"), ap("P3", 0, 8))
+        cp(ap("OV", 0, 8), ap("P3", 0, 8))
         act(ap("A32", 16, 24), ap("P3", 0, 8))
         for d in range(2):
             mm(ap("P1", 128 * d, 128 * d + 128), ap("IDB"), ap("TRI", 0, 128), True, False)
@@ -433,9 +458,9 @@ def build(rank):
                ap("NL", 8 + c, 9 + c), ALU.mult)
         tt(ap("EQ", 896, 1024), ap("P1", 0, 128), brep, ALU.is_equal)
         tt(ap("EQ", 1024, 1152), ap("P1", 128, 256), brep, ALU.is_equal)
-        tt(ap("NH", 0, 128), ind(ap("FT"), ap("OV")), brep, ALU.not_equal)
+        tt(ap("NH", 0, 128), ind(ap("FT"), ap("OV", 0, 8)), brep, ALU.not_equal)
         act(ap("AB", 0, 8), ap("A32", 8, 16), AF.Abs, bias=-mid)
-        act(ap("RB"), ap("AB", 0, 8), AF.Relu, bias=2.0 ** 30, scale=-2.0 ** 24)
+        act(ap("REL", 48, 56), ap("AB", 0, 8), AF.Relu, bias=2.0 ** 30, scale=-2.0 ** 24)
         act(ap("KM"), ap("WK", 0, 128), scale=nrow0)
         for c in range(9):
             mm(ap("P6", 0, 128), ap("EQ", 128 * c, 128 * c + 128), ap("BLKS" if c == 7 else "BLK"), c == 0, c == 8)
@@ -449,7 +474,7 @@ def build(rank):
             mm(ap(bk, c0, c1), ap("IDB"), ap("REL", c0, c1), False, False)
             mm(ap(bk, c0, c1), ap("IDB"), ap("REL", 24 + c0, 24 + c1), False, False)
             for c in range(c0, c1, 8):
-                mm(ap(bk, c, c + 8), ap("IDB"), ap("RB"), False, False)
+                mm(ap(bk, c, c + 8), ap("IDB"), ap("REL", 48, 56), False, False)
             mm(ap(bk, c0, c1), ap("MKB", 0, 128), ap("RBIG", 0, c1 - c0), False, c0 == 0)
             if c0:
                 mm(ap(bk, c0, c1), ap("MKB", 128, 256), ap("RBIG", 0, 8), False, True)
@@ -462,7 +487,7 @@ def build(rank):
             tt(ap("U32", 24, 32), ap("P3", 24, 32), ap("B32", 24, 32), ALU.min)
             cp(lt, ap("U32", 24, 32))
         act(ap("FT", lo, lo + 128), ind(ap("WF"), l1))
-        tt(ind(ap("KIN"), l2), ap("KM"), ap("N0"), ALU.add)
+        tt(ind(ap("KIN"), l2), ap("KM"), ap("N0", lo - B0, lo - B0 + 128), ALU.add)
         act(ap("XX", lo, lo + 128), ind(ap("WX", wx, wx + 256), l1))
         cp(ind(ap("FT"), lh), nrep)
         act(ap("KIN", lo, lo + 128), ind(ap("WK"), l1))

@@ -1,60 +1,78 @@
-from concourse.mybir import AluOpType as ALU, ActivationFunctionType as AF
+from concourse.mybir import AluOpType as ALU, ActivationFunctionType as AF, AxisListType as AX
 
 W, B0, NR, VIS, ST = 1792, 1280, 4, 5, 3
-TR = 1808
-TW = TR + 128
+GW = W + 16
+SP = 2048
+ZONE = 2304
+TW = SP + 128
 MAGIC = 12582912.0
 NENG = 8
-f32, bf, i32, u16 = "float32", "bfloat16", "int32", "uint16"
-h16 = "float16"
+f32, bf, i32, u16, h16 = "float32", "bfloat16", "int32", "uint16", "float16"
 CUTS = ((0, 32), (32, 48), (48, 64))
-VCUTS = CUTS
-SHIFT = ()
-EARLY = True
-TURN = True
+VCUTS = ((0, 16), (16, 32), (32, 48), (48, 64))
+HBS = False
+QMASK = (0,)
+OMASK = True
+KW = 216
+WKEY = (34816.0, 37120.0, 2304.0)
+WINC = (2048.0, 2064.0, 16.0)
+HIGH = 132 - 7.5 / 16
+WCAND = (-4160.0, 0.0, 2112.0)
+WSTAY = (-4096.0, -4096.0, -2048.0)
 
 SB = {
-    "KIN": (TW, f32), "FT": (TW, f32), "TT": (TW, f32), "TO": (TW, f32), "XX": (2 * W, bf), "IOTA": (W, f32),
-    "KRAW": (W, i32), "FRAW": (512, i32), "BRAW": (128, i32), "TRAW": (112, i32), "TCF": (112, f32), "EE": (2560, bf),
-    "PI": (8, i32), "PC": (16, f32), "JK": (72, f32), "J2": (128, f32), "JM": (256, f32), "JD": (128, f32), "J8": (32, f32),
-    "JP": (144, f32), "MASK": (128, f32), "MASK2": (128, f32), "PAIR": (128, f32), "SWAP": (128, f32), "BLK": (128, bf),
-    "BLKS": (128, bf), "IDB": (128, bf), "IDF": (128, f32), "SELX": (128, f32), "SELB": (128, bf), "SELH": (128, h16),
-    "R3": (24, f32), "RH": (24, h16), "RBIG": (16, bf), "RX2": (64, h16), "THR": (256, f32), "BOM": (8, bf), "BOX": (16, bf),
-    "PERM": (144, f32), "KC": (72, bf), "RST": (72, f32), "SG": (128, f32), "CO": (16, u16), "TRI": (256, bf),
-    "B24": (24, f32), "A24": (24, f32), "B32": (32, f32), "A32": (32, f32), "S8": (128, f32), "ONES": (128, f32),
-    "EQ": (9 * 128, bf), "MK": (256, h16), "MKB": (256, bf), "MKV": (128, h16), "MKT": (128, bf),
-    "KH": (128, h16), "OYU": (16, u16), "AB": (48, f32), "REL": (56, bf), "NL": (16, f32), "U32": (32, f32), "U24": (24, f32),
-    "OSC": (24, u16), "NLX": (128, bf), "KM": (128, f32), "U0": (128, f32), "N0": (512, f32), "YC": (144, f32),
-    "WK": (256, f32), "WF": (256, f32), "TM": (256, f32), "TS": (128, f32), "KP": (384, h16), "OB": (8, u16),
-    "XS2": (128, bf), "XS3": (128, bf), "MS2": (128, bf), "MS3": (128, bf), "ZT": (320, bf), "XB": (128, bf),
-    "OV": (16, u16), "NH": (256, bf), "AT": (32, f32), "NQ": (768, bf), "AQ": (256, f32),
+    "KIN": (TW, f32), "FT": (TW, f32), "TT": (TW + ZONE, f32), "TO": (TW + ZONE, f32), "XX": (2 * GW, bf), "IOTA": (W, f32),
+    "KRAW": (W, i32), "FRAW": (512, i32), "BRAW": (128, i32), "TRAW": (112, i32), "TCF": (112, f32), "FF": (640, f32),
+    "PI": (8, i32), "PC": (24, f32), "J2": (128, f32), "JM": (256, f32), "JD": (128, f32), "J8": (32, f32), "JB": (1024, f32),
+    "JP": (432, f32), "J3": (24, f32), "MASK2": (128, f32), "SWAP": (128, f32), "IDB": (128, bf), "IDH": (128, h16),
+    "IDF": (128, f32), "IDQ": (128, bf), "ID2K": (128, bf), "SELB": (128, bf), "SEL8": (8, h16), "SELP": (24, bf),
+    "SW1": (144, h16), "SWB": (144, h16), "RX4": (4, h16), "RX32": (32, h16), "RXB": (512, h16), "EV": (64, h16),
+    "TRA": (1024, bf), "PERM": (464, h16), "PERH": (432, bf), "PTMP": (432, f32), "T1": (48, bf), "PAIR": (128, f32),
+    "HUGE": (8, bf), "XU": (144, bf), "OP": (8, u16), "TY": (128, f32), "TZ": (128, f32), "MASK": (128, f32), "SELH": (128, h16), "RH": (8, h16),
+    "RBIG": (8, h16), "SGN": (128, f32), "EE": (1024, bf), "ZT": (256, bf), "BR": (128, f32), "MO": (256, h16),
+    "LO": (KW, h16),
+    "W24": (96, f32), "RW": (24, f32), "RWB": (24, bf), "BOX": (24, bf), "BOM": (24, bf), "SH": (72, bf), "EVN": (256, bf),
+    "AE": (128, bf), "RST": (KW, f32), "CO": (8, u16), "QUART": (64, bf), "B24": (24, f32), "A24": (24, f32),
+    "S8": (128, f32), "ONES": (128, f32), "CD1": (64, f32), "CD2": (16, f32), "D0": (64, f32), "SO": (64, f32),
+    "LH": (16, f32), "LANE": (8, f32), "TABN": (144, bf), "NLR": (128, bf), "SG": (16, bf), "YU": (128, h16), "KH": (128, h16),
+    "OYU": (16, u16), "AB": (24, f32), "REL": (16, bf), "U24": (24, f32), "OSC": (24, u16), "KM": (128, f32), "U0": (128, f32),
+    "N0": (512, f32), "YC": (144, f32), "WK": (256, f32), "WF": (256, f32), "TM": (256, h16), "TS": (128, f32),
+    "OB": (16, u16), "OG": (8, u16), "B1": (8, u16), "B2": (8, u16), "BF": (8, f32), "XB": (128, bf), "OV": (8, u16),
+    "NH": (256, h16), "NV": (128, h16), "AT": (32, f32), "AV": (8, f32),
 }
 for _h in range(2):
-    SB.update({"OFF%d" % _h: (68, u16), "XG%d" % _h: (1024, bf), "MX%d" % _h: (1024, bf), "CF%d" % _h: (130, f32),
-               "XS%d" % _h: (128, bf), "MS%d" % _h: (128, bf), "SW%d" % _h: (16, f32), "M%d" % _h: (72, f32),
-               "E%d" % _h: (72, f32), "VL%d" % _h: (72, f32), "S2%d" % _h: (72, f32), "BE%d" % _h: (128, h16)})
-SB.update({"WX": (256 * VIS, bf), "ZIN": (128 * VIS, bf), "BW": (8 * VIS, u16), "BIN": (8 * VIS, u16),
+    SB.update({"OFF%d" % _h: (64, u16), "XG%d" % _h: (1024, bf), "MX%d" % _h: (1024, bf), "CF%d" % _h: (130, h16),
+               "HB%d" % _h: (130, bf), "XS%d" % _h: (128, bf), "MS%d" % _h: (128, bf), "M%d" % _h: (KW, f32),
+               "MN%d" % _h: (8, f32), "S3%d" % _h: (24, f32), "BE%d" % _h: (128, h16), "BU%d" % _h: (128, h16),
+               "KP%d" % _h: (128, h16), "HP%d" % _h: (128, bf), "FL%d" % _h: (256, bf), "NQ%d" % _h: (128, bf)})
+SB.update({"WX": (256 * VIS, bf), "ZIN": (128 * VIS, bf), "BW": (16 * VIS, u16), "BIN": (16 * VIS, u16),
            "OL": (32 * VIS, u16), "LIN": (8 * VIS, u16), "AO": (4 * VIS, f32), "AIN": (4 * VIS, f32)})
-SCRATCH = {k: ("sbuf", [128, v[0]], v[1]) for k, v in SB.items()}
+BUF = {k: ("sbuf", [128, v[0]], v[1]) for k, v in SB.items()}
 for _k in range(8):
-    SCRATCH["P%d" % _k] = ("psum", [128, 512], f32)
+    BUF["P%d" % _k] = ("psum", [128, 512], f32)
 for _k in ("DT0", "DT1", "DT2"):
-    SCRATCH[_k] = ("dram", [128, 112], f32)
+    BUF[_k] = ("dram", [128, 112], f32)
+SCRATCH, PLACE, _end = {}, {}, {}
+for _k, _v in BUF.items():
+    if _v[0] == "sbuf" and _v[1][1] <= 64:
+        PLACE[_k] = ("S" + _v[2], _end.get(_v[2], 0))
+        _end[_v[2]] = PLACE[_k][1] - (-_v[1][1] // 16) * 16
+        SCRATCH["S" + _v[2]] = ("sbuf", [128, _end[_v[2]]], _v[2])
+    else:
+        PLACE[_k] = (_k, 0)
+        SCRATCH[_k] = _v
 DMASEM = ["dk0", "dk1", "dk2", "dk3", "dpre", "dx0", "dx1", "dz", "df", "db", "dt", "dtt", "dd1", "dto", "dout"]
 DMASEM += ["d%s%d" % (k, t) for k in "ywv" for t in range(VIS)]
-RSEM = ["r%s%d" % (k, t) for k in "bzla" for t in range(VIS)] + ["rt0", "rt1"]
+RSEM = ["r%s%d" % (k, t) for k in "bczyla" for t in range(VIS)] + ["rt0", "rt1"]
 SEMAPHORES = ["cV", "cS", "cP", "cG", "sent"] + DMASEM + RSEM
-CY = 0.9
-CG, CS, HOP, NET = 1.5, 3.5, 150.0, 3000.0
-PF, PE, FX = 8, 0.6, 50
-SLACK = 90.0
-NUDGE = {'f20_5': -1200, 'w21_8': 100, 'w01_3': -1100, 'w10_2': 3700, 's12': 2500, 's79': 2500, 'f21_11': -2500, 's70': -300, 'e24': -900, 'w21_3': -600, 'f01_6': 600, 's28': 2500, 'q3': -600, 'e37': -1200, 's40': 2500, 's22': 400, 's10': 1200, 'e53': 1500, 'e48': -1200, 's48': 100, 'w01_19': -600, 's46': -300, 'f11_5': 1200, 's20': -600, 's24': 300, 'w11_15': 600, 'e68': -2500, 'w00_0': -100, 'f10_5': -600, 'w01_9': 1200, 'e63': -1200, 'e28': -1200, 's4': -1200, 'w00_21': 1200, 'w10_16': -300, 'w21_19': -1200, 'w00_27': -600, 'o13': 500, 'w10_27': 2500, 'f10_1': 1200, 'i76': 600, 'i31': -1200, 'i72': 1200, 'w20_15': 2500, 'q6': -1200, 'f00_4': -400, 'w21_24': 3700, 'i41': -2500, 'f11_4': -300, 'i30': -3700, 'w20_16': 1200, 'i96': -600, 'i113': -100, 'i101': -2500, 'w01_30': 300, 'w10_23': 1200, 'f00_2': -1200, 's32': 100, 's77': 100, 'o7': 600, 's23': 300, 'w20_8': 100, 'i51': 300, 'w01_0': -600, 'w10_4': -1200, 'w01_29': 2500, 'f00_9': 1200, 'i124': -1200, 'b1': 2500, 'e73': 2500, 'b4': 2500, 'i6': -600, 'f00_11': -300, 'e61': 300, 'w20_32': 2500, 'f01_2': -100, 'w20_21': 1200, 'w00_10': 300, 's62': 300, 'p1': 900, 'w21_33': -1200, 'e27': -1200, 'i79': -600, 'w20_19': 100, 'f21_8': -600, 'e14': -100, 'a5': -2500, 'i118': 2500, 'e54': 300, 'w21_26': 100, 's71': -1200, 'e13': -300}
-NUDGE = {'q18': 5000, 'e2': -2500, 'i37': 2500, 'o16': -1200, 'e29': 5000, 'w11_23': -5000, 's3': 300, 'i127': 5000, 'i85': -2500, 'f00_5': 300, 'f11_7': -2500, 'q5': 1200, 'w11_7': 1200, 'i96': 300, 'f01_6': -300, 'a3': -100, 'q12': 100, 'w20_4': 2500, 'e63': 2500, 'w20_10': 600, 'i74': -2500, 'w00_18': 300, 'i33': -1200, 's58': 2500, 'i54': 100, 'w01_1': -100, 'w01_14': -1300, 'w20_27': 1200, 'w20_12': -5000, 's72': 1200, 'f10_1': -600, 'w21_35': -300, 'i59': -2500, 's28': -1200, 's45': -900, 'w00_22': 2500, 'w00_20': 1200, 'f21_0': 1200, 'f10_5': -2500, 'i66': -600, 'o22': -100, 'w21_31': -200, 'o9': -300, 'w01_4': -300, 'i91': 1200, 'i70': 4900, 'e39': 5000, 'o17': -1200, 's50': -1200, 'f20_6': -1200, 'i63': -100, 'e68': 600, 'i32': 600, 'i72': -2500, 'w10_24': 300, 'w21_32': 2500, 'e33': -2500, 'i47': 4700, 'f21_9': -1200, 's33': -100, 'w21_0': -6200, 'z5': -2500, 'w21_28': 600, 's48': 1300, 'i103': 5000, 's32': -100, 'e27': -2500, 'w00_19': 5000, 'f21_7': 1200, 'i71': -2500, 'o26': 1200, 'e13': -600, 'f20_2': 2500, 'o20': -600, 'f01_7': -2500, 'o12': 1200, 'e9': 5000, 'f21_6': -4700, 'w21_4': 100, 'f01_0': -600, 'f11_6': -2500, 'w21_25': -300, 'f00_1': -2200, 'w20_1': 100, 'i106': 1200, 'w01_5': -600, 'i81': -2500, 'f11_9': -5000, 'i42': -1200, 'e43': -300, 's38': 100, 's68': -100, 'e28': 2500, 'f11_4': 5000, 'w21_34': -5000, 'i94': -1200, 'f01_8': -2500, 'w00_25': 600, 's11': -700, 'w21_33': 300, 'w01_29': -300, 'f01_4': -300, 'i34': 600, 'w00_6': -2500, 'q15': 300, 's49': -1200, 'i99': 600, 'w00_7': -5000, 'f01_3': 600, 'r0': 600, 'w11_13': 600, 'i52': 300, 'f10_4': -100, 'f11_1': -2500, 'o5': -1200, 'e21': 600, 's53': 5000, 'i17': 1200, 's2': 100, 'w01_13': -5000, 'z7': -2500, 'w01_16': 2500, 'w01_19': 5000, 'o21': 300, 'i101': 2500, 's27': 300, 'w11_17': 2500, 'q9': 2200, 'w10_5': -1200, 'w10_0': 5000, 'w20_6': -6200, 'e7': -600, 'w01_32': 100, 'w00_21': -300, 'f00_4': 5000, 'i87': 600, 'w10_6': -5000, 'q8': -1200, 's75': 5000, 'i46': 5000, 'w00_33': 100, 'i107': -5000, 'e49': -1200, 'o1': -100, 'e25': 5000, 'i10': -600, 's39': 5000, 'w11_0': 600, 'i25': -2500, 'z3': 2500, 'w01_9': 1200, 'f01_5': 2500, 'i83': 2500, 'o18': -5000, 'w21_27': 2500, 'w21_23': 300, 'w11_31': -300, 'e57': 300, 'e3': 600, 'i27': -1200, 'e18': 300, 'w21_5': -5000, 'w21_8': -300, 'e6': -5000}
+CY, CG, CS, HOP, NET = 0.83, 1.56, 3.8, 180.0, 3500.0
+PF, PE, FX, FS = 0, 0.36, 0, 0
+PASSES, MIX, AHEAD, WAIT, SLACK = 4, 0.5, 400.0, 0.0, 90.0
 
 
 def ap(name, c0=0, c1=None, st=1, p0=0, p1=128, ps=1, off=None):
     if c1 is None:
-        c1 = SCRATCH[name][1][1]
+        c1 = BUF[name][1][1]
     return {"n": name, "c0": c0, "c1": c1, "st": st, "p0": p0, "p1": p1, "ps": ps, "off": off}
 
 
@@ -71,11 +89,11 @@ def width(a):
 
 
 def two(a):
-    return SCRATCH[a["n"]][2] in (bf, u16, "float16")
+    return BUF[a["n"]][2] in (bf, u16, h16)
 
 
 def psum(a):
-    return SCRATCH[a["n"]][0] == "psum"
+    return BUF[a["n"]][0] == "psum"
 
 
 def build(rank):
@@ -101,35 +119,48 @@ def build(rank):
             ops[i]["after"] = prev[q]
         prev[q] = i
 
-    def vcost(out, ins, per):
-        n = width(out)
+    def vcost(out, a, per, fx=FX):
         if out["off"] is not None:
-            return FX + 30 + n * CS * CY
-        if ins[0]["off"] is not None:
-            return FX + 30 + n * CG * CY
-        return FX + max(64, n * per) * CY
+            return 50 + width(out) * CS * CY
+        if a["off"] is not None:
+            return 40 + fx + width(a) * CG * CY
+        return fx + max(64, width(a) * per) * CY
 
     def cp(out, a):
-        add("V", "copy", (out, a), [a], [out], vcost(out, [a], 0.5 if two(out) and two(a) else 1))
+        add("V", "copy", (out, a), [a], [out], vcost(out, a, 0.5 if two(out) and two(a) else 1))
 
     def tt(out, a, b, op):
-        add("V", "tt", (out, a, b, op), [a, b], [out], vcost(out, [a, b], 1 if psum(a) or psum(b) else 2))
+        add("V", "tt", (out, a, b, op), [a, b], [out], vcost(out, a, 1 if psum(a) or psum(b) else 2))
 
     def ts(out, a, s1, op0, s2=None, op1=None):
-        add("V", "ts", (out, a, s1, s2, op0, op1), [a, s1, s2], [out], vcost(out, [a], 0.5 if two(out) and two(a) else 1))
+        add("V", "ts", (out, a, s1, s2, op0, op1), [a, s1, s2], [out], vcost(out, a, 0.5 if two(out) and two(a) else 1))
 
-    def scan(out, d0, d1, op0, op1):
-        add("V", "scan", (out, d0, d1, 0.0, op0, op1), [d0, d1], [out], vcost(out, [d0], 1))
+    def hot(k=1):
+        for o in ops[-k:]:
+            o["hot"] = True
+
+    def scan(out, d0, d1, op0, op1, first=0.0):
+        add("V", "scan", (out, d0, d1, first, op0, op1), [d0, d1], [out], vcost(out, d0, 1))
+
+    def least(out, a):
+        add("V", "red", (out, a, ALU.min, True, True), [a], [out], vcost(out, a, 1))
 
     def ms(out, v):
-        add("V", "memset", (out, v), [], [out], vcost(out, [out], 0.5 if two(out) else 1))
+        add("V", "memset", (out, v), [], [out], vcost(out, out, 0.5 if two(out) else 1))
 
     def act(out, a, fn=AF.Identity, bias=0.0, scale=1.0, acc=None):
-        add("S", "act", (out, a, fn, bias, scale, acc), [a, bias, scale], [out, acc], vcost(out, [a], 1) + 10)
+        add("S", "act", (out, a, fn, bias, scale, acc), [a, bias, scale], [out, acc], vcost(out, a, 1, FS))
 
     def mm(out, l, r, start=True, stop=True):
         c = max(min(64, width(l)), width(r)) * (1 if two(l) else 4)
         add("P", "mm", (out, l, r, start, stop), [l, r], [out], PF + c * PE)
+
+    def group(calls):
+        for k, x in enumerate(calls):
+            mm(x[0], x[1], x[2], k == 0, k == len(calls) - 1)
+
+    def tile(out, src, c0, c1, sel="SW1", step=1):
+        return [(out, ap(sel, 15 - a, 143 - a), ap(src, c0 + step * a, c1, 16 * step)) for a in range(16)]
 
     def iota(out, pat, base=0, cm=0):
         chain("G", add("G", "iota", (out, pat, base, cm), [], [out], 130 + 2 * width(out) * CY))
@@ -144,23 +175,26 @@ def build(rank):
         add("R", "recv", (), [], [out], 0, sem=sem, after=i, lat=NET + nbytes / 40.0)
 
     nxt, prv = (rank + 1) % NR, (rank - 1) % NR
+    KING, FTG, TTG = ap("KIN", 0, GW), ap("FT", 0, W), ap("TT", 0, W)
+    XR, XM = ap("XX", 0, GW), ap("XX", GW, 2 * GW)
     dma("S", ap("FRAW", p1=8), ("ft",), "df", 16e3)
     dma("S", ap("BRAW", p1=8), ("bs",), "db", 4e3)
     for k, c in enumerate((3, 2, 1, 0)):
         dma("Y", ap("KRAW", 448 * c, 448 * c + 448), ("kn", 0, 128, 1, 448 * c, 448 * c + 448), "dk%d" % c, 240e3 * (k + 1))
     dma("S", ap("ZIN", 0, 128), ("z0",), "dz", 300e3)
     dma("S", ap("TRAW"), ("tr",), "dt", 400e3)
-    dma("Y", ap("XX", W, 2 * W), ("x0",), "dx1", 1450e3)
+    dma("Y", ap("XX", GW, GW + W), ("x0",), "dx1", 1450e3)
     dma("Y", ap("XX", 0, W), ("x0",), "dx0", 1900e3)
-    pid, pmod, pdiv, podd, phalf, pm2, p32, row0, nrow0, k8, kst, k0 = [ap("PC", k, k + 1) for k in range(12)]
+    pid, pmod, pdiv, podd, phalf, pm2, p32, row0, nrow0, even, odd8, stay = [ap("PC", k, k + 1) for k in range(12)]
     iota(ap("PI", 0, 1), [[0, 1]], 0, 1)
-    iota(ap("IOTA", 0, 128), [[1, 128]])
+    iota(ap("IOTA", 0, 144), [[1, 144]])
     iota(ap("JD"), [[1, 8], [0, 16]])
+    iota(ap("J3"), [[1, 8], [0, 3]])
     iota(ap("JM"), [[0, 16], [1, 16]])
     iota(ap("J8"), [[0, 4], [1, 8]])
-    iota(ap("JP"), [[8, 2], [16, 8], [1, 9]], -1)
-    iota(ap("JK"), [[0, 8], [2048, 9]])
     iota(ap("J2"), [[1, 64], [0, 2]])
+    for o in range(2):
+        iota(ap("JP", KW * o, KW * o + KW), [[16, 8], [1000, 3], [1, 9]], 8 * o - 2001)
     ts(ap("PI", 1, 2), ap("PI", 0, 1), 15, ALU.bitwise_and)
     ts(ap("PI", 2, 3), ap("PI", 0, 1), 4, ALU.logical_shift_right)
     ts(ap("PI", 3, 4), ap("PI", 0, 1), 1, ALU.bitwise_and)
@@ -170,254 +204,300 @@ def build(rank):
     cp(ap("PC", 0, 7), ap("PI", 0, 7))
     ts(row0, pmod, 0.0, ALU.is_equal)
     ts(nrow0, pmod, 0.0, ALU.not_equal)
-    ts(ap("MASK"), ap("JM", 0, 128), pmod, ALU.is_equal)
-    ts(ap("BLK"), ap("JD"), pdiv, ALU.is_equal)
-    ts(ap("RX2"), ap("JD", 0, 64), p32, ALU.is_equal)
-    ts(ap("MASK2"), ap("JM", 0, 128), pm2, ALU.is_equal)
-    ts(ap("PAIR"), ap("J2"), phalf, ALU.is_equal)
-    act(ap("PC", 12, 13), podd, scale=-65536.0, bias=65536.0)
-    act(k8, podd, scale=8.0 * 2048)
-    act(ap("KC"), ap("JK"), bias=k8)
-    act(k0, podd, scale=1024.0)
-    act(kst, podd, scale=1024.0 - 15.5 * 65536, bias=15.5 * 65536)
-    act(ap("KC", 0, 72, 9), ap("JK", 0, 72, 9), bias=k0)
-    act(ap("AT", 24, 32), ap("JK", 0, 72, 9), bias=ap("PC", 12, 13))
-    act(ap("BLKS"), ap("BLK"), scale=2.0 ** -8)
-    ts(ap("SELX"), ap("JD"), pdiv, ALU.is_equal, row0, ALU.mult)
-    ts(ap("SELH"), ap("JD"), pdiv, ALU.is_equal, row0, ALU.mult)
-    act(ap("SELB"), ap("SELX"))
+    act(even, podd, scale=-1.0, bias=1.0)
+    act(odd8, podd, scale=8.0)
+    act(stay, podd, scale=16384.0 + 2048.0, bias=-2048.0)
     ts(ap("IDF"), ap("IOTA", 0, 128), pid, ALU.is_equal)
+    cp(ap("IDH"), ap("IDF"))
     act(ap("IDB"), ap("IDF"))
+    act(ap("IDQ"), ap("IDF"), scale=0.5)
+    act(ap("ID2K"), ap("IDF"), scale=2048.0)
     ts(ap("S8", p1=8), ap("JD", p1=8), ap("PC", 0, 1, p1=8), ALU.is_equal)
-    ts(ap("R3"), ap("J8", 0, 24), pdiv, ALU.is_equal)
-    ts(ap("RH"), ap("J8", 0, 24), pdiv, ALU.is_equal)
-    act(ap("RBIG"), ap("R3", 0, 16), scale=4096.0)
-    act(ap("THR", 0, 128), ap("MASK"), scale=-1023.25, bias=1024.0)
-    act(ap("THR", 128, 256), ap("MASK"), scale=-1024.0 + 2.0 ** -9, bias=1024.0)
-    act(ap("BOM"), ap("R3", 0, 8), scale=2.0 ** 17)
-    act(ap("BOX", 0, 8), ap("R3", 0, 8), scale=-2.0 ** 16)
-    act(ap("BOX", 8, 16), ap("SELX", 0, 128, 16), scale=2.0 ** 32)
-    ts(ap("PERM"), ap("JP"), pid, ALU.is_equal)
-    ms(ap("PERM", 0, 144, 9), 0.0)
-    tt(ap("SWAP"), ap("PAIR"), ap("IDF"), ALU.subtract)
-    ms(ap("RST"), 0.0)
-    ms(ap("RST", 0, 72, 9), 2.0 ** 60)
-    act(ap("SG"), ap("JM", 0, 128), AF.Sign)
-    cp(ap("CO", 8, 16), ap("J8", 0, 8))
-    ts(ap("TRI", 0, 128), ap("JM", 0, 128), pmod, ALU.is_le, 4096.0, ALU.mult)
-    act(ap("A32", 0, 8), ap("J8", 0, 8), scale=16.0, bias=pmod)
-    for c0, off in ((0, TR), (8, TR), (16, 16)):
-        act(ap("B24", c0, c0 + 8), ap("A32", 0, 8), bias=float(off))
-    for c0, off in ((0, 128), (8, TR), (16, TR), (24, TR)):
-        act(ap("B32", c0, c0 + 8), ap("A32", 0, 8), bias=float(off))
-    for n, c0, c1, v in (("A24", 16, 24, 0.0), ("YC", 0, 16, float(W)),
-                         ("KIN", W, TW, -1.0), ("FT", W, TW, -1.0), ("TT", W, TW, -1.0), ("AO", 0, 4 * VIS, 0.0)):
-        act(ap(n, c0, c1), ap("JM", 0, c1 - c0), scale=0.0, bias=v)
-    act(ap("ONES"), ap("JD"), scale=0.0, bias=1.0)
-    act(ap("TRI", 128, 256), ap("JD"), scale=0.0, bias=-0.5)
+    act(ap("PC", 12, 13), pid, bias=15.0)
+    act(ap("PC", 13, 14), row0, scale=4096.0)
+    ts(ap("SW1"), ap("IOTA", 0, 144), ap("PC", 12, 13), ALU.is_equal, row0, ALU.mult)
+    ts(ap("SWB"), ap("IOTA", 0, 144), ap("PC", 12, 13), ALU.is_equal, ap("PC", 13, 14), ALU.mult)
+    ts(ap("MASK2"), ap("JM", 0, 128), pm2, ALU.is_equal, -2048.0, ALU.mult)
+    ts(ap("SWAP"), ap("J2"), phalf, ALU.is_equal, 128.0, ALU.mult)
+    ts(ap("PAIR"), ap("J2"), phalf, ALU.is_equal)
+    ts(ap("J2"), ap("IDF"), 256.0, ALU.mult)
+    tt(ap("SWAP"), ap("SWAP"), ap("J2"), ALU.subtract)
+    act(ap("HUGE"), ap("J8", 0, 8), scale=0.0, bias=2.0 ** 40)
     for h in range(2):
-        act(ap("XS%d" % h), ap("JD"), scale=0.0)
-        act(ap("MS%d" % h), ap("JD"), scale=0.0, bias=1024.0)
-        act(ap("CF%d" % h), ap("JM", 0, 130), scale=0.0)
-    act(ap("TM"), ap("JM"), scale=0.0)
-    if EARLY:
-        ms(ap("KP", 0, 256), 0.0)
-        ms(ap("NQ"), 0.0)
-    ms(ap("EQ", 0, 896), 0.0)
-    if SHIFT:
-        ms(ap("XG1", 0, 512), 0.0)
+        mm(ap("P%d" % (4 + h), 225, 248, 3), ap("IDB"), ap("HUGE"))
+    ts(ap("SELB"), ap("JD"), pdiv, ALU.is_equal, row0, ALU.mult)
+    ts(ap("SEL8"), ap("J8", 0, 8), pdiv, ALU.is_equal, row0, ALU.mult)
+    ts(ap("RX4"), ap("J8", 0, 4), p32, ALU.is_equal)
+    for j in range(3):
+        for k, tab in enumerate((WKEY, WINC, WCAND, WSTAY)):
+            act(ap("W24", 24 * k + j, 24 * k + 24, 3), ap("J8", 0, 8), scale=0.0, bias=tab[j])
+        act(ap("SELP", j, 24, 3), ap("SELB", 0, 128, 16), scale=(16.0, 0.0, -16.0)[j])
+    ts(ap("RW"), ap("J3"), pdiv, ALU.is_equal)
+    tt(ap("RW"), ap("RW"), ap("W24", 0, 24), ALU.mult)
+    act(ap("RWB"), ap("RW"))
+    act(ap("BOX"), ap("RW"), scale=-1.0)
+    act(ap("BOM"), ap("RW"), scale=2.0)
+    for k, v in enumerate((32.0, -32.0, 32768.0)):
+        ts(ap("SH", 24 * k, 24 * k + 24), ap("RW"), row0, ALU.mult, v, ALU.mult)
+    act(ap("T1", 0, 24), ap("W24", 0, 24), scale=-2048.0)
+    act(ap("T1", 24, 48), ap("W24", 0, 24), scale=stay)
+    ts(ap("MASK"), ap("JM", 0, 128), pmod, ALU.is_equal)
+    ts(ap("SELH"), ap("JD"), pdiv, ALU.is_equal, row0, ALU.mult)
+    ts(ap("RH"), ap("J8", 0, 8), pdiv, ALU.is_equal)
+    ts(ap("RBIG"), ap("J8", 0, 8), pdiv, ALU.is_equal, 4096.0, ALU.mult)
+    act(ap("SGN"), ap("JM", 0, 128), AF.Sign)
     for k in range(16):
-        (cp if k % 2 else act)(ap("EE", k, 2048, 16), ap("IDF"))
+        act(ap("EE", k, 1024, 16, p1=64), ap("IDF", 0, 64, p1=64))
+    ts(ap("AB"), ap("W24", 24, 48), odd8, ALU.mult)
+    tt(ap("LO", 1, KW, 9), ap("AB"), ap("W24", 48, 72), ALU.add)
+    for s in range(2, 9):
+        tt(ap("LO", s, KW, 9), ap("LO", s - 1, KW, 9), ap("W24", 24, 48), ALU.add)
+    act(ap("A24"), ap("W24", 48, 72), scale=podd)
+    act(ap("U24"), ap("W24", 72, 96), scale=even)
+    tt(ap("LO", 0, KW, 9), ap("A24"), ap("U24"), ALU.add)
+    ms(ap("PERM", 432, 464), 0.0)
+    ts(ap("PERM", 0, 432), ap("JP"), pid, ALU.is_equal)
+    ms(ap("PERM", 0, 432, 9), 0.0)
+    ts(ap("PTMP"), ap("PERM", 0, 432), -16.0, ALU.mult)
+    ts(ap("JP"), ap("PERM", 18, 450), 16.0, ALU.mult)
+    tt(ap("PERH"), ap("PTMP"), ap("JP"), ALU.add)
+    act(ap("RST"), ap("JM", 0, KW), scale=0.0)
+    act(ap("RST", 0, KW, 9), ap("J3"), scale=0.0, bias=2.0 ** 60)
+    ts(ap("CO"), ap("J8", 0, 8), 3.0, ALU.mult, 2.0, ALU.add)
+    act(ap("LANE"), ap("J8", 0, 8), scale=16.0, bias=pmod)
+    for c0, off in ((0, SP), (8, SP), (16, 16)):
+        act(ap("B24", c0, c0 + 8), ap("LANE"), bias=float(off))
+    for n, c0, c1, v in (("YC", 0, 16, float(W)), ("KIN", W, GW, -1.0), ("AO", 0, 4 * VIS, 0.0), ("XX", W, GW, 0.0),
+                         ("XX", GW + W, 2 * GW, 0.0), ("QUART", 0, 64, -0.5), ("ONES", 0, 128, 1.0), ("TABN", 0, 16, 0.0),
+                         ("TABN", 16, 144, float(ZONE)), ("EVN", 0, 256, 0.0), ("CD1", 0, 64, 0.0), ("CD2", 0, 16, 0.0),
+                         ("D0", 0, 64, 0.0), ("XU", 0, 144, 1024.0)):
+        act(ap(n, c0, c1), ap("JM", 0, c1 - c0), scale=0.0, bias=v)
+    act(ap("A24", 16, 24), ap("LANE"), scale=0.0)
+    act(ap("EVN", 0, 128, 2), ap("JM", 0, 64), scale=0.0, bias=1.0 / 16)
+    act(ap("EVN", 128, 256, 2), ap("JM", 0, 64), scale=0.0, bias=15.5 / 16)
+    for k, (sc, v) in {0: (0.0, 32768.0), 1: (1.0, SP + ZONE), 3: (1.0, SP - 2048), 4: (1.0, SP - 2048), 6: (1.0, 0),
+                       2: (0.0, 4096.0), 5: (0.0, 4096.0)}.items():
+        act(ap("CD1", k, 64, 8), ap("LANE"), scale=sc, bias=float(v))
+    act(ap("CD2", 1, 16, 2), ap("LANE"), bias=float(SP))
+    for k, v in {1: -65536.0, 3: -float(ZONE), 6: 128.0 - SP}.items():
+        act(ap("D0", k, 64, 8), ap("LANE"), scale=0.0, bias=v)
+    for h in range(2):
+        for n in ("XS", "MS", "HP", "NQ"):
+            act(ap("%s%d" % (n, h)), ap("JD"), scale=0.0)
+        act(ap("HB%d" % h), ap("JM", 0, 130), scale=0.0)
+        act(ap("FL%d" % h), ap("JM"), scale=0.0)
+        ms(ap("CF%d" % h), 0.0)
+        ms(ap("KP%d" % h), 0.0)
+    ms(ap("TM"), 0.0)
     for c in range(4):
         cp(ap("KIN", 448 * c, 448 * c + 448), ap("KRAW", 448 * c, 448 * c + 448))
-    cp(ap("TO", 0, 512, p1=8), ap("FRAW", p1=8))
-    cp(ap("TM", 0, 256, 2, p1=8), ap("BRAW", p1=8))
-    mm(ap("P3"), ap("S8", p1=8), ap("TO", 0, 512, p1=8))
+    cp(ap("FF", 0, 512, p1=8), ap("FRAW", p1=8))
+    cp(ap("FF", 512, 640, p1=8), ap("BRAW", p1=8))
+    mm(ap("P3"), ap("S8", p1=8), ap("FF", 0, 512, p1=8))
     act(ap("FT", B0, W), ap("P3"))
+    mm(ap("P2", 0, 128), ap("S8", p1=8), ap("FF", 512, 640, p1=8))
+    tt(ap("TM", 0, 256, 2), ap("P2", 0, 128), ap("MASK"), ALU.mult)
+    act(ap("BR"), ap("P2", 0, 128))
     iota(ap("IOTA", B0, W), [[1, W - B0]], B0)
     iota(ap("FT", 0, B0), [[0, B0]], -1)
     act(ap("N0"), ap("IOTA", B0, W), scale=row0)
     cp(ap("TCF"), ap("TRAW"))
     send(nxt, ap("DT0"), ap("TCF"), "rt0", 57e3)
-    iota(ap("IOTA", 128, B0), [[1, B0 - 128]], 128)
-    iota(ap("TO"), [[0, TW]], -1)
+    iota(ap("IOTA", 144, B0), [[1, B0 - 144]], 144)
+    tag[:] = ["j", 0]
+    iota(ap("JB"), [[-16, 8], [1, 128]], -1)
+    ts(ap("TRA"), ap("JB"), pmod, ALU.is_ge, 2.0 ** 26, ALU.mult)
+    ms(ap("TRA", 0, 1024, 128), 2.0 * ZONE)
+    iota(ap("JB", 0, 512), [[1, 4], [0, 128]])
+    ts(ap("RXB"), ap("JB", 0, 512), p32, ALU.is_equal, -8192.0, ALU.mult)
+    ts(ap("EV"), ap("PAIR", 0, 128, 2), 8192.0, ALU.mult)
+    ms(ap("RX32"), 0.0)
+    for k in (2, 5):
+        cp(ap("RX32", k, 32, 8), ap("RX4"))
     for a in range(16):
         dma("Y", ap("TT", 0, W, p0=a, ps=16), ap("DT0"), "dtt", 920e3)
 
-    R8 = ap("R3", 0, 8)
     turn = []
     for t in range(VIS):
         r = (rank - t) % NR
         lo = B0 + 128 * r
         mid = lo + 63.5
         last = t == VIS - 1
-        zin = ap("ZIN", 128 * t, 128 * t + 128)
         wx = 256 * t
-        tag[:] = ["o", 0]
         nrep = ap("IOTA", lo, lo + 128)
-        mm(ap("P6", 128, 256), ap("KIN", lo, lo + 128), ap("SELX"))
-        tt(ap("MK", 128, 256), ap("P6", 128, 256), ap("MASK"), ALU.mult)
-        mm(ap("P7", 88, 112), ap("MK", 128, 256), ap("RH"))
-        mm(ap("P4", 256, 384), ap("FT", lo, lo + 128), ap("SELX"))
-        ms(ap("XX", W + lo, W + lo + 128), 1024.0)
-        tt(ap("MK", 0, 128), ap("P4", 256, 384), ap("MASK"), ALU.mult)
-        mm(ap("P7", 64, 88), ap("MK", 0, 128), ap("RH"))
-        cp(ap("OYU"), ap("P7", 80, 96))
-        tt(ap("NH", 0, 128), ind(ap("KIN"), ap("OYU", 0, 8)), nrep, ALU.not_equal)
-        tt(ap("NH", 128, 256), ind(ap("FT"), ap("OYU", 8, 16)), nrep, ALU.not_equal)
-        act(ap("AB"), ap("P7", 64, 112), AF.Abs, bias=-mid)
-        act(ap("A24", 0, 16), ap("P7", 80, 96))
-        act(ap("REL", 0, 48), ap("AB"), AF.Relu, bias=2.0 ** 30, scale=-2.0 ** 24)
-        act(ap("KM"), ind(ap("KIN"), ap("OYU", 0, 8)), scale=nrow0)
-        act(ap("U0"), ap("KIN", lo, lo + 128), scale=row0)
+
+        def zin(c0, c1):
+            return ap("ZIN", 128 * t + c0, 128 * t + c1)
+
+        def place(s, h):
+            return ap("OB", 8 * h, 8 * h + 4) if s == 0 else ap("B%d" % s, 4 * h, 4 * h + 4)
+
+        def arrive(h):
+            tag[:] = ["b%d_" % h, 0]
+            tm, c0, c1 = ap("TM", 128 * h, 128 * h + 128, 2), 64 * h, 64 * h + 64
+            if t:
+                came = ap("BIN", 16 * t - 16 + 8 * h, 16 * t - 12 + 8 * h)
+                tt(tm, ind(TTG, came), ap("MASK", 0, 64), ALU.mult)
+                hot()
+                act(ap("BR", c0, c1), ind(TTG, came))
+            scan(ap("TS", c0, c1), ap("SGN", 0, 64), tm, ALU.mult, ALU.add)
+            cp(place(0, h), ap("TS", c0 + 15, c1, 16))
+            hot(2)
+            mm(ap("P%d" % (2 * h + 1), 0, 128, p1=64), zin(c0, c1), ap("IDB"))
+            act(ap("ZT", 128 * h, 128 * h + 128, p1=64), ap("P%d" % (2 * h + 1), 0, 128, p1=64), bias=-128.0)
+            for bk in range(2):
+                mm(ap("P%d" % (2 * h + bk)), ap("ZT", 128 * h, 128 * h + 128, p1=64), ap("EE", 512 * bk, 512 * bk + 512, p1=64))
+
+        def front(s, h):
+            off, xg, mx, cf, hb, xs, ms_ = ["%s%d" % (n, h) for n in ("OFF", "XG", "MX", "CF", "HB", "XS", "MS")]
+            tag[:] = ["f%d%d_" % (s, h), 0]
+            cp(ap(off), ind(KING, place(s, h)))
+            hot()
+            for c0, c1 in CUTS:
+                act(ap(xg, 16 * c0, 16 * c1), ind(XM, ap(off, c0, c1)), bias=-128.0)
+                if turn:
+                    ops[-1]["after"] = turn[0]
+                turn[:] = [len(ops) - 1]
+            act(ap(xs, 0, 128, 2), ind(XR, place(s, h)))
+            cp(ap(cf, 1, 129, 2), ap(off))
+            if HBS:
+                act(ap(hb, 1, 129, 2), ind(KING, place(s, h)), scale=1.0 / 16, bias=HIGH)
+            else:
+                ts(ap(hb, 1, 129, 2), ap(off), 1.0 / 16, ALU.mult, HIGH, ALU.add)
+            tt(ap(ms_, 0, 128, 2), ap(xs, 0, 128, 2), zin(64 * h, 64 * h + 64), ALU.max)
+            for c0, c1 in VCUTS:
+                z0 = 16 * c0 % 512
+                tt(ap(mx, 16 * c0, 16 * c1), ap(xg, 16 * c0, 16 * c1), ap("P%d" % (2 * h + c0 // 32), z0, z0 + 16 * (c1 - c0)), ALU.max)
+
+        def early(h):
+            tag[:] = ["q%d_" % h, 0]
+            op, at = ap("OB", 8 * h + 4, 8 * h + 8), ap("OP", 4 * h, 4 * h + 4)
+            group(tile(ap("P6", 8, 12), "CF%d" % h, 1, 128, step=2))
+            ts(at, ap("P6", 8, 12), lo - 1.0, ALU.subtract, 129.0, ALU.min)
+            cp(op, ap("P6", 8, 12))
+            act(ap("XS%d" % h, 1, 128, 2), ind(ap("XU"), at))
+            tt(ap("MS%d" % h, 1, 128, 2), ap("XS%d" % h, 1, 128, 2), zin(64 * h, 64 * h + 64), ALU.max)
+            cp(ap("KP%d" % h, 1, 128, 2), ind(KING, op))
+            act(ap("HP%d" % h, 1, 128, 2), ind(KING, op), scale=1.0 / 16, bias=HIGH)
+            act(ap("FL%d" % h, 1, 128, 2), ind(XM, place(0, h)), AF.Relu, bias=-512.0)
+            tt(ap("NQ%d" % h, 1, 128, 2), ind(FTG, op), ap("BR", 64 * h, 64 * h + 64), ALU.not_equal)
+
+        def back(s, h):
+            xg, mx, cf, hb, xs, ms_, m, mn, s3, be = ["%s%d" % (n, h) for n in ("XG", "MX", "CF", "HB", "XS", "MS", "M", "MN", "S3", "BE")]
+            kb = "P%d" % (4 + h)
+            tag[:] = ["w%d%d_" % (s, h), 0]
+            key, own, ownb = ap(kb, 0, KW), ap(kb, 0, KW, 9), ap(kb, 18, KW, 27)
+            grp = [(key, ap("IDH"), ap("LO")), (own, ap("IDB"), ap("T1", 24, 48) if s else ap("T1", 0, 24))]
+            grp += [(key, ap(src, 1 - o, 129 - o), ap(pm, KW * o, KW * o + KW)) for src, pm in ((cf, "PERM"), (hb, "PERH")) for o in range(2)]
+            dist = [(own, ap(xs), ap("BOX")), (own, ap(ms_), ap("BOM"))]
+            shift = [(own, ap("EVN", 128, 256), ap("RWB")), (own, ap("AE"), ap("RWB"))] if t else []
+            kin = [(ap(kb, 1 + k, KW, 9), ap(src, k, 1024, 8), ap(wt)) for src, wt in ((xg, "BOX"), (mx, "BOM")) for k in range(8)]
+            if s:
+                grp += [(ownb, ap("PAIR"), ap(mn))] + shift + dist + kin
+            else:
+                grp += kin + [(own, ap("FL%d" % h, 0, 128), ap("SH", 0, 24)),
+                              (own, ap("NQ%d" % h), ap("SH", 48, 72)), (ownb, ap("TM", 128 * h, 128 * h + 128), ap("RH")),
+                              (ownb, ap("KP%d" % h), ap("SEL8")), (own, ap("HP%d" % h), ap("SELP"))] + dist + shift
+            group(grp)
+            scan(ap(m), ap("RST"), key, ALU.add, ALU.min)
+            hot()
+            mm(ap(kb, 226, 248, 3), ap("SWAP"), ap(m, 17, KW, 27))
+            mm(ap(kb, 224, 248, 3), ap("IDF"), ap(m, 8, KW, 27))
+            scan(ap(s3), ap(m, 8, KW, 9), ap(kb, 224, 248), ALU.subtract, ALU.min, -1.0)
+            hot()
+            tt(ap(be), ind(ap(s3), ap("CO")), ap("MASK2"), ALU.max)
+            hot()
+            mm(ap(kb, 256, 260), ap(be), ap("RX4"))
+            if s < ST - 1:
+                ts(place(s + 1, h), ap(kb, 256, 260), 4096.0, ALU.add)
+                hot()
+                act(ap(mn), ap(s3, 2, 24, 3), AF.Relu, bias=2048.0)
+
+        def finish(h):
+            tag[:] = ["g%d_" % h, 0]
+            kb, c0, c1 = "P%d" % (4 + h), 64 * h, 64 * h + 64
+            bw = ap("BW", 16 * t + 8 * h, 16 * t + 8 * h + 4)
+            ts(ap("BU%d" % h), ind(ap("S3%d" % h), ap("CO")), -2048.0, ALU.max)
+            for c in range(4 * h, 4 * h + 4):
+                w, at = min(16 * c + 16, 127), 128 * (c % 4) + 1
+                if h:
+                    mm(ap("P1", at + 64, at + w), ap("BU1"), ap("EV", 0, w - 64), False, False)
+                else:
+                    mm(ap("P0", at, at + w), ap("BU0"), ap("EV", 0, w), False, False)
+                mm(ap("P%d" % h, at, at + w), ap("BE%d" % h), ap("RXB", at - 1, at - 1 + w), False, c % 4 == 3)
+            if not h:
+                for c in range(4):
+                    mm(ap("P1", 128 * c + 1, 128 * c + 65), ap("BU0"), ap("EV"), False, False)
+            ts(bw, ap(kb, 256, 260), 4096.0, ALU.add)
+            hot()
+            send(prv if last else nxt, ap("BIN", 16 * t + 8 * h, 16 * t + 8 * h + 4), bw, "r%s%d" % ("bc"[h], t), 1e3)
+            for c in range(4 * h, 4 * h + 4):
+                least(ap("D0", 8 * c + 2, 8 * c + 3), ap("P%d" % h, 128 * (c % 4), 128 * (c % 4) + 1 + min(16 * c + 16, 127)))
+            act(ap("XB", c0, c1), ind(XR, bw))
+            cp(ap("KH", c0, c1), ind(KING, bw))
+            act(ap("WF", c0, c1), ind(ap("IOTA"), bw))
+            act(ap("WK", c0, c1), ind(KING, bw))
+            group([(ap(kb, 320, 384), ap("IDQ"), zin(c0, c1)), (ap(kb, 320, 384), ap("IDQ"), ap("QUART")),
+                   (ap(kb, 320, 384), ap("IDQ"), ap("XB", c0, c1))])
+            ts(ap("WX", wx + c0, wx + c1), ap(kb, 320, 384), MAGIC, ALU.add, MAGIC, ALU.subtract)
+            if not last:
+                send(nxt, ap("ZIN", 128 * t + 128 + c0, 128 * t + 128 + c1), ap("WX", wx + c0, wx + c1), "r%s%d" % ("zy"[h], t), 16e3)
+
+        tag[:] = ["a", 0]
+        ms(ap("XX", GW + lo, GW + lo + 128), 1024.0)
+        if t:
+            act(ap("AE"), ap("EVN", 0, 128), scale=ap("AIN", 4 * t - 4, 4 * t - 3))
         dma("Y", ap("YC", 16, 144), ap("FT", lo, lo + 128), "dy%d" % t, 64e3)
         dma("Y", ap("WK", 128, 256), ap("KIN", lo, lo + 128), "dw%d" % t, 64e3)
         dma("Y", ap("WX", wx + 128, wx + 256), ap("XX", lo, lo + 128), "dw%d" % t, 32e3)
-        mm(ap("P6", 256, 384), ap("NH", 0, 128), ap("SELB"))
-        tt(ap("MKB", 0, 128), ap("P6", 256, 384), ap("MASK"), ALU.mult)
-        mm(ap("P4", 384, 512), ap("NH", 128, 256), ap("SELB"))
-        tt(ap("MKB", 128, 256), ap("P4", 384, 512), ap("MASK"), ALU.mult)
-        mm(ap("P7", 128, 152), ap("IDF"), ap("A24"), True, False)
-        mm(ap("P7", 128, 152), ap("IDB"), ap("REL", 0, 24), False, False)
-        mm(ap("P7", 128, 152), ap("IDB"), ap("REL", 24, 48), False, False)
-        mm(ap("P7", 128, 144), ap("MKB", 0, 128), ap("RBIG", 0, 16), False, False)
-        mm(ap("P7", 136, 144), ap("MKB", 128, 256), ap("RBIG", 0, 8), False, True)
+        for h in range(2):
+            arrive(h)
+        if last:
+            dma("Y", ap("DT1"), ap("TT", 0, W, ps=16), "dd1", 57e3)
+            send(prv, ap("DT2"), ap("DT1"), "rt1", 57e3)
+            dma("Y", ap("TO", 0, W, ps=16), ap("DT2"), "dto", 57e3)
+        tag[:] = ["n", 0]
+        cp(ap("YU"), ap("KIN", lo, lo + 128))
+        group(tile(ap("P6", 72, 80), "YU", 0, 128))
+        cp(ap("OYU", 8, 16), ap("P6", 72, 80))
+        act(ap("XU", 1, 129), ind(XM, ap("OYU", 8, 16)))
+        act(ap("AB", 8, 16), ap("P6", 72, 80), AF.Abs, bias=-mid)
+        act(ap("A24", 8, 16), ap("P6", 72, 80))
+        for h in range(2):
+            front(0, h)
+            early(h)
+        tag[:] = ["o", 0]
+        tt(ap("TY"), ap("FT", lo, lo + 128), ap("MASK"), ALU.mult)
+        scan(ap("TZ"), ap("SGN"), ap("TY"), ALU.mult, ALU.add)
+        cp(ap("OYU", 0, 8), ap("TZ", 15, 128, 16))
+        act(ap("AB", 0, 8), ap("TZ", 15, 128, 16), AF.Abs, bias=-mid)
+        act(ap("A24", 0, 8), ap("TZ", 15, 128, 16))
+        tt(ap("NH", 0, 128), ind(KING, ap("OYU", 0, 8)), nrep, ALU.not_equal)
+        tt(ap("NH", 128, 256), ind(FTG, ap("OYU", 8, 16)), nrep, ALU.not_equal)
+        act(ap("REL"), ap("AB", 0, 16), AF.Relu, bias=2.0 ** 30, scale=-2.0 ** 24)
+        act(ap("KM"), ind(KING, ap("OYU", 0, 8)), scale=nrow0)
+        act(ap("U0"), ap("KIN", lo, lo + 128), scale=row0)
+        if OMASK:
+            mm(ap("P7", 256, 384), ap("NH", 0, 128), ap("SELH"))
+            group([(ap("P7", 384, 512), ap("NH", c, c + 128), ap("SELH")) for c in (0, 128)])
+            for c in (0, 128):
+                tt(ap("MO", c, c + 128), ap("P7", 256 + c, 384 + c), ap("MASK"), ALU.mult)
+            miss = [(ap("P7", 128 + 8 * k, 136 + 8 * k), ap("MO", 128 * k, 128 * k + 128), ap("RBIG")) for k in range(2)]
+        else:
+            miss = tile(ap("P7", 136, 144), "NH", 0, 128, "SWB") + tile(ap("P7", 128, 144), "NH", 0, 256, "SWB")
+        group([(ap("P7", 128, 152), ap("IDF"), ap("A24"))]
+              + [(ap("P7", 128 + c, 136 + c), ap("IDB"), ap("REL", k, k + 8)) for c in (0, 8, 16) for k in (0, 8)] + miss)
         tt(ap("U24"), ap("P7", 128, 152), ap("B24"), ALU.min)
         cp(ap("OSC"), ap("U24"))
-        tag[:] = ["b" if t else "a", 0]
-        if t == 0:
-            mm(ap("P2", 0, 128), ap("TM", 0, 256, 2, p1=8), ap("S8", p1=8))
-            tt(ap("MKV"), ap("P2", 0, 128), ap("MASK"), ALU.mult)
-            mm(ap("P1", 0, 8), ap("MKV"), ap("RH", 0, 8))
-            cp(ap("OB"), ap("P1", 0, 8))
-        else:
-            tt(ap("TM", 0, 256, 2), ind(ap("TT"), ap("BIN", 8 * t - 8, 8 * t)), ap("MASK"), ALU.mult)
-            scan(ap("TS"), ap("SG"), ap("TM", 0, 256, 2), ALU.mult, ALU.add)
-            cp(ap("OB"), ap("TS", 15, 128, 16))
-            act(ap("KC", 0, 72, 9), ap("AT", 24, 32), scale=ap("AIN", 4 * t - 4, 4 * t - 3), bias=kst)
-            if last:
-                dma("Y", ap("DT1"), ap("TT", 0, W, ps=16), "dd1", 57e3)
-                send(prv, ap("DT2"), ap("DT1"), "rt1", 57e3)
-                dma("Y", ap("TO", 0, W, ps=16), ap("DT2"), "dto", 57e3)
-        tag[:] = ["z", 0]
-        mm(ap("P5", 384, 512), zin, ap("IDB"))
-        act(ap("ZT", 0, 128), ap("P5", 384, 512))
-        if SHIFT:
-            act(ap("ZT", 128, 256), ap("P5", 384, 512), scale=-1.0)
-            for k in range(2):
-                act(ap("ZT", 256 + k, 320, 2), ap("ZIN", 128 * t + 64, 128 * t + 96))
-        for h in range(2):
-            mm(ap("P%d" % (6 + h), 448, 512), ap("IDB"), ap("ZIN", 128 * t + 64 * h, 128 * t + 64 * h + 64))
-        for k in (0, 1, 3) if SHIFT else range(4):
-            mm(ap("P%d" % k), ap("ZT", 0, 128), ap("EE", 512 * k, 512 * k + 512))
-
-        def names(h):
-            return ["%s%d" % (n, h) for n in ("OFF", "XG", "MX", "CF", "M", "E", "VL", "S2", "BE", "SW")]
-
-        def front(s, h):
-            off, xg, mx, cf = names(h)[:4]
-            xs, ms_ = [("%s%d" % (n, h + (2 if s == 0 and EARLY else 0))) for n in ("XS", "MS")]
-            tag[:] = ["f%d%d_" % (s, h), 0]
-            at = ap(off, 0, 4) if s else ap("OB", 4 * h, 4 * h + 4)
-            cp(ap(off, 4, 68), ind(ap("KIN"), at))
-            for c0, c1 in CUTS:
-                act(ap("EE", 2048, 2560) if h in SHIFT and c0 == 0 else ap(xg, 16 * c0, 16 * c1), ind(ap("XX", W, 2 * W), ap(off, 4 + c0, 4 + c1)))
-                if turn and TURN:
-                    ops[-1]["after"] = turn[0]
-                turn[:] = [len(ops) - 1]
-            act(ap(xs, 0, 128, 2), ind(ap("XX", 0, W), at))
-            act(ap(cf, 1, 129, 2), ind(ap("KIN"), at))
-            tt(ap(ms_, 0, 128, 2), ap(xs, 0, 128, 2), ap("P%d" % (6 + h), 448, 512), ALU.max)
-            for c0, c1 in VCUTS:
-                z0 = 16 * c0 % 512
-                if h in SHIFT and c0 == 0:
-                    mm(ap("P2"), ap("ZT", 128, 256), ap("EE", 1024, 1536), True, False)
-                    mm(ap("P2"), ap("IDB"), ap("EE", 2048, 2560), False, True)
-                    act(ap(mx, 0, 512), ap("P2"), AF.Abs, scale=0.5)
-                    continue
-                tt(ap(mx, 16 * c0, 16 * c1), ap(xg, 16 * c0, 16 * c1), ap("P%d" % (2 * h + c0 // 32), z0, z0 + 16 * (c1 - c0)), ALU.max)
-
-        def back(s, h):
-            off, xg, mx, cf, mm_, ee, vl, s2, be, sw = names(h)
-            late = s == 0 and EARLY
-            xs, ms_ = [("%s%d" % (n, h + (2 if late else 0))) for n in ("XS", "MS")]
-            kb, nb = "P%d" % (4 + h), "P%d" % (6 + h)
-            tag[:] = ["w%d%d_" % (s, h), 0]
-            mm(ap(nb, 0, 72), ap(cf, 1, 129), ap("PERM", 0, 72), True, False)
-            mm(ap(nb, 0, 72), ap(cf, 0, 128), ap("PERM", 72, 144), False, False)
-            stay = ap(nb, 0, 72, 9)
-            if late:
-                mm(stay, ap("KP", 128 * h, 128 * h + 128), ap("SELH", 0, 128, 16), False, False)
-            if s > 0:
-                mm(stay, ap("PAIR"), ap(sw, 0, 8), False, True)
-            elif t > 0:
-                mm(stay, ap("TM", 128 * h, 128 * h + 128), R8, False, True)
-            else:
-                mm(stay, ap("TM", 128 * h, 128 * h + 128, p1=8), ap("IDF", 0, 8, p1=8), False, True)
-            grp = [(ap(kb, 0, 72), ap("IDB"), ap("KC"))]
-            if h in SHIFT:
-                grp.append((ap(kb, 0, 72, 9, p1=64), ap("ZT", 256, 320), ap("BOX", 0, 8)))
-            own = [(ap(kb, 0, 72, 9), ap(xs), ap("BOX", 0, 8)), (ap(kb, 0, 72, 9), ap(ms_), ap("BOM"))]
-            kin = [(ap(kb, 1 + k, 72, 9), ap(src, k, 1024, 8), ap(wt, 0, 8)) for src, wt in ((xg, "BOX"), (mx, "BOM")) for k in range(8)]
-            shut = [(ap(kb, 0, 72, 9), ap("NQ", 256 * k + 128 * h, 256 * k + 128 * h + 128), ap("BOX", 8, 16)) for k in (1, 2, 0)]
-            grp += kin + shut + own if late else own + kin
-            for k, x in enumerate(grp):
-                mm(x[0], x[1], x[2], k == 0, k == len(grp) - 1)
-            key = ap(kb, 0, 72)
-            scan(ap(mm_), ap("RST"), key, ALU.add, ALU.min)
-            tt(ap(ee), key, ap(mm_), ALU.subtract)
-            tt(ap(vl), ap(nb, 0, 72), ap(ee), ALU.subtract)
-            mm(ap(kb, 128, 136), ap("SWAP"), ap(mm_, 8, 72, 9))
-            scan(ap(s2), ap(ee), ap(vl), ALU.min, ALU.max)
-            tt(ap(sw, 8, 16), ap(kb, 128, 136), ap(mm_, 8, 72, 9), ALU.is_gt)
-            tt(ap(sw, 0, 8), ap(s2, 8, 72, 9), ap(sw, 8, 16), ALU.mult)
-            tt(ap(be), ind(ap(sw, 0, 8), ap("CO", 8, 16)), ap("MASK2"), ALU.mult)
-            mm(ap(kb, 272, 276), ap(be), ap("RX2", 0, 64, 16))
-            if s < ST - 1:
-                cp(ap(off, 0, 4), ap(kb, 272, 276))
-            else:
-                bw = ap("BW", 8 * t + 4 * h, 8 * t + 4 * h + 4)
-                cp(bw, ap(kb, 272, 276))
-                act(ap("WF", 64 * h, 64 * h + 64), ind(ap("IOTA"), bw))
-                act(ap("A32", 8 + 4 * h, 12 + 4 * h), ap(kb, 272, 276))
-                cp(ap("KH", 64 * h, 64 * h + 64), ind(ap("KIN"), bw))
-                act(ap("XB", 64 * h, 64 * h + 64), ind(ap("XX", 0, W), bw))
-                act(ap("WK", 64 * h, 64 * h + 64), ind(ap("KIN"), bw))
-
-        if EARLY:
-            front(0, 0)
-            front(0, 1)
-            tag[:] = ["q", 0]
-            cp(ap("KP", 256, 384), ind(ap("KIN"), ap("OB")))
-            mm(ap("P5", 128, 256), ap("KP", 256, 384), ap("SELH"))
-            tt(ap("MKV"), ap("P5", 128, 256), ap("MASK"), ALU.mult)
-            mm(ap("P5", 256, 264), ap("MKV"), ap("RH", 0, 8))
-            cp(ap("OV", 8, 16), ap("P5", 256, 264))
-            act(ap("TS"), ind(ap("IOTA"), ap("OB")))
-            cp(ap("KP", 1, 256, 2), ind(ap("KIN"), ap("OV", 8, 16)))
-            tt(ap("NQ", 1, 256, 2), ind(ap("FT"), ap("OV", 8, 16)), ap("TS"), ALU.not_equal)
-            mm(ap("P5", 128, 256), ap("KP", 1, 256, 2), ap("SELH"))
-            tt(ap("MKV"), ap("P5", 128, 256), ap("MASK"), ALU.mult)
-            mm(ap("P5", 256, 264), ap("MKV"), ap("RH", 0, 8))
-            cp(ap("OV", 0, 8), ap("P5", 256, 264))
-            for h in range(2):
-                act(ap("XS%d" % (h + 2), 1, 128, 2), ind(ap("XX", W, 2 * W), ap("OV", 4 * h, 4 * h + 4)))
-                tt(ap("MS%d" % (h + 2), 1, 128, 2), ap("XS%d" % (h + 2), 1, 128, 2), ap("P%d" % (6 + h), 448, 512), ALU.max)
-            act(ap("AQ", 0, 128), ap("TS"), AF.Abs, bias=-mid)
-            act(ap("NQ", 257, 512, 2), ap("AQ", 0, 128), AF.Relu, scale=-1.0, bias=64.0)
-            for h in range(2):
-                act(ap("AQ", 128 + 64 * h, 192 + 64 * h), ap("CF%d" % h, 1, 129, 2), AF.Abs, bias=-mid)
-            act(ap("NQ", 513, 768, 2), ap("AQ", 128, 256), AF.Relu, bias=-64.0)
         tag[:] = ["p", 0]
         tt(ind(ap("KIN"), ap("OSC", 0, 8)), ap("KM"), ap("U0"), ALU.add)
         act(ap("FT", lo, lo + 128), ind(ap("YC"), ap("OSC", 16, 24)))
         cp(ind(ap("FT"), ap("OSC", 8, 16)), ap("YC", 16, 144))
         dma("Y", ap("WF", 128, 256), ap("FT", lo, lo + 128), "dv%d" % t, 64e3)
-        act(ap("NL", 0, 8), ap("U24", 16, 24), AF.Sign)
-        act(ap("NL", 8, 16), ap("NL", 0, 8), scale=2.0 ** -8 - 1.0, bias=1.0)
-        act(ap("NLX"), ind(ap("NL", 0, 8), ap("CO", 8, 16)), scale=4096.0)
+        act(ap("SG", 0, 8), ap("U24", 16, 24), AF.Sign, bias=-0.5)
+        act(ap("NLR"), ind(ap("TABN"), ap("OSC", 16, 24)))
         if not last:
-            act(ap("AT", 8, 16), ap("NL", 0, 8), scale=-1.0, bias=-523.5 / 1024, acc=ap("AT", 16, 17))
+            act(ap("AT", 8, 16), ap("SG", 0, 8), scale=-0.5, bias=-0.5 - 523.5 / 1024, acc=ap("AT", 16, 17))
         tag[:] = ["r", 0]
         if last:
             rest = [(c0, c1) for c0, c1 in ((B0, lo), (lo + 128, W)) if c0 < c1]
@@ -425,88 +505,67 @@ def build(rank):
                 dma("Y", ("yx", 0, 128, 1, c0 - B0, c1 - B0), ap("XX", c0, c1), "dpre", 100e3)
                 dma("Y", ("yk", 0, 128, 1, c0 - B0, c1 - B0), ap("KIN", c0, c1), "dpre", 200e3)
         for s in range(ST):
+            if s:
+                front(s, 0)
+                front(s, 1)
+            if s == ST - 1:
+                tag[:] = ["u", 0]
+                cp(ap("BF"), ap("B1"))
+                act(ap("AB", 16, 24), ap("BF"), AF.Abs, bias=-mid)
+                act(ap("SG", 8, 16), ap("AB", 16, 24), AF.Sign, bias=64.0, scale=-1.0)
+                mm(ap("P6", 0, 64), ap("IDF"), ap("CD1"), True, False)
+                mm(ap("P6", 3, 64, 8), ap("ID2K"), ap("SG", 0, 8), False, False)
+                mm(ap("P6", 4, 64, 8), ap("ID2K"), ap("SG", 8, 16), False, False)
+                for h in range(2):
+                    mm(ap("P%d" % h), ap("IDB"), ap("TRA", 512 * h, 512 * h + 512), True, False)
+                    for c in range(4 * h, 4 * h + 4):
+                        w, at = min(16 * c + 16, 127), 128 * (c % 4) + 1
+                        mm(ap("P%d" % h, at, at + w), ap("SELB"), ap("NLR", 0, w), False, False)
             for h in range(2):
-                if s or not EARLY:
-                    front(s, h)
                 back(s, h)
+                if s == ST - 1:
+                    mm(ap("P6", 32 * h, 32 * h + 32), ap("BE%d" % h), ap("RX32"), False, h == 1)
+                    finish(h)
         tag[:] = ["e" if last else "s", 0]
-        bw = ap("BW", 8 * t, 8 * t + 8)
-        send(prv if last else nxt, ap("BIN", 8 * t, 8 * t + 8), bw, "rb%d" % t, 2e3)
         brep = ap("WF", 0, 128)
-        mm(ap("P0", 0, 128), ap("IDB"), zin, True, False)
-        mm(ap("P0", 0, 128), ap("IDB"), ap("TRI", 128, 256), False, False)
-        mm(ap("P0", 0, 128), ap("IDB"), ap("XB"), False, True)
-        act(ap("TS"), ap("P0", 0, 128), scale=0.5, bias=MAGIC)
-        act(ap("WX", wx, wx + 128), ap("TS"), bias=-MAGIC)
-        if not last:
-            send(nxt, ap("ZIN", 128 * t + 128, 128 * t + 256), ap("WX", wx, wx + 128), "rz%d" % t, 32e3)
-        else:
-            dma("Y", ("yz",), ap("WX", wx, wx + 128), "dout", 32e3)
-        mm(ap("P2", 0, 128), ap("KH"), ap("SELH"))
-        tt(ap("MKV"), ap("P2", 0, 128), ap("MASK"), ALU.mult)
-        mm(ap("P3", 0, 8), ap("MKV"), ap("RH", 0, 8))
-        cp(ap("OV", 0, 8), ap("P3", 0, 8))
-        act(ap("A32", 16, 24), ap("P3", 0, 8))
-        for d in range(2):
-            mm(ap("P1", 128 * d, 128 * d + 128), ap("IDB"), ap("TRI", 0, 128), True, False)
-            if d:
-                mm(ap("P1", 128, 256), ap("IDB"), ap("NLX"), False, False)
-            for h in range(2):
-                mm(ap("P1", 128 * d + 64 * h, 128 * d + 64 * h + 64), ap("BE%d" % h), ap("RX2"), False, h == 1)
-        for c in range(7):
-            ts(ap("EQ", 144 * c + 16, 128 * c + 128), ap("WF", 16 * c + 16, 128), ap("A32", 8 + c, 9 + c), ALU.is_equal,
-               ap("NL", 8 + c, 9 + c), ALU.mult)
-        tt(ap("EQ", 896, 1024), ap("P1", 0, 128), brep, ALU.is_equal)
-        tt(ap("EQ", 1024, 1152), ap("P1", 128, 256), brep, ALU.is_equal)
-        tt(ap("NH", 0, 128), ind(ap("FT"), ap("OV", 0, 8)), brep, ALU.not_equal)
-        act(ap("AB", 0, 8), ap("A32", 8, 16), AF.Abs, bias=-mid)
-        act(ap("REL", 48, 56), ap("AB", 0, 8), AF.Relu, bias=2.0 ** 30, scale=-2.0 ** 24)
-        act(ap("KM"), ap("WK", 0, 128), scale=nrow0)
-        for c in range(9):
-            mm(ap("P6", 0, 128), ap("EQ", 128 * c, 128 * c + 128), ap("BLKS" if c == 7 else "BLK"), c == 0, c == 8)
-        tt(ap("MKB", 0, 128), ap("P6", 0, 128), ap("THR", 0, 128), ALU.is_ge)
-        mm(ap("P4", 128, 256), ap("NH", 0, 128), ap("SELB"))
-        tt(ap("MKB", 128, 256), ap("P4", 128, 256), ap("MASK"), ALU.mult)
         ol = 32 * t
-        l1, l2, lh, lt = [ap("OL", ol + 8 * k, ol + 8 * k + 8) for k in range(4)]
-        for bk, c0, c1 in (("P7", 0, 16), ("P5", 16, 24)):
-            mm(ap(bk, c0, c1), ap("IDF"), ap("A32", c0, c1), True, False)
-            mm(ap(bk, c0, c1), ap("IDB"), ap("REL", c0, c1), False, False)
-            mm(ap(bk, c0, c1), ap("IDB"), ap("REL", 24 + c0, 24 + c1), False, False)
-            for c in range(c0, c1, 8):
-                mm(ap(bk, c, c + 8), ap("IDB"), ap("REL", 48, 56), False, False)
-            mm(ap(bk, c0, c1), ap("MKB", 0, 128), ap("RBIG", 0, c1 - c0), False, c0 == 0)
-            if c0:
-                mm(ap(bk, c0, c1), ap("MKB", 128, 256), ap("RBIG", 0, 8), False, True)
-            tt(ap("U32", c0, c1), ap(bk, c0, c1), ap("B32", c0, c1), ALU.min)
-            cp(ap("OL", ol + c0, ol + c1), ap("U32", c0, c1))
+        l2, l1, lh, lt = [ap("OL", ol + 8 * k, ol + 8 * k + 8) for k in range(4)]
+        scan(ap("SO"), ap("D0"), ap("P6", 0, 64), ALU.add, ALU.max)
+        cp(l2, ap("SO", 5, 64, 8))
+        cp(l1, ap("SO", 6, 64, 8))
+        hot(3)
+        group(tile(ap("P7", 32, 40), "KH", 0, 128))
+        cp(ap("OV"), ap("P7", 32, 40))
+        act(ap("AV"), ap("P7", 32, 40))
+        tt(ap("NV"), ind(FTG, ap("OV")), brep, ALU.not_equal)
+        group([(ap("P7", 64, 80), ap("IDF"), ap("CD2")), (ap("P7", 64, 80, 2), ap("IDF"), ap("AV"))]
+              + tile(ap("P7", 64, 80, 2), "NV", 0, 128, "SWB"))
+        scan(ap("LH"), ap("SO", 0, 64, 4), ap("P7", 64, 80), ALU.max, ALU.min)
+        cp(lh, ap("LH", 1, 16, 2))
+        act(ap("KM"), ap("WK", 0, 128), scale=nrow0)
         if not last:
-            tt(ap("MKT"), ap("P6", 0, 128), ap("THR", 128, 256), ALU.is_ge)
-            mm(ap("P3", 24, 32), ap("IDF"), ap("A32", 8, 16), True, False)
-            mm(ap("P3", 24, 32), ap("MKT"), ap("RBIG", 0, 8), False, True)
-            tt(ap("U32", 24, 32), ap("P3", 24, 32), ap("B32", 24, 32), ALU.min)
-            cp(lt, ap("U32", 24, 32))
-        act(ap("FT", lo, lo + 128), ind(ap("WF"), l1))
+            act(ap("XX", GW + lo, GW + lo + 128), ind(ap("WX", wx, wx + 256), l1))
         tt(ind(ap("KIN"), l2), ap("KM"), ap("N0", lo - B0, lo - B0 + 128), ALU.add)
+        act(ap("KIN", lo, lo + 128), ind(ap("WK"), l1))
+        act(ap("FT", lo, lo + 128), ind(ap("WF"), l1))
         act(ap("XX", lo, lo + 128), ind(ap("WX", wx, wx + 256), l1))
         cp(ind(ap("FT"), lh), nrep)
-        act(ap("KIN", lo, lo + 128), ind(ap("WK"), l1))
         if not last:
-            act(ap("XX", W + lo, W + lo + 128), ap("XX", lo, lo + 128))
-            act(ap("AT", 8, 16), ap("U32", 0, 8), scale=1.0 / 128, acc=ap("AT", 17, 18))
-            mm(ap("P4", 0, 1), ap("ONES"), ap("AT", 16, 17), True, False)
-            mm(ap("P4", 0, 1), ap("ONES"), ap("AT", 17, 18), False, True)
-            act(ap("AT", 0, 1), ap("P4", 0, 1), scale=1.0 / 32, bias=MAGIC)
-            act(ap("AT", 1, 2), ap("AT", 0, 1), scale=-32.0, bias=32.0 * MAGIC)
-            act(ap("AO", 4 * t, 4 * t + 1), ap("P4", 0, 1), bias=ap("AT", 1, 2))
+            cp(lt, ap("SO", 2, 64, 8))
+            act(ap("AT", 8, 16), ap("SO", 6, 64, 8), scale=1.0 / 128, acc=ap("AT", 17, 18))
+            group([(ap("P6", 192, 193), ap("ONES"), ap("AT", 16, 17)), (ap("P6", 192, 193), ap("ONES"), ap("AT", 17, 18))])
+            ts(ap("AT", 0, 1), ap("P6", 192, 193), 32.0 * MAGIC, ALU.add, 32.0 * MAGIC, ALU.subtract)
+            tt(ap("AO", 4 * t, 4 * t + 1), ap("P6", 192, 193), ap("AT", 0, 1), ALU.subtract)
             send(nxt, ap("AIN", 4 * t, 4 * t + 4), ap("AO", 4 * t, 4 * t + 4), "ra%d" % t, 2e3)
             if t < VIS - 2:
                 send(nxt, ap("LIN", 8 * t, 8 * t + 8), lt, "rl%d" % t, 2e3)
             if t > 0:
                 cp(ind(ap("TT"), ap("LIN", 8 * t - 8, 8 * t)), brep)
         else:
-            act(ap("TS"), ind(ap("IOTA"), ap("BIN", 8 * t, 8 * t + 8)))
-            cp(ind(ap("TO"), ap("OL", ol - 8, ol)), ap("TS"))
+            dma("Y", ("yz",), ap("WX", wx, wx + 128), "dout", 32e3)
+            for h in range(2):
+                act(ap("TS", 64 * h, 64 * h + 64), ind(ap("IOTA"), ap("BIN", 16 * t + 8 * h, 16 * t + 8 * h + 4)))
+                cp(ind(ap("TO"), ap("OL", ol - 8 + 4 * h, ol - 4 + 4 * h)), ap("TS", 64 * h, 64 * h + 64))
             dma("Y", ("yt",), ap("TO", 0, W, ps=16), "dout", 57e3)
             dma("Y", ("yx", 0, 128, 1, lo - B0, lo - B0 + 128), ap("XX", lo, lo + 128), "dout", 32e3)
             dma("S", ("yf",), ap("FT", B0, W, ps=16), "dout", 16e3)
@@ -577,39 +636,58 @@ def depend(ops):
 
 def schedule(ops, deps):
     n = len(ops)
-    users = [[] for _ in range(n)]
+    before, after = [[] for _ in range(n)], [[] for _ in range(n)]
     for i, d in enumerate(deps):
         for j, s in d.items():
-            users[j].append((i, (HOP if s else 0.0) + (ops[j].get("lat", 0.0) if s or ops[i]["e"] == "R" else 0.0)))
+            w = (HOP if s else 0.0) + (ops[j].get("lat", 0.0) if s or ops[i]["e"] == "R" else 0.0)
+            before[i].append((j, w))
+            after[j].append((i, w))
+    tail = [o.get("lat", 0.0) for o in ops]
+
+    def run(pred, succ, first, prio):
+        left = [len(p) for p in pred]
+        rdy = list(first)
+        ready = {e: [] for e in "VSPGYR"}
+        for i in range(n):
+            if not left[i]:
+                ready[ops[i]["e"]].append(i)
+        free = {e: 0.0 for e in ready}
+        fin, seq = [0.0] * n, []
+        for _ in range(n):
+            t0, e = min((max(free[e], min(rdy[i] for i in l)) - AHEAD * (e == "P"), e) for e, l in ready.items() if l)
+            t0 += AHEAD * (e == "P")
+            i = max((i for i in ready[e] if rdy[i] <= t0 + SLACK), key=lambda k: prio[k])
+            if not ops[i].get("hot"):
+                soon = [k for k in ready[e] if ops[k].get("hot") and rdy[k] <= t0 + min(WAIT, ops[i]["c"])]
+                if soon:
+                    i = min(soon, key=lambda k: rdy[k])
+            ready[e].remove(i)
+            fin[i] = free[e] = max(free[e], rdy[i]) + ops[i]["c"]
+            seq.append(i)
+            for u, w in succ[i]:
+                rdy[u] = max(rdy[u], fin[i] + w)
+                left[u] -= 1
+                if not left[u]:
+                    ready[ops[u]["e"]].append(u)
+        return fin, seq
+
     prio = [0.0] * n
     for i in range(n - 1, -1, -1):
-        prio[i] = ops[i]["c"] + max([ops[i].get("lat", 0.0)] + [prio[u] + w for u, w in users[i]])
-    prio = [p + NUDGE.get(o["cl"], 0.0) for p, o in zip(prio, ops)]
-    left = [len(d) for d in deps]
-    rdy = [0.0] * n
-    ready = {e: [] for e in "VSPGYR"}
-    for i in range(n):
-        if not left[i]:
-            ready[ops[i]["e"]].append(i)
-    free = {e: 0.0 for e in ready}
-    order = {e: [] for e in ready}
-    end = 0.0
-    seq = ops[0]["seq"] = []
-    for _ in range(n):
-        t0, e = min((max(free[e], min(rdy[i] for i in l)), e) for e, l in ready.items() if l)
-        i = max((i for i in ready[e] if rdy[i] <= t0 + SLACK), key=lambda k: (prio[k], -k))
-        ready[e].remove(i)
-        st = max(free[e], rdy[i])
-        free[e] = st + ops[i]["c"]
-        ops[i]["t"] = (st, free[e] + ops[i].get("lat", 0.0))
-        end = max(end, ops[i]["t"][1])
-        order[e].append(i)
-        seq.append(i)
-        for u, w in users[i]:
-            rdy[u] = max(rdy[u], free[e] + w)
-            left[u] -= 1
-            if not left[u]:
-                ready[ops[u]["e"]].append(u)
+        prio[i] = ops[i]["c"] + max([tail[i]] + [prio[u] + w for u, w in after[i]])
+    best = None
+    for _ in range(PASSES):
+        fin, seq = run(before, after, [0.0] * n, prio)
+        end = max(f + x for f, x in zip(fin, tail))
+        if best is None or end < best[0]:
+            best = (end, fin, seq)
+        back = run(after, before, tail, fin)[0]
+        prio = [MIX * b + (1 - MIX) * p for b, p in zip(back, prio)]
+    end, fin, seq = best
+    ops[0]["seq"] = seq
+    order = {e: [] for e in "VSPGYR"}
+    for i in seq:
+        ops[i]["t"] = (fin[i] - ops[i]["c"], fin[i] + tail[i])
+        order[ops[i]["e"]].append(i)
     return order, end
 
 
@@ -669,9 +747,10 @@ def rank_program(g, core, T, topo):
             return T[a[0]][:] if len(a) == 1 else T[a[0]][a[1]:a[2]:a[3], a[4]:a[5]]
         if not isinstance(a, dict):
             return a
-        if SCRATCH[a["n"]][0] == "dram":
+        if BUF[a["n"]][0] == "dram":
             return T[a["n"]][:]
-        x = T[a["n"]][a["p0"]:a["p1"]:a["ps"], a["c0"]:a["c1"]:a["st"]]
+        n, at = PLACE[a["n"]]
+        x = T[n][a["p0"]:a["p1"]:a["ps"], at + a["c0"]:at + a["c1"]:a["st"]]
         return x if a["off"] is None else x.indirect(real(a["off"]))
 
     sent = 0
@@ -704,13 +783,15 @@ def rank_program(g, core, T, topo):
                 x = E.tensor_scalar(*(a if a[5] is not None else a[:5]))
             elif k == "scan":
                 x = E.tensor_tensor_scan(*a)
+            elif k == "red":
+                x = E.tensor_reduce(a[0], a[1], AX.X, a[2], negate=a[3], apply_absolute_value=a[4])
             elif k == "memset":
                 x = E.memset(*a)
             elif k == "act":
                 x = E.activation(a[0], a[1], a[2], bias=a[3], scale=a[4], accum_out=a[5])
             elif k == "mm":
                 x = E.matmul(*a)
-            elif SCRATCH[o["a"][0]["n"]][2] == i32:
+            elif BUF[o["a"][0]["n"]][2] == i32:
                 x = E.iota(*a)
             else:
                 x = E.iota(*a, allow_small_or_imprecise_dtypes=True)

from concourse.mybir import AluOpType as ALU, ActivationFunctionType as AF, AxisListType as AX

W, B0, NR, VIS, ST = 1792, 1280, 4, 5, 3
GW = W + 16
SP = 2048
ZONE = 2304
TW = SP + 128
MAGIC = 12582912.0
NENG = 8
f32, bf, i32, u16, h16 = "float32", "bfloat16", "int32", "uint16", "float16"
CUTS = ((0, 32), (32, 48), (48, 64))
VCUTS = ((0, 16), (16, 32), (32, 48), (48, 64))
HBS = False
QMASK = (0,)
OMASK = True
KW = 216
WKEY = (34816.0, 37120.0, 2304.0)
WINC = (2048.0, 2064.0, 16.0)
HIGH = 132 - 7.5 / 16
WCAND = (-4160.0, 0.0, 2112.0)
WSTAY = (-4096.0, -4096.0, -2048.0)

SB = {
    "KIN": (TW, f32), "FT": (TW, f32), "TT": (TW + ZONE, f32), "TO": (TW + ZONE, f32), "XX": (2 * GW, bf), "IOTA": (W, f32),
    "KRAW": (W, i32), "FRAW": (512, i32), "BRAW": (128, i32), "TRAW": (112, i32), "TCF": (112, f32), "FF": (640, f32),
    "PI": (8, i32), "PC": (24, f32), "J2": (128, f32), "JM": (256, f32), "JD": (128, f32), "J8": (32, f32), "JB": (1024, f32),
    "JP": (432, f32), "J3": (24, f32), "MASK2": (128, f32), "SWAP": (128, f32), "IDB": (128, bf), "IDH": (128, h16),
    "IDF": (128, f32), "IDQ": (128, bf), "ID2K": (128, bf), "SELB": (128, bf), "SEL8": (8, h16), "SELP": (24, bf),
    "SW1": (144, h16), "SWB": (144, h16), "RX4": (4, h16), "RX32": (32, h16), "RXB": (512, h16), "EV": (64, h16),
    "TRA": (1024, bf), "PERM": (464, h16), "PERH": (432, bf), "PTMP": (432, f32), "T1": (48, bf), "PAIR": (128, f32),
    "HUGE": (8, bf), "XU": (144, bf), "OP": (8, u16), "TY": (128, f32), "TZ": (128, f32), "MASK": (128, f32), "SELH": (128, h16), "RH": (8, h16),
    "RBIG": (8, h16), "SGN": (128, f32), "EE": (1024, bf), "ZT": (256, bf), "BR": (128, f32), "MO": (256, h16),
    "LO": (KW, h16),
    "W24": (96, f32), "RW": (24, f32), "RWB": (24, bf), "BOX": (24, bf), "BOM": (24, bf), "SH": (72, bf), "EVN": (256, bf),
    "AE": (128, bf), "RST": (KW, f32), "CO": (8, u16), "QUART": (64, bf), "B24": (24, f32), "A24": (24, f32),
    "S8": (128, f32), "ONES": (128, f32), "CD1": (64, f32), "CD2": (16, f32), "D0": (64, f32), "SO": (64, f32),
    "LH": (16, f32), "LANE": (8, f32), "TABN": (144, bf), "NLR": (128, bf), "SG": (16, bf), "YU": (128, h16), "KH": (128, h16),
    "OYU": (16, u16), "AB": (24, f32), "REL": (16, bf), "U24": (24, f32), "OSC": (24, u16), "KM": (128, f32), "U0": (128, f32),
    "N0": (512, f32), "YC": (144, f32), "WK": (256, f32), "WF": (256, f32), "TM": (256, h16), "TS": (128, f32),
    "OB": (16, u16), "OG": (8, u16), "B1": (8, u16), "B2": (8, u16), "BF": (8, f32), "XB": (128, bf), "OV": (8, u16),
    "NH": (256, h16), "NV": (128, h16), "AT": (32, f32), "AV": (8, f32),
}
for _h in range(2):
    SB.update({"OFF%d" % _h: (64, u16), "XG%d" % _h: (1024, bf), "MX%d" % _h: (1024, bf), "CF%d" % _h: (130, h16),
               "HB%d" % _h: (130, bf), "XS%d" % _h: (128, bf), "MS%d" % _h: (128, bf), "M%d" % _h: (KW, f32),
               "MN%d" % _h: (8, f32), "S3%d" % _h: (24, f32), "BE%d" % _h: (128, h16), "BU%d" % _h: (128, h16),
               "KP%d" % _h: (128, h16), "HP%d" % _h: (128, bf), "FL%d" % _h: (256, bf), "NQ%d" % _h: (128, bf)})
SB.update({"WX": (256 * VIS, bf), "ZIN": (128 * VIS, bf), "BW": (16 * VIS, u16), "BIN": (16 * VIS, u16),
           "OL": (32 * VIS, u16), "LIN": (8 * VIS, u16), "AO": (4 * VIS, f32), "AIN": (4 * VIS, f32)})
BUF = {k: ("sbuf", [128, v[0]], v[1]) for k, v in SB.items()}
for _k in range(8):
    BUF["P%d" % _k] = ("psum", [128, 512], f32)
for _k in ("DT0", "DT1", "DT2"):
    BUF[_k] = ("dram", [128, 112], f32)
SCRATCH, PLACE, _end = {}, {}, {}
for _k, _v in BUF.items():
    if _v[0] == "sbuf" and _v[1][1] <= 64:
        PLACE[_k] = ("S" + _v[2], _end.get(_v[2], 0))
        _end[_v[2]] = PLACE[_k][1] - (-_v[1][1] // 16) * 16
        SCRATCH["S" + _v[2]] = ("sbuf", [128, _end[_v[2]]], _v[2])
    else:
        PLACE[_k] = (_k, 0)
        SCRATCH[_k] = _v
DMASEM = ["dk0", "dk1", "dk2", "dk3", "dpre", "dx0", "dx1", "dz", "df", "db", "dt", "dtt", "dd1", "dto", "dout"]
DMASEM += ["d%s%d" % (k, t) for k in "ywv" for t in range(VIS)]
RSEM = ["r%s%d" % (k, t) for k in "bczyla" for t in range(VIS)] + ["rt0", "rt1"]
SEMAPHORES = ["cV", "cS", "cP", "cG", "sent"] + DMASEM + RSEM
CY, CG, CS, HOP, NET = 0.83, 1.56, 3.8, 180.0, 3500.0
PF, PE, FX, FS = 0, 0.36, 0, 0
PASSES, MIX, AHEAD, WAIT, SLACK = 4, 0.5, 400.0, 0.0, 90.0


def ap(name, c0=0, c1=None, st=1, p0=0, p1=128, ps=1, off=None):
    if c1 is None:
        c1 = BUF[name][1][1]
    return {"n": name, "c0": c0, "c1": c1, "st": st, "p0": p0, "p1": p1, "ps": ps, "off": off}


def ind(win, off):
    d = dict(win)
    d["off"] = off
    return d


def width(a):
    if a["off"] is not None:
        return 16 * width(a["off"])
    return len(range(a["c0"], a["c1"], a["st"]))


def two(a):
    return BUF[a["n"]][2] in (bf, u16, h16)


def psum(a):
    return BUF[a["n"]][0] == "psum"


def build(rank):
    ops = []
    tag = ["i", 0]
    prev = {}

    def add(eng, kind, args, rd, wr, cost, **kw):
        r = []
        for a in rd + wr:
            if isinstance(a, dict) and a["off"] is not None:
                r.append(a["off"])
        r += [a for a in rd if isinstance(a, dict)]
        o = {"e": eng, "k": kind, "a": args, "r": r, "w": [a for a in wr if isinstance(a, dict)], "c": cost}
        o.update(kw)
        o["cl"] = "%s%d" % (tag[0], tag[1])
        tag[1] += 1
        ops.append(o)
        return len(ops) - 1

    def chain(q, i):
        if q in prev:
            ops[i]["after"] = prev[q]
        prev[q] = i

    def vcost(out, a, per, fx=FX):
        if out["off"] is not None:
            return 50 + width(out) * CS * CY
        if a["off"] is not None:
            return 40 + fx + width(a) * CG * CY
        return fx + max(64, width(a) * per) * CY

    def cp(out, a):
        add("V", "copy", (out, a), [a], [out], vcost(out, a, 0.5 if two(out) and two(a) else 1))

    def tt(out, a, b, op):
        add("V", "tt", (out, a, b, op), [a, b], [out], vcost(out, a, 1 if psum(a) or psum(b) else 2))

    def ts(out, a, s1, op0, s2=None, op1=None):
        add("V", "ts", (out, a, s1, s2, op0, op1), [a, s1, s2], [out], vcost(out, a, 0.5 if two(out) and two(a) else 1))

    def hot(k=1):
        for o in ops[-k:]:
            o["hot"] = True

    def scan(out, d0, d1, op0, op1, first=0.0):
        add("V", "scan", (out, d0, d1, first, op0, op1), [d0, d1], [out], vcost(out, d0, 1))

    def least(out, a):
        add("V", "red", (out, a, ALU.min, True, True), [a], [out], vcost(out, a, 1))

    def ms(out, v):
        add("V", "memset", (out, v), [], [out], vcost(out, out, 0.5 if two(out) else 1))

    def act(out, a, fn=AF.Identity, bias=0.0, scale=1.0, acc=None):
        add("S", "act", (out, a, fn, bias, scale, acc), [a, bias, scale], [out, acc], vcost(out, a, 1, FS))

    def mm(out, l, r, start=True, stop=True):
        c = max(min(64, width(l)), width(r)) * (1 if two(l) else 4)
        add("P", "mm", (out, l, r, start, stop), [l, r], [out], PF + c * PE)

    def group(calls):
        for k, x in enumerate(calls):
            mm(x[0], x[1], x[2], k == 0, k == len(calls) - 1)

    def tile(out, src, c0, c1, sel="SW1", step=1):
        return [(out, ap(sel, 15 - a, 143 - a), ap(src, c0 + step * a, c1, 16 * step)) for a in range(16)]

    def iota(out, pat, base=0, cm=0):
        chain("G", add("G", "iota", (out, pat, base, cm), [], [out], 130 + 2 * width(out) * CY))

    def dma(q, out, a, sem, nbytes, behind=None):
        i = add(q, "dma", (out, a), [a], [out], 60, sem=sem, lat=1900 + nbytes / 180.0, behind=behind)
        if tag[0] == "i":
            chain(q, i)

    def send(dst, out, a, sem, nbytes):
        i = add("G", "send", (dst, out, a, sem), [a], [], 300)
        add("R", "recv", (), [], [out], 0, sem=sem, after=i, lat=NET + nbytes / 40.0)

    nxt, prv = (rank + 1) % NR, (rank - 1) % NR
    KING, FTG, TTG = ap("KIN", 0, GW), ap("FT", 0, W), ap("TT", 0, W)
    XR, XM = ap("XX", 0, GW), ap("XX", GW, 2 * GW)
    dma("S", ap("FRAW", p1=8), ("ft",), "df", 16e3)
    dma("S", ap("BRAW", p1=8), ("bs",), "db", 4e3)
    for k, c in enumerate((3, 2, 1, 0)):
        dma("Y", ap("KRAW", 448 * c, 448 * c + 448), ("kn", 0, 128, 1, 448 * c, 448 * c + 448), "dk%d" % c, 240e3 * (k + 1))
    dma("S", ap("ZIN", 0, 128), ("z0",), "dz", 300e3)
    dma("S", ap("TRAW"), ("tr",), "dt", 400e3)
    dma("Y", ap("XX", GW, GW + W), ("x0",), "dx1", 1450e3)
    dma("Y", ap("XX", 0, W), ("x0",), "dx0", 1900e3)
    pid, pmod, pdiv, podd, phalf, pm2, p32, row0, nrow0, even, odd8, stay = [ap("PC", k, k + 1) for k in range(12)]
    iota(ap("PI", 0, 1), [[0, 1]], 0, 1)
    iota(ap("IOTA", 0, 144), [[1, 144]])
    iota(ap("JD"), [[1, 8], [0, 16]])
    iota(ap("J3"), [[1, 8], [0, 3]])
    iota(ap("JM"), [[0, 16], [1, 16]])
    iota(ap("J8"), [[0, 4], [1, 8]])
    iota(ap("J2"), [[1, 64], [0, 2]])
    for o in range(2):
        iota(ap("JP", KW * o, KW * o + KW), [[16, 8], [1000, 3], [1, 9]], 8 * o - 2001)
    ts(ap("PI", 1, 2), ap("PI", 0, 1), 15, ALU.bitwise_and)
    ts(ap("PI", 2, 3), ap("PI", 0, 1), 4, ALU.logical_shift_right)
    ts(ap("PI", 3, 4), ap("PI", 0, 1), 1, ALU.bitwise_and)
    ts(ap("PI", 4, 5), ap("PI", 0, 1), 1, ALU.logical_shift_right)
    ts(ap("PI", 5, 6), ap("PI", 0, 1), 1, ALU.logical_shift_right, 15, ALU.bitwise_and)
    ts(ap("PI", 6, 7), ap("PI", 0, 1), 5, ALU.logical_shift_right)
    cp(ap("PC", 0, 7), ap("PI", 0, 7))
    ts(row0, pmod, 0.0, ALU.is_equal)
    ts(nrow0, pmod, 0.0, ALU.not_equal)
    act(even, podd, scale=-1.0, bias=1.0)
    act(odd8, podd, scale=8.0)
    act(stay, podd, scale=16384.0 + 2048.0, bias=-2048.0)
    ts(ap("IDF"), ap("IOTA", 0, 128), pid, ALU.is_equal)
    cp(ap("IDH"), ap("IDF"))
    act(ap("IDB"), ap("IDF"))
    act(ap("IDQ"), ap("IDF"), scale=0.5)
    act(ap("ID2K"), ap("IDF"), scale=2048.0)
    ts(ap("S8", p1=8), ap("JD", p1=8), ap("PC", 0, 1, p1=8), ALU.is_equal)
    act(ap("PC", 12, 13), pid, bias=15.0)
    act(ap("PC", 13, 14), row0, scale=4096.0)
    ts(ap("SW1"), ap("IOTA", 0, 144), ap("PC", 12, 13), ALU.is_equal, row0, ALU.mult)
    ts(ap("SWB"), ap("IOTA", 0, 144), ap("PC", 12, 13), ALU.is_equal, ap("PC", 13, 14), ALU.mult)
    ts(ap("MASK2"), ap("JM", 0, 128), pm2, ALU.is_equal, -2048.0, ALU.mult)
    ts(ap("SWAP"), ap("J2"), phalf, ALU.is_equal, 128.0, ALU.mult)
    ts(ap("PAIR"), ap("J2"), phalf, ALU.is_equal)
    ts(ap("J2"), ap("IDF"), 256.0, ALU.mult)
    tt(ap("SWAP"), ap("SWAP"), ap("J2"), ALU.subtract)
    act(ap("HUGE"), ap("J8", 0, 8), scale=0.0, bias=2.0 ** 40)
    for h in range(2):
        mm(ap("P%d" % (4 + h), 225, 248, 3), ap("IDB"), ap("HUGE"))
    ts(ap("SELB"), ap("JD"), pdiv, ALU.is_equal, row0, ALU.mult)
    ts(ap("SEL8"), ap("J8", 0, 8), pdiv, ALU.is_equal, row0, ALU.mult)
    ts(ap("RX4"), ap("J8", 0, 4), p32, ALU.is_equal)
    for j in range(3):
        for k, tab in enumerate((WKEY, WINC, WCAND, WSTAY)):
            act(ap("W24", 24 * k + j, 24 * k + 24, 3), ap("J8", 0, 8), scale=0.0, bias=tab[j])
        act(ap("SELP", j, 24, 3), ap("SELB", 0, 128, 16), scale=(16.0, 0.0, -16.0)[j])
    ts(ap("RW"), ap("J3"), pdiv, ALU.is_equal)
    tt(ap("RW"), ap("RW"), ap("W24", 0, 24), ALU.mult)
    act(ap("RWB"), ap("RW"))
    act(ap("BOX"), ap("RW"), scale=-1.0)
    act(ap("BOM"), ap("RW"), scale=2.0)
    for k, v in enumerate((32.0, -32.0, 32768.0)):
        ts(ap("SH", 24 * k, 24 * k + 24), ap("RW"), row0, ALU.mult, v, ALU.mult)
    act(ap("T1", 0, 24), ap("W24", 0, 24), scale=-2048.0)
    act(ap("T1", 24, 48), ap("W24", 0, 24), scale=stay)
    ts(ap("MASK"), ap("JM", 0, 128), pmod, ALU.is_equal)
    ts(ap("SELH"), ap("JD"), pdiv, ALU.is_equal, row0, ALU.mult)
    ts(ap("RH"), ap("J8", 0, 8), pdiv, ALU.is_equal)
    ts(ap("RBIG"), ap("J8", 0, 8), pdiv, ALU.is_equal, 4096.0, ALU.mult)
    act(ap("SGN"), ap("JM", 0, 128), AF.Sign)
    for k in range(16):
        act(ap("EE", k, 1024, 16, p1=64), ap("IDF", 0, 64, p1=64))
    ts(ap("AB"), ap("W24", 24, 48), odd8, ALU.mult)
    tt(ap("LO", 1, KW, 9), ap("AB"), ap("W24", 48, 72), ALU.add)
    for s in range(2, 9):
        tt(ap("LO", s, KW, 9), ap("LO", s - 1, KW, 9), ap("W24", 24, 48), ALU.add)
    act(ap("A24"), ap("W24", 48, 72), scale=podd)
    act(ap("U24"), ap("W24", 72, 96), scale=even)
    tt(ap("LO", 0, KW, 9), ap("A24"), ap("U24"), ALU.add)
    ms(ap("PERM", 432, 464), 0.0)
    ts(ap("PERM", 0, 432), ap("JP"), pid, ALU.is_equal)
    ms(ap("PERM", 0, 432, 9), 0.0)
    ts(ap("PTMP"), ap("PERM", 0, 432), -16.0, ALU.mult)
    ts(ap("JP"), ap("PERM", 18, 450), 16.0, ALU.mult)
    tt(ap("PERH"), ap("PTMP"), ap("JP"), ALU.add)
    act(ap("RST"), ap("JM", 0, KW), scale=0.0)
    act(ap("RST", 0, KW, 9), ap("J3"), scale=0.0, bias=2.0 ** 60)
    ts(ap("CO"), ap("J8", 0, 8), 3.0, ALU.mult, 2.0, ALU.add)
    act(ap("LANE"), ap("J8", 0, 8), scale=16.0, bias=pmod)
    for c0, off in ((0, SP), (8, SP), (16, 16)):
        act(ap("B24", c0, c0 + 8), ap("LANE"), bias=float(off))
    for n, c0, c1, v in (("YC", 0, 16, float(W)), ("KIN", W, GW, -1.0), ("AO", 0, 4 * VIS, 0.0), ("XX", W, GW, 0.0),
                         ("XX", GW + W, 2 * GW, 0.0), ("QUART", 0, 64, -0.5), ("ONES", 0, 128, 1.0), ("TABN", 0, 16, 0.0),
                         ("TABN", 16, 144, float(ZONE)), ("EVN", 0, 256, 0.0), ("CD1", 0, 64, 0.0), ("CD2", 0, 16, 0.0),
                         ("D0", 0, 64, 0.0), ("XU", 0, 144, 1024.0)):
        act(ap(n, c0, c1), ap("JM", 0, c1 - c0), scale=0.0, bias=v)
    act(ap("A24", 16, 24), ap("LANE"), scale=0.0)
    act(ap("EVN", 0, 128, 2), ap("JM", 0, 64), scale=0.0, bias=1.0 / 16)
    act(ap("EVN", 128, 256, 2), ap("JM", 0, 64), scale=0.0, bias=15.5 / 16)
    for k, (sc, v) in {0: (0.0, 32768.0), 1: (1.0, SP + ZONE), 3: (1.0, SP - 2048), 4: (1.0, SP - 2048), 6: (1.0, 0),
                       2: (0.0, 4096.0), 5: (0.0, 4096.0)}.items():
        act(ap("CD1", k, 64, 8), ap("LANE"), scale=sc, bias=float(v))
    act(ap("CD2", 1, 16, 2), ap("LANE"), bias=float(SP))
    for k, v in {1: -65536.0, 3: -float(ZONE), 6: 128.0 - SP}.items():
        act(ap("D0", k, 64, 8), ap("LANE"), scale=0.0, bias=v)
    for h in range(2):
        for n in ("XS", "MS", "HP", "NQ"):
            act(ap("%s%d" % (n, h)), ap("JD"), scale=0.0)
        act(ap("HB%d" % h), ap("JM", 0, 130), scale=0.0)
        act(ap("FL%d" % h), ap("JM"), scale=0.0)
        ms(ap("CF%d" % h), 0.0)
        ms(ap("KP%d" % h), 0.0)
    ms(ap("TM"), 0.0)
    for c in range(4):
        cp(ap("KIN", 448 * c, 448 * c + 448), ap("KRAW", 448 * c, 448 * c + 448))
    cp(ap("FF", 0, 512, p1=8), ap("FRAW", p1=8))
    cp(ap("FF", 512, 640, p1=8), ap("BRAW", p1=8))
    mm(ap("P3"), ap("S8", p1=8), ap("FF", 0, 512, p1=8))
    act(ap("FT", B0, W), ap("P3"))
    mm(ap("P2", 0, 128), ap("S8", p1=8), ap("FF", 512, 640, p1=8))
    tt(ap("TM", 0, 256, 2), ap("P2", 0, 128), ap("MASK"), ALU.mult)
    act(ap("BR"), ap("P2", 0, 128))
    iota(ap("IOTA", B0, W), [[1, W - B0]], B0)
    iota(ap("FT", 0, B0), [[0, B0]], -1)
    act(ap("N0"), ap("IOTA", B0, W), scale=row0)
    cp(ap("TCF"), ap("TRAW"))
    send(nxt, ap("DT0"), ap("TCF"), "rt0", 57e3)
    iota(ap("IOTA", 144, B0), [[1, B0 - 144]], 144)
    tag[:] = ["j", 0]
    iota(ap("JB"), [[-16, 8], [1, 128]], -1)
    ts(ap("TRA"), ap("JB"), pmod, ALU.is_ge, 2.0 ** 26, ALU.mult)
    ms(ap("TRA", 0, 1024, 128), 2.0 * ZONE)
    iota(ap("JB", 0, 512), [[1, 4], [0, 128]])
    ts(ap("RXB"), ap("JB", 0, 512), p32, ALU.is_equal, -8192.0, ALU.mult)
    ts(ap("EV"), ap("PAIR", 0, 128, 2), 8192.0, ALU.mult)
    ms(ap("RX32"), 0.0)
    for k in (2, 5):
        cp(ap("RX32", k, 32, 8), ap("RX4"))
    for a in range(16):
        dma("Y", ap("TT", 0, W, p0=a, ps=16), ap("DT0"), "dtt", 920e3)

    turn = []
    for t in range(VIS):
        r = (rank - t) % NR
        lo = B0 + 128 * r
        mid = lo + 63.5
        last = t == VIS - 1
        wx = 256 * t
        nrep = ap("IOTA", lo, lo + 128)

        def zin(c0, c1):
            return ap("ZIN", 128 * t + c0, 128 * t + c1)

        def place(s, h):
            return ap("OB", 8 * h, 8 * h + 4) if s == 0 else ap("B%d" % s, 4 * h, 4 * h + 4)

        def arrive(h):
            tag[:] = ["b%d_" % h, 0]
            tm, c0, c1 = ap("TM", 128 * h, 128 * h + 128, 2), 64 * h, 64 * h + 64
            if t:
                came = ap("BIN", 16 * t - 16 + 8 * h, 16 * t - 12 + 8 * h)
                tt(tm, ind(TTG, came), ap("MASK", 0, 64), ALU.mult)
                hot()
                act(ap("BR", c0, c1), ind(TTG, came))
            scan(ap("TS", c0, c1), ap("SGN", 0, 64), tm, ALU.mult, ALU.add)
            cp(place(0, h), ap("TS", c0 + 15, c1, 16))
            hot(2)
            mm(ap("P%d" % (2 * h + 1), 0, 128, p1=64), zin(c0, c1), ap("IDB"))
            act(ap("ZT", 128 * h, 128 * h + 128, p1=64), ap("P%d" % (2 * h + 1), 0, 128, p1=64), bias=-128.0)
            for bk in range(2):
                mm(ap("P%d" % (2 * h + bk)), ap("ZT", 128 * h, 128 * h + 128, p1=64), ap("EE", 512 * bk, 512 * bk + 512, p1=64))

        def front(s, h):
            off, xg, mx, cf, hb, xs, ms_ = ["%s%d" % (n, h) for n in ("OFF", "XG", "MX", "CF", "HB", "XS", "MS")]
            tag[:] = ["f%d%d_" % (s, h), 0]
            cp(ap(off), ind(KING, place(s, h)))
            hot()
            for c0, c1 in CUTS:
                act(ap(xg, 16 * c0, 16 * c1), ind(XM, ap(off, c0, c1)), bias=-128.0)
                if turn:
                    ops[-1]["after"] = turn[0]
                turn[:] = [len(ops) - 1]
            act(ap(xs, 0, 128, 2), ind(XR, place(s, h)))
            cp(ap(cf, 1, 129, 2), ap(off))
            if HBS:
                act(ap(hb, 1, 129, 2), ind(KING, place(s, h)), scale=1.0 / 16, bias=HIGH)
            else:
                ts(ap(hb, 1, 129, 2), ap(off), 1.0 / 16, ALU.mult, HIGH, ALU.add)
            tt(ap(ms_, 0, 128, 2), ap(xs, 0, 128, 2), zin(64 * h, 64 * h + 64), ALU.max)
            for c0, c1 in VCUTS:
                z0 = 16 * c0 % 512
                tt(ap(mx, 16 * c0, 16 * c1), ap(xg, 16 * c0, 16 * c1), ap("P%d" % (2 * h + c0 // 32), z0, z0 + 16 * (c1 - c0)), ALU.max)

        def early(h):
            tag[:] = ["q%d_" % h, 0]
            op, at = ap("OB", 8 * h + 4, 8 * h + 8), ap("OP", 4 * h, 4 * h + 4)
            group(tile(ap("P6", 8, 12), "CF%d" % h, 1, 128, step=2))
            ts(at, ap("P6", 8, 12), lo - 1.0, ALU.subtract, 129.0, ALU.min)
            cp(op, ap("P6", 8, 12))
            act(ap("XS%d" % h, 1, 128, 2), ind(ap("XU"), at))
            tt(ap("MS%d" % h, 1, 128, 2), ap("XS%d" % h, 1, 128, 2), zin(64 * h, 64 * h + 64), ALU.max)
            cp(ap("KP%d" % h, 1, 128, 2), ind(KING, op))
            act(ap("HP%d" % h, 1, 128, 2), ind(KING, op), scale=1.0 / 16, bias=HIGH)
            act(ap("FL%d" % h, 1, 128, 2), ind(XM, place(0, h)), AF.Relu, bias=-512.0)
            tt(ap("NQ%d" % h, 1, 128, 2), ind(FTG, op), ap("BR", 64 * h, 64 * h + 64), ALU.not_equal)

        def back(s, h):
            xg, mx, cf, hb, xs, ms_, m, mn, s3, be = ["%s%d" % (n, h) for n in ("XG", "MX", "CF", "HB", "XS", "MS", "M", "MN", "S3", "BE")]
            kb = "P%d" % (4 + h)
            tag[:] = ["w%d%d_" % (s, h), 0]
            key, own, ownb = ap(kb, 0, KW), ap(kb, 0, KW, 9), ap(kb, 18, KW, 27)
            grp = [(key, ap("IDH"), ap("LO")), (own, ap("IDB"), ap("T1", 24, 48) if s else ap("T1", 0, 24))]
            grp += [(key, ap(src, 1 - o, 129 - o), ap(pm, KW * o, KW * o + KW)) for src, pm in ((cf, "PERM"), (hb, "PERH")) for o in range(2)]
            dist = [(own, ap(xs), ap("BOX")), (own, ap(ms_), ap("BOM"))]
            shift = [(own, ap("EVN", 128, 256), ap("RWB")), (own, ap("AE"), ap("RWB"))] if t else []
            kin = [(ap(kb, 1 + k, KW, 9), ap(src, k, 1024, 8), ap(wt)) for src, wt in ((xg, "BOX"), (mx, "BOM")) for k in range(8)]
            if s:
                grp += [(ownb, ap("PAIR"), ap(mn))] + shift + dist + kin
            else:
                grp += kin + [(own, ap("FL%d" % h, 0, 128), ap("SH", 0, 24)),
                              (own, ap("NQ%d" % h), ap("SH", 48, 72)), (ownb, ap("TM", 128 * h, 128 * h + 128), ap("RH")),
                              (ownb, ap("KP%d" % h), ap("SEL8")), (own, ap("HP%d" % h), ap("SELP"))] + dist + shift
            group(grp)
            scan(ap(m), ap("RST"), key, ALU.add, ALU.min)
            hot()
            mm(ap(kb, 226, 248, 3), ap("SWAP"), ap(m, 17, KW, 27))
            mm(ap(kb, 224, 248, 3), ap("IDF"), ap(m, 8, KW, 27))
            scan(ap(s3), ap(m, 8, KW, 9), ap(kb, 224, 248), ALU.subtract, ALU.min, -1.0)
            hot()
            tt(ap(be), ind(ap(s3), ap("CO")), ap("MASK2"), ALU.max)
            hot()
            mm(ap(kb, 256, 260), ap(be), ap("RX4"))
            if s < ST - 1:
                ts(place(s + 1, h), ap(kb, 256, 260), 4096.0, ALU.add)
                hot()
                act(ap(mn), ap(s3, 2, 24, 3), AF.Relu, bias=2048.0)

        def finish(h):
            tag[:] = ["g%d_" % h, 0]
            kb, c0, c1 = "P%d" % (4 + h), 64 * h, 64 * h + 64
            bw = ap("BW", 16 * t + 8 * h, 16 * t + 8 * h + 4)
            ts(ap("BU%d" % h), ind(ap("S3%d" % h), ap("CO")), -2048.0, ALU.max)
            for c in range(4 * h, 4 * h + 4):
                w, at = min(16 * c + 16, 127), 128 * (c % 4) + 1
                if h:
                    mm(ap("P1", at + 64, at + w), ap("BU1"), ap("EV", 0, w - 64), False, False)
                else:
                    mm(ap("P0", at, at + w), ap("BU0"), ap("EV", 0, w), False, False)
                mm(ap("P%d" % h, at, at + w), ap("BE%d" % h), ap("RXB", at - 1, at - 1 + w), False, c % 4 == 3)
            if not h:
                for c in range(4):
                    mm(ap("P1", 128 * c + 1, 128 * c + 65), ap("BU0"), ap("EV"), False, False)
            ts(bw, ap(kb, 256, 260), 4096.0, ALU.add)
            hot()
            send(prv if last else nxt, ap("BIN", 16 * t + 8 * h, 16 * t + 8 * h + 4), bw, "r%s%d" % ("bc"[h], t), 1e3)
            for c in range(4 * h, 4 * h + 4):
                least(ap("D0", 8 * c + 2, 8 * c + 3), ap("P%d" % h, 128 * (c % 4), 128 * (c % 4) + 1 + min(16 * c + 16, 127)))
            act(ap("XB", c0, c1), ind(XR, bw))
            cp(ap("KH", c0, c1), ind(KING, bw))
            act(ap("WF", c0, c1), ind(ap("IOTA"), bw))
            act(ap("WK", c0, c1), ind(KING, bw))
            group([(ap(kb, 320, 384), ap("IDQ"), zin(c0, c1)), (ap(kb, 320, 384), ap("IDQ"), ap("QUART")),
                   (ap(kb, 320, 384), ap("IDQ"), ap("XB", c0, c1))])
            ts(ap("WX", wx + c0, wx + c1), ap(kb, 320, 384), MAGIC, ALU.add, MAGIC, ALU.subtract)
            if not last:
                send(nxt, ap("ZIN", 128 * t + 128 + c0, 128 * t + 128 + c1), ap("WX", wx + c0, wx + c1), "r%s%d" % ("zy"[h], t), 16e3)

        tag[:] = ["a", 0]
        ms(ap("XX", GW + lo, GW + lo + 128), 1024.0)
        if t:
            act(ap("AE"), ap("EVN", 0, 128), scale=ap("AIN", 4 * t - 4, 4 * t - 3))
        dma("Y", ap("YC", 16, 144), ap("FT", lo, lo + 128), "dy%d" % t, 64e3)
        dma("Y", ap("WK", 128, 256), ap("KIN", lo, lo + 128), "dw%d" % t, 64e3)
        dma("Y", ap("WX", wx + 128, wx + 256), ap("XX", lo, lo + 128), "dw%d" % t, 32e3)
        for h in range(2):
            arrive(h)
        if last:
            dma("Y", ap("DT1"), ap("TT", 0, W, ps=16), "dd1", 57e3)
            send(prv, ap("DT2"), ap("DT1"), "rt1", 57e3)
            dma("Y", ap("TO", 0, W, ps=16), ap("DT2"), "dto", 57e3)
        tag[:] = ["n", 0]
        cp(ap("YU"), ap("KIN", lo, lo + 128))
        group(tile(ap("P6", 72, 80), "YU", 0, 128))
        cp(ap("OYU", 8, 16), ap("P6", 72, 80))
        act(ap("XU", 1, 129), ind(XM, ap("OYU", 8, 16)))
        act(ap("AB", 8, 16), ap("P6", 72, 80), AF.Abs, bias=-mid)
        act(ap("A24", 8, 16), ap("P6", 72, 80))
        for h in range(2):
            front(0, h)
            early(h)
        tag[:] = ["o", 0]
        tt(ap("TY"), ap("FT", lo, lo + 128), ap("MASK"), ALU.mult)
        scan(ap("TZ"), ap("SGN"), ap("TY"), ALU.mult, ALU.add)
        cp(ap("OYU", 0, 8), ap("TZ", 15, 128, 16))
        act(ap("AB", 0, 8), ap("TZ", 15, 128, 16), AF.Abs, bias=-mid)
        act(ap("A24", 0, 8), ap("TZ", 15, 128, 16))
        tt(ap("NH", 0, 128), ind(KING, ap("OYU", 0, 8)), nrep, ALU.not_equal)
        tt(ap("NH", 128, 256), ind(FTG, ap("OYU", 8, 16)), nrep, ALU.not_equal)
        act(ap("REL"), ap("AB", 0, 16), AF.Relu, bias=2.0 ** 30, scale=-2.0 ** 24)
        act(ap("KM"), ind(KING, ap("OYU", 0, 8)), scale=nrow0)
        act(ap("U0"), ap("KIN", lo, lo + 128), scale=row0)
        if OMASK:
            mm(ap("P7", 256, 384), ap("NH", 0, 128), ap("SELH"))
            group([(ap("P7", 384, 512), ap("NH", c, c + 128), ap("SELH")) for c in (0, 128)])
            for c in (0, 128):
                tt(ap("MO", c, c + 128), ap("P7", 256 + c, 384 + c), ap("MASK"), ALU.mult)
            miss = [(ap("P7", 128 + 8 * k, 136 + 8 * k), ap("MO", 128 * k, 128 * k + 128), ap("RBIG")) for k in range(2)]
        else:
            miss = tile(ap("P7", 136, 144), "NH", 0, 128, "SWB") + tile(ap("P7", 128, 144), "NH", 0, 256, "SWB")
        group([(ap("P7", 128, 152), ap("IDF"), ap("A24"))]
              + [(ap("P7", 128 + c, 136 + c), ap("IDB"), ap("REL", k, k + 8)) for c in (0, 8, 16) for k in (0, 8)] + miss)
        tt(ap("U24"), ap("P7", 128, 152), ap("B24"), ALU.min)
        cp(ap("OSC"), ap("U24"))
        tag[:] = ["p", 0]
        tt(ind(ap("KIN"), ap("OSC", 0, 8)), ap("KM"), ap("U0"), ALU.add)
        act(ap("FT", lo, lo + 128), ind(ap("YC"), ap("OSC", 16, 24)))
        cp(ind(ap("FT"), ap("OSC", 8, 16)), ap("YC", 16, 144))
        dma("Y", ap("WF", 128, 256), ap("FT", lo, lo + 128), "dv%d" % t, 64e3)
        act(ap("SG", 0, 8), ap("U24", 16, 24), AF.Sign, bias=-0.5)
        act(ap("NLR"), ind(ap("TABN"), ap("OSC", 16, 24)))
        if not last:
            act(ap("AT", 8, 16), ap("SG", 0, 8), scale=-0.5, bias=-0.5 - 523.5 / 1024, acc=ap("AT", 16, 17))
        tag[:] = ["r", 0]
        if last:
            rest = [(c0, c1) for c0, c1 in ((B0, lo), (lo + 128, W)) if c0 < c1]
            for c0, c1 in rest:
                dma("Y", ("yx", 0, 128, 1, c0 - B0, c1 - B0), ap("XX", c0, c1), "dpre", 100e3)
                dma("Y", ("yk", 0, 128, 1, c0 - B0, c1 - B0), ap("KIN", c0, c1), "dpre", 200e3)
        for s in range(ST):
            if s:
                front(s, 0)
                front(s, 1)
            if s == ST - 1:
                tag[:] = ["u", 0]
                cp(ap("BF"), ap("B1"))
                act(ap("AB", 16, 24), ap("BF"), AF.Abs, bias=-mid)
                act(ap("SG", 8, 16), ap("AB", 16, 24), AF.Sign, bias=64.0, scale=-1.0)
                mm(ap("P6", 0, 64), ap("IDF"), ap("CD1"), True, False)
                mm(ap("P6", 3, 64, 8), ap("ID2K"), ap("SG", 0, 8), False, False)
                mm(ap("P6", 4, 64, 8), ap("ID2K"), ap("SG", 8, 16), False, False)
                for h in range(2):
                    mm(ap("P%d" % h), ap("IDB"), ap("TRA", 512 * h, 512 * h + 512), True, False)
                    for c in range(4 * h, 4 * h + 4):
                        w, at = min(16 * c + 16, 127), 128 * (c % 4) + 1
                        mm(ap("P%d" % h, at, at + w), ap("SELB"), ap("NLR", 0, w), False, False)
            for h in range(2):
                back(s, h)
                if s == ST - 1:
                    mm(ap("P6", 32 * h, 32 * h + 32), ap("BE%d" % h), ap("RX32"), False, h == 1)
                    finish(h)
        tag[:] = ["e" if last else "s", 0]
        brep = ap("WF", 0, 128)
        ol = 32 * t
        l2, l1, lh, lt = [ap("OL", ol + 8 * k, ol + 8 * k + 8) for k in range(4)]
        scan(ap("SO"), ap("D0"), ap("P6", 0, 64), ALU.add, ALU.max)
        cp(l2, ap("SO", 5, 64, 8))
        cp(l1, ap("SO", 6, 64, 8))
        hot(3)
        group(tile(ap("P7", 32, 40), "KH", 0, 128))
        cp(ap("OV"), ap("P7", 32, 40))
        act(ap("AV"), ap("P7", 32, 40))
        tt(ap("NV"), ind(FTG, ap("OV")), brep, ALU.not_equal)
        group([(ap("P7", 64, 80), ap("IDF"), ap("CD2")), (ap("P7", 64, 80, 2), ap("IDF"), ap("AV"))]
              + tile(ap("P7", 64, 80, 2), "NV", 0, 128, "SWB"))
        scan(ap("LH"), ap("SO", 0, 64, 4), ap("P7", 64, 80), ALU.max, ALU.min)
        cp(lh, ap("LH", 1, 16, 2))
        act(ap("KM"), ap("WK", 0, 128), scale=nrow0)
        if not last:
            act(ap("XX", GW + lo, GW + lo + 128), ind(ap("WX", wx, wx + 256), l1))
        tt(ind(ap("KIN"), l2), ap("KM"), ap("N0", lo - B0, lo - B0 + 128), ALU.add)
        act(ap("KIN", lo, lo + 128), ind(ap("WK"), l1))
        act(ap("FT", lo, lo + 128), ind(ap("WF"), l1))
        act(ap("XX", lo, lo + 128), ind(ap("WX", wx, wx + 256), l1))
        cp(ind(ap("FT"), lh), nrep)
        if not last:
            cp(lt, ap("SO", 2, 64, 8))
            act(ap("AT", 8, 16), ap("SO", 6, 64, 8), scale=1.0 / 128, acc=ap("AT", 17, 18))
            group([(ap("P6", 192, 193), ap("ONES"), ap("AT", 16, 17)), (ap("P6", 192, 193), ap("ONES"), ap("AT", 17, 18))])
            ts(ap("AT", 0, 1), ap("P6", 192, 193), 32.0 * MAGIC, ALU.add, 32.0 * MAGIC, ALU.subtract)
            tt(ap("AO", 4 * t, 4 * t + 1), ap("P6", 192, 193), ap("AT", 0, 1), ALU.subtract)
            send(nxt, ap("AIN", 4 * t, 4 * t + 4), ap("AO", 4 * t, 4 * t + 4), "ra%d" % t, 2e3)
            if t < VIS - 2:
                send(nxt, ap("LIN", 8 * t, 8 * t + 8), lt, "rl%d" % t, 2e3)
            if t > 0:
                cp(ind(ap("TT"), ap("LIN", 8 * t - 8, 8 * t)), brep)
        else:
            dma("Y", ("yz",), ap("WX", wx, wx + 128), "dout", 32e3)
            for h in range(2):
                act(ap("TS", 64 * h, 64 * h + 64), ind(ap("IOTA"), ap("BIN", 16 * t + 8 * h, 16 * t + 8 * h + 4)))
                cp(ind(ap("TO"), ap("OL", ol - 8 + 4 * h, ol - 4 + 4 * h)), ap("TS", 64 * h, 64 * h + 64))
            dma("Y", ("yt",), ap("TO", 0, W, ps=16), "dout", 57e3)
            dma("Y", ("yx", 0, 128, 1, lo - B0, lo - B0 + 128), ap("XX", lo, lo + 128), "dout", 32e3)
            dma("S", ("yf",), ap("FT", B0, W, ps=16), "dout", 16e3)
            dma("S", ("yp",), ap("KIN", 0, B0, ps=16), "dout", 41e3)
            dma("Y", ("yk", 0, 128, 1, lo - B0, lo - B0 + 128), ap("KIN", lo, lo + 128), "dout", 64e3)
            for c0, c1 in rest:
                dma("Y", ("yk", 0, 128, 16, c0 - B0, c1 - B0), ap("KIN", c0, c1, ps=16), "dout", 12e3, "dpre")
    return ops


def depend(ops):
    hist = {}
    bank = {}
    deps = []
    for i, o in enumerate(ops):
        d = {}
        acc = [(a, False) for a in o["r"]] + [(a, True) for a in o["w"]]
        for a, wr in acc:
            if psum(a):
                bk = bank.setdefault(a["n"], [o["e"], []])
                if bk[0] != o["e"]:
                    bk[:] = [o["e"], [x[0] for x in hist[a["n"]]]]
                    hist[a["n"]] = []
                for j in bk[1]:
                    d[j] = True
            for (j, b, bw) in hist.get(a["n"], []):
                if j != i and (wr or bw) and a["c0"] < b["c1"] and b["c0"] < a["c1"] and a["p0"] < b["p1"] and b["p0"] < a["p1"]:
                    if ops[j]["k"] == "dma" and o["k"] == "dma" and ops[j]["sem"] == o["sem"]:
                        continue
                    if a["st"] == b["st"] > 1 and (a["c0"] - b["c0"]) % a["st"] and not psum(a):
                        continue
                    d[j] = d.get(j, False) or not (o["e"] == "P" and ops[j]["e"] == "P")
        for a, wr in acc:
            h = hist.setdefault(a["n"], [])
            if psum(a):
                if o["e"] == "P":
                    h[:] = []
            elif wr and a["st"] == 1 and a["ps"] == 1 and a["off"] is None:
                h[:] = [x for x in h if x[0] == i or not (a["c0"] <= x[1]["c0"] and x[1]["c1"] <= a["c1"] and a["p0"] <= x[1]["p0"] and x[1]["p1"] <= a["p1"])]
            elif wr and a["off"] is not None:
                h[:] = [x for x in h if x[0] == i]
            if o["e"] == "P":
                h[:] = [x for x in h if ops[x[0]]["e"] != "P" or ops[x[0]]["w"][0]["n"] != o["w"][0]["n"] or x[2] != wr or x[1] != a]
            h.append((i, a, wr))
        if "after" in o:
            d.setdefault(o["after"], False)
        deps.append(d)
    grp = {}
    for i, o in enumerate(ops):
        if o["k"] == "dma":
            grp.setdefault(o["sem"], []).append(i)
    for i, d in enumerate(deps):
        if ops[i].get("behind"):
            d[grp[ops[i]["behind"]][0]] = True
        for j in list(d):
            if ops[j]["k"] == "dma" and d[j]:
                for k in grp[ops[j]["sem"]]:
                    d[k] = True
    lastmm = {}
    for i, o in enumerate(ops):
        if o["e"] == "P":
            n = o["w"][0]["n"]
            if n in lastmm:
                deps[i].setdefault(lastmm[n], False)
            lastmm[n] = i
    return deps, grp


def schedule(ops, deps):
    n = len(ops)
    before, after = [[] for _ in range(n)], [[] for _ in range(n)]
    for i, d in enumerate(deps):
        for j, s in d.items():
            w = (HOP if s else 0.0) + (ops[j].get("lat", 0.0) if s or ops[i]["e"] == "R" else 0.0)
            before[i].append((j, w))
            after[j].append((i, w))
    tail = [o.get("lat", 0.0) for o in ops]

    def run(pred, succ, first, prio):
        left = [len(p) for p in pred]
        rdy = list(first)
        ready = {e: [] for e in "VSPGYR"}
        for i in range(n):
            if not left[i]:
                ready[ops[i]["e"]].append(i)
        free = {e: 0.0 for e in ready}
        fin, seq = [0.0] * n, []
        for _ in range(n):
            t0, e = min((max(free[e], min(rdy[i] for i in l)) - AHEAD * (e == "P"), e) for e, l in ready.items() if l)
            t0 += AHEAD * (e == "P")
            i = max((i for i in ready[e] if rdy[i] <= t0 + SLACK), key=lambda k: prio[k])
            if not ops[i].get("hot"):
                soon = [k for k in ready[e] if ops[k].get("hot") and rdy[k] <= t0 + min(WAIT, ops[i]["c"])]
                if soon:
                    i = min(soon, key=lambda k: rdy[k])
            ready[e].remove(i)
            fin[i] = free[e] = max(free[e], rdy[i]) + ops[i]["c"]
            seq.append(i)
            for u, w in succ[i]:
                rdy[u] = max(rdy[u], fin[i] + w)
                left[u] -= 1
                if not left[u]:
                    ready[ops[u]["e"]].append(u)
        return fin, seq

    prio = [0.0] * n
    for i in range(n - 1, -1, -1):
        prio[i] = ops[i]["c"] + max([tail[i]] + [prio[u] + w for u, w in after[i]])
    best = None
    for _ in range(PASSES):
        fin, seq = run(before, after, [0.0] * n, prio)
        end = max(f + x for f, x in zip(fin, tail))
        if best is None or end < best[0]:
            best = (end, fin, seq)
        back = run(after, before, tail, fin)[0]
        prio = [MIX * b + (1 - MIX) * p for b, p in zip(back, prio)]
    end, fin, seq = best
    ops[0]["seq"] = seq
    order = {e: [] for e in "VSPGYR"}
    for i in seq:
        ops[i]["t"] = (fin[i] - ops[i]["c"], fin[i] + tail[i])
        order[ops[i]["e"]].append(i)
    return order, end


def plan(rank):
    ops = build(rank)
    deps, grp = depend(ops)
    order, total = schedule(ops, deps)
    pos = {}
    for e, l in order.items():
        for k, i in enumerate(l):
            pos[i] = k
    waits = {}
    marked = set()
    seen = {e: {} for e in order}
    knew = {}
    for i in ops[0]["seq"]:
        e = ops[i]["e"]
        need = {}
        for j, s in deps[i].items():
            if s:
                o = ops[j]
                if o["k"] == "dma":
                    need[o["sem"]] = 16 * len(grp[o["sem"]])
                elif o["k"] == "recv":
                    need[o["sem"]] = NENG
                else:
                    need[o["e"]] = max(need.get(o["e"], -1), pos[j])
        w = []
        for k, v in sorted(need.items(), key=lambda x: -ops[order[x[0]][x[1]]]["t"][0] if x[0] in order else 0):
            if seen[e].get(k, -1) < v:
                w.append((k, v))
                seen[e][k] = v
                if k in order:
                    marked.add(order[k][v])
                    for k2, v2 in knew[order[k][v]].items():
                        seen[e][k2] = max(seen[e].get(k2, -1), v2)
        waits[i] = w
        knew[i] = dict(seen[e])
    return ops, order, waits, marked, grp, total


def rank_program(g, core, T, topo):
    rank = T.rank_of(core)
    if rank is None:
        return
    ops, order, waits, marked, grp, total = plan(rank)
    q = {"V": g.vector, "S": g.scalar, "P": g.tensor, "G": g, "Y": g.sync}
    count = {}
    for e in "VSPG":
        c = 0
        for k, i in enumerate(order[e]):
            c += i in marked
            count[e, k] = c

    def real(a):
        if isinstance(a, tuple):
            return T[a[0]][:] if len(a) == 1 else T[a[0]][a[1]:a[2]:a[3], a[4]:a[5]]
        if not isinstance(a, dict):
            return a
        if BUF[a["n"]][0] == "dram":
            return T[a["n"]][:]
        n, at = PLACE[a["n"]]
        x = T[n][a["p0"]:a["p1"]:a["ps"], at + a["c0"]:at + a["c1"]:a["st"]]
        return x if a["off"] is None else x.indirect(real(a["off"]))

    sent = 0
    for e in "YSVPG":
        E = q[e]
        for i in order[e]:
            o = ops[i]
            for k, v in waits[i]:
                if k in q:
                    E.wait_ge(T.sem["c" + k], count[k, v])
                else:
                    E.wait_ge(T.sem[k], v)
            a = [real(x) for x in o["a"]]
            k = o["k"]
            if k == "send":
                dst = T.cores[a[0]]
                rid, pid = topo.addr(dst, core)
                m = sum(1 << x for x in topo.engines(core, dst)[:NENG])
                g.remote_dma(a[1], a[2], T.sem[a[3]], T.sem["sent"], pid, rid, m)
                sent += NENG
                continue
            if k == "dma":
                E.dma_start(a[0], a[1]).then_inc(T.sem[o["sem"]], 16)
                continue
            if k == "copy":
                x = E.tensor_copy(a[0], a[1])
            elif k == "tt":
                x = E.tensor_tensor(*a)
            elif k == "ts":
                x = E.tensor_scalar(*(a if a[5] is not None else a[:5]))
            elif k == "scan":
                x = E.tensor_tensor_scan(*a)
            elif k == "red":
                x = E.tensor_reduce(a[0], a[1], AX.X, a[2], negate=a[3], apply_absolute_value=a[4])
            elif k == "memset":
                x = E.memset(*a)
            elif k == "act":
                x = E.activation(a[0], a[1], a[2], bias=a[3], scale=a[4], accum_out=a[5])
            elif k == "mm":
                x = E.matmul(*a)
            elif BUF[o["a"][0]["n"]][2] == i32:
                x = E.iota(*a)
            else:
                x = E.iota(*a, allow_small_or_imprecise_dtypes=True)
            if i in marked:
                x.then_inc(T.sem["c" + e], 1)
    g.wait_ge(T.sem["sent"], sent)
    g.sync.wait_ge(T.sem["dout"], 16 * len(grp["dout"]))
